import numpy as np
import ml_dtypes


def mxq(x, axis, fmt="e4m3"):
    dtype, down = {"e4m3": (ml_dtypes.float8_e4m3fn, 7), "e5m2": (ml_dtypes.float8_e5m2, 14)}[fmt]
    v = np.moveaxis(np.asarray(x, np.float32).astype(ml_dtypes.bfloat16).astype(np.float64), axis, -1)
    blocks = v.reshape(v.shape[:-1] + (-1, 32))
    amax = np.abs(blocks).max(-1, keepdims=True)
    byte = np.maximum(np.where(amax > 0, np.frexp(amax)[1] - 1 + 127, 0) - down, 1)
    scale = np.exp2(byte - 127.0)
    codes = (blocks / scale).astype(np.float32).astype(dtype).astype(np.float64)
    return np.moveaxis((codes * scale).reshape(v.shape), -1, axis)


WIDE = False


def mx_kscale(k):
    if not WIDE:
        return np.ones(k)
    levels = np.array([10, -10, 5, -5, 0])
    if k % 512:
        return np.exp2(np.random.permutation(np.resize(levels, k // 32))).repeat(32)
    a = np.empty((k // 512, 16))
    for p in range(k // 512):
        a[p, :8] = np.random.permutation(np.resize(levels, 8))
        for g in range(8):
            far = levels[np.abs(levels - a[p, g]) >= 10]
            a[p, g + 8] = far[np.random.randint(len(far))]
    return np.exp2(a.ravel()).repeat(32)


def f64(x):
    return np.asarray(x).astype(np.float64)


def striped(idx):
    return np.tile(idx.reshape(-1, 16).T, (8, 1)).astype(np.uint16)


def unstriped(offs):
    return offs[:16].T.reshape(-1).astype(np.int64)


E2M1 = np.array([0.0, 0.5, 1.0, 1.5, 2.0, 3.0, 4.0, 6.0, -0.0, -0.5, -1.0, -1.5, -2.0, -3.0, -4.0, -6.0])


def pack_weight(w, fmt):
    k, n = w.shape
    w = f64(np.asarray(w, np.float32).astype(ml_dtypes.bfloat16)).reshape(k // 32, 32, n)
    amax = np.abs(w).max(1)
    if fmt == "e4m3":
        byte = np.frexp(amax)[1] - 1 + 127 - 7
    else:
        mant, ex = np.frexp(amax / 6.0)
        byte = np.where(mant > 0.5, ex, ex - 1) + 127
    byte = np.clip(np.where(amax > 0, byte, 1), 1, 254)
    scaled = (w * np.exp2(127.0 - byte)[:, None, :]).reshape(k, n).astype(np.float32)
    by_word = np.ascontiguousarray(scaled.reshape(k // 512, 128, 4, n).transpose(0, 1, 3, 2))
    if fmt == "e4m3":
        words = by_word.astype(ml_dtypes.float8_e4m3fn).view(np.uint8)
    else:
        c = by_word.astype(ml_dtypes.float4_e2m1fn).view(np.uint8) & 0xF
        words = (c[..., 0::2] | (c[..., 1::2] << 4)).reshape(k // 512, 128, 2 * n)
    return np.ascontiguousarray(words), np.ascontiguousarray(byte.astype(np.uint8).reshape(k // 512, 16, n))


def unpack_weight(words, scales, fmt):
    g, _, n = scales.shape
    words = np.ascontiguousarray(words).reshape(g, 128, n, -1)
    if fmt == "e4m3":
        vals = words.view(ml_dtypes.float8_e4m3fn).astype(np.float64)
    else:
        nib = np.empty((g, 128, n, 4), np.uint8)
        nib[..., 0::2] = words & 0xF
        nib[..., 1::2] = words >> 4
        vals = E2M1[nib]
    vals = vals * np.repeat(np.exp2(scales.astype(np.float64) - 127.0), 8, axis=1)[..., None]
    return vals.transpose(0, 1, 3, 2).reshape(g * 512, n)


def d_relu(v):
    return (v > 0).astype(np.float64)


K, T, E, C, H, N = 512, 1024, 4, 128, 512, 1024


def by_expert(wq, xq):
    return np.concatenate([wq[e].T @ xq[:, e * C:(e + 1) * C] for e in range(E)], axis=1)


def setup_inputs():
    n = np.random.standard_normal
    v = mx_kscale(N)
    u = mx_kscale(H)
    slot_token = np.random.permutation(T)[:E * C]
    w_slot = np.random.uniform(0.2, 1.0, E * C)
    dy = pack_weight(n((N, T)) * v[:, None], "e4m3")
    wt = pack_weight(n((N, K)) / np.sqrt(N) / v[:, None], "e2m1")
    wbt = [pack_weight(m, "e2m1") for m in n((E, N, H)) / np.sqrt(N) / v[None, :, None] * u]
    wat = [pack_weight(m, "e2m1") for m in n((E, H, K)) / np.sqrt(H) / u[None, :, None]]
    return {
        "dy_words": dy[0],
        "dy_scales": dy[1],
        "wt_words": wt[0],
        "wt_scales": wt[1],
        "wbt_words": np.stack([m[0] for m in wbt]),
        "wbt_scales": np.stack([m[1] for m in wbt]),
        "wat_words": np.stack([m[0] for m in wat]),
        "wat_scales": np.stack([m[1] for m in wat]),
        "a": (n((H, E * C))).astype(np.float32),
        "gate": (np.tile(w_slot, (128, 1))).astype(np.float32),
        "offs": striped(slot_token),
    }


def reference(dy_words, dy_scales, wt_words, wt_scales, wbt_words, wbt_scales, wat_words, wat_scales, a, gate, offs):
    wt = unpack_weight(wt_words, wt_scales, "e2m1")
    wbt = np.stack([unpack_weight(wbt_words[e], wbt_scales[e], "e2m1") for e in range(E)])
    wat = np.stack([unpack_weight(wat_words[e], wat_scales[e], "e2m1") for e in range(E)])
    idx = unstriped(offs)
    dy = unpack_weight(dy_words, dy_scales, "e4m3")
    base = wt.T @ dy
    dh = f64(gate[:1]) * by_expert(wbt, dy[:, idx]) * d_relu(f64(a))
    dx = by_expert(wat, mxq(dh, 0, "e4m3"))
    c = np.zeros((K, T))
    c[:, idx] = dx
    return base + c

@@ -1,0 +1,224 @@
+from contextlib import ExitStack
+
+import concourse.mybir as mybir
+from concourse.masks import make_identity
+
+K, T, E, C, H, N = 512, 1024, 4, 128, 512, 1024
+S = E * C
+FLOPS = 2 * N * K * T + 2 * N * H * S + 2 * H * K * S
+
+F32 = mybir.dt.float32
+BF16 = mybir.dt.bfloat16
+I32 = mybir.dt.int32
+U32 = mybir.dt.uint32
+U16 = mybir.dt.uint16
+U8 = mybir.dt.uint8
+FP8X4 = mybir.dt.float8_e4m3fn_x4
+FP4X4 = mybir.dt.float4_e2m1fn_x4
+ALU = mybir.AluOpType
+COPY = mybir.ActivationFunctionType.Copy
+
+P = 128
+PASSES = N // 512
+KT = K // P
+BANK = 512
+POOL_ADDS = 3
+SPLIT_KT = 2
+
+
+def tile_moe_adb_relu_kernel(
+    tc, dy_words, dy_scales, wt_words, wt_scales, wbt_words, wbt_scales, wat_words, wat_scales, a, gate, offs, out
+):
+    nc = tc.nc
+    with ExitStack() as ctx:
+        keep = ctx.enter_context(tc.tile_pool(name="keep", bufs=1))
+        ring = ctx.enter_context(tc.tile_pool(name="ring", bufs=2))
+        psum = ctx.enter_context(tc.psum_pool(name="psum", bufs=1))
+
+        offsets = keep.tile([P, S // 16], U16, name="offsets")
+        nc.sync.dma_start(offsets[:], offs)
+
+        def scale_plane(name, count, width):
+            plane = keep.tile([P, count, width], U8, name=name, align_bytes=64)
+            nc.vector.memset(plane[:].rearrange("p c w -> p (c w)").bitcast(I32), 0)
+            return plane
+
+        def load_scales(plane, rows):
+            by_r = rows.bitcast(I32).rearrange("c (q r) w -> r q c w", r=4)
+            for r in range(4):
+                nc.sync.dma_start(plane[r:P:32, :, :].bitcast(I32), by_r[r])
+
+        dy_s = scale_plane("dy_s", PASSES, T)
+        wb_s = scale_plane("wb_s", E * PASSES, H)
+        wa_s = scale_plane("wa_s", E, K)
+        wt_s = scale_plane("wt_s", PASSES, K)
+        zero = keep.tile([P, 8], F32, name="zero")
+        nc.vector.memset(zero[:], 0.0)
+
+        ident = keep.tile([P, P], F32, name="ident")
+        make_identity(nc, ident[:])
+
+        windows = [keep.tile([P, T], F32, name=f"window{kt}") for kt in range(KT)]
+        for kt in range(KT):
+            nc.scalar.activation(windows[kt][:], zero[:, 0:1].to_broadcast([P, T]), COPY)
+
+        dy_w = [keep.tile([P, T], I32, name=f"dy_w{s}", align_bytes=64) for s in range(PASSES)]
+        wb_w = [keep.tile([P, PASSES, 2 * H], U8, name=f"wb_w{e}", align_bytes=64) for e in range(E)]
+        wa_w = [keep.tile([P, 2 * K], U8, name=f"wa_w{e}", align_bytes=64) for e in range(E)]
+        wt_w = keep.tile([P, PASSES, 2 * K], U8, name="wt_w", align_bytes=64)
+        a_sb = [keep.tile([P, 4, C], F32, name=f"a_sb{e}") for e in range(E)]
+        g_col = keep.tile([P, E], F32, name="g_col")
+
+        for s in range(PASSES):
+            nc.sync.dma_start(dy_w[s][:], dy_words[s].rearrange("p t d -> p (t d)").bitcast(I32))
+            if s == 0:
+                load_scales(dy_s, dy_scales)
+        load_scales(wb_s, wbt_scales.rearrange("e s b w -> (e s) b w"))
+        with nc.allow_non_contiguous_dma(reason="one gate value a partition and adapter"):
+            nc.sync.dma_start(g_col[:], gate[0].rearrange("(e u) -> u e", e=E))
+        a_rows = a.rearrange("(p t) j -> p t j", t=4)
+
+        def load_wa(e):
+            nc.sync.dma_start(wa_w[e][:].bitcast(I32), wat_words[e, 0].bitcast(I32))
+
+        for e in range(E):
+            nc.sync.dma_start(wb_w[e][:].bitcast(I32), wbt_words[e].bitcast(I32).rearrange("s p w -> p s w"))
+            nc.sync.dma_start(a_sb[e][:], a_rows[:, :, e * C : (e + 1) * C])
+            if e == 1:
+                load_scales(wa_s, wat_scales.rearrange("e s b w -> (e s) b w"))
+            if e >= 1:
+                load_wa(e - 1)
+        load_wa(E - 1)
+        load_scales(wt_s, wt_scales)
+        nc.sync.dma_start(wt_w[:].bitcast(I32), wt_words.bitcast(I32).rearrange("s p w -> p s w"))
+
+        slot_s = keep.tile([P, PASSES, S], U8, name="slot_s", align_bytes=64)
+        slot_w = keep.tile([P, PASSES, S], U32, name="slot_w", align_bytes=64)
+
+        def slot_offsets(e0, e1):
+            return offsets[:, e0 * C // 16 : e1 * C // 16]
+
+        def gather_words(s, e0, e1):
+            nc.vector.tensor_copy(slot_w[:, s, e0 * C : e1 * C], dy_w[s][:].bitcast(U32).indirect(slot_offsets(e0, e1)))
+
+        def gather_scales(s, e0, e1):
+            nc.vector.tensor_copy(slot_s[:, s, e0 * C : e1 * C], dy_s[:, s, :].indirect(slot_offsets(e0, e1)))
+
+        gather_words(0, 0, E)
+        for e0, e1 in ((0, 1), (1, 2), (2, 4)):
+            gather_scales(0, e0, e1)
+            gather_scales(1, e0, e1)
+            gather_words(1, e0, e1)
+
+        dx = keep.tile([P, KT, S], F32, name="dx")
+        h_sb, dh, dh_w, dh_s = {}, {}, {}, {}
+
+        def first_product(e):
+            cols = slice(e * C, (e + 1) * C)
+            h_ps = psum.tile([P, H], F32, name="h_ps", bufs=2)
+            for s in range(PASSES):
+                nc.tensor.matmul_mx(
+                    out=h_ps[:],
+                    lhsT=slot_w[:, s, cols].bitcast(FP8X4),
+                    lhsT_scale=slot_s[:, s, cols],
+                    rhs=wb_w[e][:, s, :].bitcast(FP4X4),
+                    rhs_scale=wb_s[:, e * PASSES + s, :],
+                    start=(s == 0),
+                    stop=(s == PASSES - 1),
+                )
+            h_sb[e] = keep.tile([P, 4, P], F32, name=f"h_sb{e}")
+            nc.scalar.activation(
+                h_sb[e][:], h_ps[:].rearrange("u (m t) -> u t m", t=4), COPY, scale=g_col[:, e : e + 1]
+            )
+
+        def turn_and_mask(e):
+            turned = psum.tile([P, 4, C], F32, name="turned", bufs=2)
+            for t in range(4):
+                nc.tensor.transpose(turned[:, t, :], h_sb[e][:, t, :], ident[:])
+            dh[e] = keep.tile([P, C, 4], BF16, name=f"dh{e}", align_bytes=64)
+            nc.vector.scalar_tensor_tensor(
+                out=dh[e][:],
+                in0=a_sb[e][:].rearrange("p t u -> p u t"),
+                scalar=0.0,
+                in1=turned[:].rearrange("p t u -> p u t"),
+                op0=ALU.is_gt,
+                op1=ALU.mult,
+            )
+
+        def quantize(e):
+            dh_w[e] = keep.tile([P, C], U32, name=f"dh_w{e}", align_bytes=64)
+            dh_s[e] = keep.tile([P, C], U8, name=f"dh_s{e}", align_bytes=64)
+            nc.vector.quantize_mx(
+                out=dh_w[e][:].bitcast(FP8X4), scales=dh_s[e][:], in_=dh[e][:].rearrange("p u t -> p (u t)")
+            )
+
+        def second_product(e):
+            dx_ps = psum.tile([P, KT, C], F32, name="dx_ps", bufs=1)
+            for kt in range(KT):
+                nc.tensor.matmul_mx(
+                    out=dx_ps[:, kt, :],
+                    lhsT=wa_w[e][:, 2 * kt * P : 2 * (kt + 1) * P].bitcast(FP4X4),
+                    lhsT_scale=wa_s[:, e, kt * P : (kt + 1) * P],
+                    rhs=dh_w[e][:].bitcast(FP8X4),
+                    rhs_scale=dh_s[e][:],
+                    start=True,
+                    stop=True,
+                )
+            nc.scalar.copy(dx[:, :, e * C : (e + 1) * C], dx_ps[:])
+
+        def scatter(kt, e0, e1):
+            nc.vector.tensor_copy(
+                windows[kt][:].indirect(offsets[:, e0 * C // 16 : e1 * C // 16]), dx[:, kt, e0 * C : e1 * C]
+            )
+
+        first_product(0)
+        first_product(1)
+        turn_and_mask(0)
+        first_product(2)
+        quantize(0)
+        turn_and_mask(1)
+        second_product(0)
+        quantize(1)
+        first_product(3)
+        turn_and_mask(2)
+        second_product(1)
+        scatter(0, 0, 1)
+        quantize(2)
+        turn_and_mask(3)
+        second_product(2)
+        scatter(1, 0, 1)
+        quantize(3)
+        second_product(3)
+        scatter(0, 1, 2)
+        scatter(1, 1, 2)
+        scatter(0, 2, 3)
+        scatter(1, 2, 3)
+        scatter(0, 3, 4)
+        scatter(1, 3, 4)
+
+        for kt in range(KT):
+            rows = slice(kt * P, (kt + 1) * P)
+            if kt >= SPLIT_KT:
+                nc.vector.tensor_copy(windows[kt][:].indirect(offsets[:]), dx[:, kt, :])
+            result = keep.tile([P, T], F32, name=f"result{kt}")
+            for half in range(T // BANK):
+                tok = slice(half * BANK, (half + 1) * BANK)
+                base_ps = psum.tile([P, BANK], F32, name="base_ps", bufs=3)
+                for s in range(PASSES):
+                    nc.tensor.matmul_mx(
+                        out=base_ps[:],
+                        lhsT=wt_w[:, s, 2 * kt * P : 2 * (kt + 1) * P].bitcast(FP4X4),
+                        lhsT_scale=wt_s[:, s, kt * P : (kt + 1) * P],
+                        rhs=dy_w[s][:, tok].bitcast(FP8X4),
+                        rhs_scale=dy_s[:, s, tok],
+                        start=(s == 0),
+                        stop=(s == PASSES - 1),
+                    )
+                if kt < POOL_ADDS:
+                    nc.scalar.copy(result[:, tok], base_ps[:])
+                else:
+                    nc.vector.tensor_tensor(result[:, tok], windows[kt][:, tok], base_ps[:], ALU.add)
+                    nc.sync.dma_start(out[rows, tok], result[:, tok])
+            if kt < POOL_ADDS:
+                nc.gpsimd.tensor_tensor(result[:], result[:], windows[kt][:], ALU.add)
+                nc.sync.dma_start(out[rows, :], result[:])

@@ -22,8 +22,6 @@ P = 128
 PASSES = N // 512
 KT = K // P
 BANK = 512
-POOL_ADDS = 3
-SPLIT_KT = 2
 
 
 def tile_moe_adb_relu_kernel(
@@ -32,7 +30,6 @@ def tile_moe_adb_relu_kernel(
     nc = tc.nc
     with ExitStack() as ctx:
         keep = ctx.enter_context(tc.tile_pool(name="keep", bufs=1))
-        ring = ctx.enter_context(tc.tile_pool(name="ring", bufs=2))
         psum = ctx.enter_context(tc.psum_pool(name="psum", bufs=1))
 
         offsets = keep.tile([P, S // 16], U16, name="offsets")
@@ -43,10 +40,10 @@ def tile_moe_adb_relu_kernel(
             nc.vector.memset(plane[:].rearrange("p c w -> p (c w)").bitcast(I32), 0)
             return plane
 
-        def load_scales(plane, rows):
+        def load_scales(plane, rows, queue):
             by_r = rows.bitcast(I32).rearrange("c (q r) w -> r q c w", r=4)
             for r in range(4):
-                nc.sync.dma_start(plane[r:P:32, :, :].bitcast(I32), by_r[r])
+                queue.dma_start(plane[r:P:32, :, :].bitcast(I32), by_r[r])
 
         dy_s = scale_plane("dy_s", PASSES, T)
         wb_s = scale_plane("wb_s", E * PASSES, H)
@@ -64,33 +61,50 @@ def tile_moe_adb_relu_kernel(
 
         dy_w = [keep.tile([P, T], I32, name=f"dy_w{s}", align_bytes=64) for s in range(PASSES)]
         wb_w = [keep.tile([P, PASSES, 2 * H], U8, name=f"wb_w{e}", align_bytes=64) for e in range(E)]
-        wa_w = [keep.tile([P, 2 * K], U8, name=f"wa_w{e}", align_bytes=64) for e in range(E)]
+        wa_w = [keep.tile([P, 2, 2 * K], U8, name=f"wa_w{i}", align_bytes=64) for i in range(E // 2)]
         wt_w = keep.tile([P, PASSES, 2 * K], U8, name="wt_w", align_bytes=64)
-        a_sb = [keep.tile([P, 4, C], F32, name=f"a_sb{e}") for e in range(E)]
+        a_sb = [keep.tile([P, 4, 2 * C], F32, name=f"a_sb{i}") for i in range(E // 2)]
         g_col = keep.tile([P, E], F32, name="g_col")
-
-        for s in range(PASSES):
-            nc.sync.dma_start(dy_w[s][:], dy_words[s].rearrange("p t d -> p (t d)").bitcast(I32))
-            if s == 0:
-                load_scales(dy_s, dy_scales)
-        load_scales(wb_s, wbt_scales.rearrange("e s b w -> (e s) b w"))
-        with nc.allow_non_contiguous_dma(reason="one gate value a partition and adapter"):
-            nc.sync.dma_start(g_col[:], gate[0].rearrange("(e u) -> u e", e=E))
         a_rows = a.rearrange("(p t) j -> p t j", t=4)
 
-        def load_wa(e):
-            nc.sync.dma_start(wa_w[e][:].bitcast(I32), wat_words[e, 0].bitcast(I32))
+        def load_dy(s):
+            nc.sync.dma_start(dy_w[s][:], dy_words[s].rearrange("p t d -> p (t d)").bitcast(I32))
 
-        for e in range(E):
+        def load_wb(e):
             nc.sync.dma_start(wb_w[e][:].bitcast(I32), wbt_words[e].bitcast(I32).rearrange("s p w -> p s w"))
-            nc.sync.dma_start(a_sb[e][:], a_rows[:, :, e * C : (e + 1) * C])
-            if e == 1:
-                load_scales(wa_s, wat_scales.rearrange("e s b w -> (e s) b w"))
-            if e >= 1:
-                load_wa(e - 1)
-        load_wa(E - 1)
-        load_scales(wt_s, wt_scales)
-        nc.sync.dma_start(wt_w[:].bitcast(I32), wt_words.bitcast(I32).rearrange("s p w -> p s w"))
+
+        def load_a(i):
+            nc.sync.dma_start(a_sb[i][:], a_rows[:, :, 2 * i * C : 2 * (i + 1) * C])
+
+        def load_wa(i):
+            pair = wat_words[2 * i : 2 * (i + 1)].bitcast(I32).rearrange("e s p w -> p (e s) w")
+            nc.sync.dma_start(wa_w[i][:].bitcast(I32), pair)
+
+        def load_gate(queue):
+            with nc.allow_non_contiguous_dma(reason="one gate value a partition and adapter"):
+                queue.dma_start(g_col[:], gate[0].rearrange("(e u) -> u e", e=E))
+
+        def load_wt():
+            nc.sync.dma_start(wt_w[:].bitcast(I32), wt_words.bitcast(I32).rearrange("s p w -> p s w"))
+
+        wb_rows = wbt_scales.rearrange("e s b w -> (e s) b w")
+        wa_rows = wat_scales.rearrange("e s b w -> (e s) b w")
+        load_dy(0)
+        load_scales(dy_s, dy_scales, nc.sync)
+        load_dy(1)
+        load_wb(0)
+        load_scales(wb_s, wb_rows, nc.sync)
+        load_gate(nc.gpsimd)
+        load_scales(wa_s, wa_rows, nc.gpsimd)
+        load_scales(wt_s, wt_scales, nc.gpsimd)
+        load_wb(1)
+        load_a(0)
+        load_wb(2)
+        load_wa(0)
+        load_wb(3)
+        load_a(1)
+        load_wa(1)
+        load_wt()
 
         slot_s = keep.tile([P, PASSES, S], U8, name="slot_s", align_bytes=64)
         slot_w = keep.tile([P, PASSES, S], U32, name="slot_w", align_bytes=64)
@@ -103,12 +117,6 @@ def tile_moe_adb_relu_kernel(
 
         def gather_scales(s, e0, e1):
             nc.vector.tensor_copy(slot_s[:, s, e0 * C : e1 * C], dy_s[:, s, :].indirect(slot_offsets(e0, e1)))
-
-        gather_words(0, 0, E)
-        for e0, e1 in ((0, 1), (1, 2), (2, 4)):
-            gather_scales(0, e0, e1)
-            gather_scales(1, e0, e1)
-            gather_words(1, e0, e1)
 
         dx = keep.tile([P, KT, S], F32, name="dx")
         h_sb, dh, dh_w, dh_s = {}, {}, {}, {}
@@ -132,13 +140,13 @@ def tile_moe_adb_relu_kernel(
             )
 
         def turn_and_mask(e):
-            turned = psum.tile([P, 4, C], F32, name="turned", bufs=2)
+            turned = psum.tile([P, 4, C], F32, name="turned", bufs=1)
             for t in range(4):
                 nc.tensor.transpose(turned[:, t, :], h_sb[e][:, t, :], ident[:])
             dh[e] = keep.tile([P, C, 4], BF16, name=f"dh{e}", align_bytes=64)
             nc.vector.scalar_tensor_tensor(
                 out=dh[e][:],
-                in0=a_sb[e][:].rearrange("p t u -> p u t"),
+                in0=a_sb[e // 2][:, :, (e % 2) * C : (e % 2 + 1) * C].rearrange("p t u -> p u t"),
                 scalar=0.0,
                 in1=turned[:].rearrange("p t u -> p u t"),
                 op0=ALU.is_gt,
@@ -157,7 +165,7 @@ def tile_moe_adb_relu_kernel(
             for kt in range(KT):
                 nc.tensor.matmul_mx(
                     out=dx_ps[:, kt, :],
-                    lhsT=wa_w[e][:, 2 * kt * P : 2 * (kt + 1) * P].bitcast(FP4X4),
+                    lhsT=wa_w[e // 2][:, e % 2, 2 * kt * P : 2 * (kt + 1) * P].bitcast(FP4X4),
                     lhsT_scale=wa_s[:, e, kt * P : (kt + 1) * P],
                     rhs=dh_w[e][:].bitcast(FP8X4),
                     rhs_scale=dh_s[e][:],
@@ -171,39 +179,12 @@ def tile_moe_adb_relu_kernel(
                 windows[kt][:].indirect(offsets[:, e0 * C // 16 : e1 * C // 16]), dx[:, kt, e0 * C : e1 * C]
             )
 
-        first_product(0)
-        first_product(1)
-        turn_and_mask(0)
-        first_product(2)
-        quantize(0)
-        turn_and_mask(1)
-        second_product(0)
-        quantize(1)
-        first_product(3)
-        turn_and_mask(2)
-        second_product(1)
-        scatter(0, 0, 1)
-        quantize(2)
-        turn_and_mask(3)
-        second_product(2)
-        scatter(1, 0, 1)
-        quantize(3)
-        second_product(3)
-        scatter(0, 1, 2)
-        scatter(1, 1, 2)
-        scatter(0, 2, 3)
-        scatter(1, 2, 3)
-        scatter(0, 3, 4)
-        scatter(1, 3, 4)
-
-        for kt in range(KT):
+        def add_and_store(kt):
             rows = slice(kt * P, (kt + 1) * P)
-            if kt >= SPLIT_KT:
-                nc.vector.tensor_copy(windows[kt][:].indirect(offsets[:]), dx[:, kt, :])
             result = keep.tile([P, T], F32, name=f"result{kt}")
             for half in range(T // BANK):
                 tok = slice(half * BANK, (half + 1) * BANK)
-                base_ps = psum.tile([P, BANK], F32, name="base_ps", bufs=3)
+                base_ps = psum.tile([P, BANK], F32, name="base_ps", bufs=4)
                 for s in range(PASSES):
                     nc.tensor.matmul_mx(
                         out=base_ps[:],
@@ -214,11 +195,45 @@ def tile_moe_adb_relu_kernel(
                         start=(s == 0),
                         stop=(s == PASSES - 1),
                     )
-                if kt < POOL_ADDS:
-                    nc.scalar.copy(result[:, tok], base_ps[:])
-                else:
-                    nc.vector.tensor_tensor(result[:, tok], windows[kt][:, tok], base_ps[:], ALU.add)
-                    nc.sync.dma_start(out[rows, tok], result[:, tok])
-            if kt < POOL_ADDS:
-                nc.gpsimd.tensor_tensor(result[:], result[:], windows[kt][:], ALU.add)
-                nc.sync.dma_start(out[rows, :], result[:])
+                nc.vector.tensor_tensor(result[:, tok], windows[kt][:, tok], base_ps[:], ALU.add)
+                nc.sync.dma_start(out[rows, tok], result[:, tok])
+
+        gather_words(0, 0, 1)
+        gather_scales(0, 0, 1)
+        gather_scales(1, 0, 1)
+        gather_words(0, 1, 4)
+        gather_words(1, 0, 1)
+        first_product(0)
+        gather_scales(0, 1, 2)
+        gather_scales(1, 1, 2)
+        gather_words(1, 1, 2)
+        first_product(1)
+        gather_scales(0, 2, 4)
+        gather_scales(1, 2, 4)
+        gather_words(1, 2, 4)
+        turn_and_mask(0)
+        first_product(2)
+        quantize(0)
+        turn_and_mask(1)
+        second_product(0)
+        first_product(3)
+        quantize(1)
+        turn_and_mask(2)
+        second_product(1)
+        scatter(0, 0, 1)
+        quantize(2)
+        turn_and_mask(3)
+        second_product(2)
+        scatter(1, 0, 1)
+        quantize(3)
+        second_product(3)
+        scatter(0, 1, 2)
+        scatter(1, 1, 3)
+        scatter(0, 2, 4)
+        scatter(1, 3, 4)
+        add_and_store(0)
+        scatter(2, 0, 4)
+        add_and_store(1)
+        scatter(3, 0, 4)
+        add_and_store(2)
+        add_and_store(3)

@@ -94,16 +94,16 @@ def tile_moe_adb_relu_kernel(
         load_dy(1)
         load_wb(0)
         load_scales(wb_s, wb_rows, nc.sync)
-        load_gate(nc.gpsimd)
-        load_scales(wa_s, wa_rows, nc.gpsimd)
-        load_scales(wt_s, wt_scales, nc.gpsimd)
+        load_gate(nc.sync)
         load_wb(1)
-        load_a(0)
+        load_scales(wa_s, wa_rows, nc.gpsimd)
         load_wb(2)
-        load_wa(0)
         load_wb(3)
-        load_a(1)
         load_wa(1)
+        load_a(0)
+        load_a(1)
+        load_wa(0)
+        load_scales(wt_s, wt_scales, nc.sync)
         load_wt()
 
         slot_s = keep.tile([P, PASSES, S], U8, name="slot_s", align_bytes=64)
@@ -119,11 +119,11 @@ def tile_moe_adb_relu_kernel(
             nc.vector.tensor_copy(slot_s[:, s, e0 * C : e1 * C], dy_s[:, s, :].indirect(slot_offsets(e0, e1)))
 
         dx = keep.tile([P, KT, S], F32, name="dx")
-        h_sb, dh, dh_w, dh_s = {}, {}, {}, {}
+        h_sb, dh, dh_w, dh_s, result = {}, {}, {}, {}, {}
 
         def first_product(e):
             cols = slice(e * C, (e + 1) * C)
-            h_ps = psum.tile([P, H], F32, name="h_ps", bufs=2)
+            h_ps = psum.tile([P, H], F32, name="h_ps", tag="bank", bufs=8)
             for s in range(PASSES):
                 nc.tensor.matmul_mx(
                     out=h_ps[:],
@@ -140,7 +140,7 @@ def tile_moe_adb_relu_kernel(
             )
 
         def turn_and_mask(e):
-            turned = psum.tile([P, 4, C], F32, name="turned", bufs=1)
+            turned = psum.tile([P, 4, C], F32, name="turned", tag="bank", bufs=8)
             for t in range(4):
                 nc.tensor.transpose(turned[:, t, :], h_sb[e][:, t, :], ident[:])
             dh[e] = keep.tile([P, C, 4], BF16, name=f"dh{e}", align_bytes=64)
@@ -161,7 +161,7 @@ def tile_moe_adb_relu_kernel(
             )
 
         def second_product(e):
-            dx_ps = psum.tile([P, KT, C], F32, name="dx_ps", bufs=1)
+            dx_ps = psum.tile([P, KT, C], F32, name="dx_ps", tag="bank", bufs=8)
             for kt in range(KT):
                 nc.tensor.matmul_mx(
                     out=dx_ps[:, kt, :],
@@ -179,61 +179,90 @@ def tile_moe_adb_relu_kernel(
                 windows[kt][:].indirect(offsets[:, e0 * C // 16 : e1 * C // 16]), dx[:, kt, e0 * C : e1 * C]
             )
 
-        def add_and_store(kt):
-            rows = slice(kt * P, (kt + 1) * P)
-            result = keep.tile([P, T], F32, name=f"result{kt}")
-            for half in range(T // BANK):
-                tok = slice(half * BANK, (half + 1) * BANK)
-                base_ps = psum.tile([P, BANK], F32, name="base_ps", bufs=4)
-                for s in range(PASSES):
-                    nc.tensor.matmul_mx(
-                        out=base_ps[:],
-                        lhsT=wt_w[:, s, 2 * kt * P : 2 * (kt + 1) * P].bitcast(FP4X4),
-                        lhsT_scale=wt_s[:, s, kt * P : (kt + 1) * P],
-                        rhs=dy_w[s][:, tok].bitcast(FP8X4),
-                        rhs_scale=dy_s[:, s, tok],
-                        start=(s == 0),
-                        stop=(s == PASSES - 1),
-                    )
-                nc.vector.tensor_tensor(result[:, tok], windows[kt][:, tok], base_ps[:], ALU.add)
-                nc.sync.dma_start(out[rows, tok], result[:, tok])
+        def base_product(kt, half):
+            tok = slice(half * BANK, (half + 1) * BANK)
+            base_ps = psum.tile([P, BANK], F32, name="base_ps", tag="bank", bufs=8)
+            for s in range(PASSES):
+                nc.tensor.matmul_mx(
+                    out=base_ps[:],
+                    lhsT=wt_w[:, s, 2 * kt * P : 2 * (kt + 1) * P].bitcast(FP4X4),
+                    lhsT_scale=wt_s[:, s, kt * P : (kt + 1) * P],
+                    rhs=dy_w[s][:, tok].bitcast(FP8X4),
+                    rhs_scale=dy_s[:, s, tok],
+                    start=(s == 0),
+                    stop=(s == PASSES - 1),
+                )
+            return base_ps
 
-        gather_words(0, 0, 1)
+        def base_to_sbuf(kt, half):
+            result[kt, half] = keep.tile([P, BANK], F32, name=f"result{kt}_{half}")
+            nc.scalar.copy(result[kt, half][:], base_product(kt, half)[:])
+
+        def store(kt, half):
+            nc.sync.dma_start(out[kt * P : (kt + 1) * P, half * BANK : (half + 1) * BANK], result[kt, half][:])
+
+        def add_on_gpsimd(kt, half):
+            total = result[kt, half]
+            nc.gpsimd.tensor_tensor(total[:], total[:], windows[kt][:, half * BANK : (half + 1) * BANK], ALU.add)
+            store(kt, half)
+
+        def add_on_vector(kt, half, base_ps):
+            result[kt, half] = keep.tile([P, BANK], F32, name=f"result{kt}_{half}")
+            nc.vector.tensor_tensor(
+                result[kt, half][:], windows[kt][:, half * BANK : (half + 1) * BANK], base_ps[:], ALU.add
+            )
+            store(kt, half)
+
+        pending = {}
+        gather_words(0, 0, 2)
         gather_scales(0, 0, 1)
-        gather_scales(1, 0, 1)
-        gather_words(0, 1, 4)
         gather_words(1, 0, 1)
-        first_product(0)
+        gather_scales(1, 0, 1)
         gather_scales(0, 1, 2)
-        gather_scales(1, 1, 2)
         gather_words(1, 1, 2)
+        first_product(0)
+        gather_scales(1, 1, 2)
         first_product(1)
-        gather_scales(0, 2, 4)
-        gather_scales(1, 2, 4)
-        gather_words(1, 2, 4)
-        turn_and_mask(0)
+        gather_words(0, 2, 4)
+        gather_scales(1, 2, 3)
+        gather_scales(0, 2, 3)
+        gather_words(1, 2, 3)
+        gather_scales(0, 3, 4)
+        gather_scales(1, 3, 4)
+        gather_words(1, 3, 4)
         first_product(2)
-        quantize(0)
-        turn_and_mask(1)
-        second_product(0)
+        turn_and_mask(0)
         first_product(3)
+        turn_and_mask(1)
+        quantize(0)
         quantize(1)
         turn_and_mask(2)
-        second_product(1)
-        scatter(0, 0, 1)
-        quantize(2)
         turn_and_mask(3)
+        second_product(0)
+        quantize(2)
+        second_product(1)
+        base_to_sbuf(0, 1)
         second_product(2)
-        scatter(1, 0, 1)
         quantize(3)
         second_product(3)
-        scatter(0, 1, 2)
-        scatter(1, 1, 3)
-        scatter(0, 2, 4)
-        scatter(1, 3, 4)
-        add_and_store(0)
+        base_to_sbuf(0, 0)
+        scatter(0, 0, 1)
+        base_to_sbuf(1, 1)
+        base_to_sbuf(1, 0)
+        base_to_sbuf(2, 0)
+        scatter(1, 0, 2)
+        scatter(0, 1, 4)
+        add_on_gpsimd(0, 0)
+        scatter(1, 2, 4)
+        add_on_gpsimd(0, 1)
+        add_on_gpsimd(1, 0)
+        base_to_sbuf(2, 1)
+        pending[3, 0] = base_product(3, 0)
+        pending[3, 1] = base_product(3, 1)
+        add_on_gpsimd(1, 1)
         scatter(2, 0, 4)
-        add_and_store(1)
+        add_on_gpsimd(2, 0)
         scatter(3, 0, 4)
-        add_and_store(2)
-        add_and_store(3)
+        add_on_gpsimd(2, 1)
+        add_on_vector(3, 0, pending[3, 0])
+        add_on_vector(3, 1, pending[3, 1])

@@ -52,6 +52,9 @@ def tile_moe_adb_relu_kernel(
         zero = keep.tile([P, 8], F32, name="zero")
         nc.vector.memset(zero[:], 0.0)
 
+        g_row = keep.tile([P, S], F32, name="g_row")
+        nc.vector.memset(g_row[:], 0.0)
+
         ident = keep.tile([P, P], F32, name="ident")
         make_identity(nc, ident[:])
 
@@ -81,8 +84,7 @@ def tile_moe_adb_relu_kernel(
             nc.sync.dma_start(wa_w[i][:].bitcast(I32), pair)
 
         def load_gate(queue):
-            with nc.allow_non_contiguous_dma(reason="one gate value a partition and adapter"):
-                queue.dma_start(g_col[:], gate[0].rearrange("(e u) -> u e", e=E))
+            queue.dma_start(g_row[0:1, :], gate[0:1, :])
 
         def load_wt():
             nc.sync.dma_start(wt_w[:].bitcast(I32), wt_words.bitcast(I32).rearrange("s p w -> p s w"))
@@ -96,15 +98,20 @@ def tile_moe_adb_relu_kernel(
         load_scales(wb_s, wb_rows, nc.sync)
         load_gate(nc.sync)
         load_wb(1)
-        load_scales(wa_s, wa_rows, nc.gpsimd)
         load_wb(2)
         load_wb(3)
-        load_wa(1)
-        load_a(0)
-        load_a(1)
         load_wa(0)
+        load_a(0)
+        load_scales(wa_s, wa_rows, nc.sync)
+        load_a(1)
         load_scales(wt_s, wt_scales, nc.sync)
         load_wt()
+        load_wa(1)
+
+        g_ps = psum.tile([P, E, P], F32, name="g_ps", tag="chain", bufs=4)
+        for e in range(E):
+            nc.tensor.transpose(g_ps[:, e, :], g_row[:, e * C : (e + 1) * C], ident[:])
+        nc.scalar.copy(g_col[:], g_ps[:, :, 0])
 
         slot_s = keep.tile([P, PASSES, S], U8, name="slot_s", align_bytes=64)
         slot_w = keep.tile([P, PASSES, S], U32, name="slot_w", align_bytes=64)
@@ -123,7 +130,7 @@ def tile_moe_adb_relu_kernel(
 
         def first_product(e):
             cols = slice(e * C, (e + 1) * C)
-            h_ps = psum.tile([P, H], F32, name="h_ps", tag="bank", bufs=8)
+            h_ps = psum.tile([P, H], F32, name="h_ps", tag="chain", bufs=4)
             for s in range(PASSES):
                 nc.tensor.matmul_mx(
                     out=h_ps[:],
@@ -140,7 +147,7 @@ def tile_moe_adb_relu_kernel(
             )
 
         def turn_and_mask(e):
-            turned = psum.tile([P, 4, C], F32, name="turned", tag="bank", bufs=8)
+            turned = psum.tile([P, 4, C], F32, name="turned", tag="chain", bufs=4)
             for t in range(4):
                 nc.tensor.transpose(turned[:, t, :], h_sb[e][:, t, :], ident[:])
             dh[e] = keep.tile([P, C, 4], BF16, name=f"dh{e}", align_bytes=64)
@@ -161,7 +168,7 @@ def tile_moe_adb_relu_kernel(
             )
 
         def second_product(e):
-            dx_ps = psum.tile([P, KT, C], F32, name="dx_ps", tag="bank", bufs=8)
+            dx_ps = psum.tile([P, KT, C], F32, name="dx_ps", tag="chain", bufs=4)
             for kt in range(KT):
                 nc.tensor.matmul_mx(
                     out=dx_ps[:, kt, :],
@@ -181,7 +188,7 @@ def tile_moe_adb_relu_kernel(
 
         def base_product(kt, half):
             tok = slice(half * BANK, (half + 1) * BANK)
-            base_ps = psum.tile([P, BANK], F32, name="base_ps", tag="bank", bufs=8)
+            base_ps = psum.tile([P, BANK], F32, name="base_ps", bufs=4)
             for s in range(PASSES):
                 nc.tensor.matmul_mx(
                     out=base_ps[:],
@@ -214,23 +221,22 @@ def tile_moe_adb_relu_kernel(
             store(kt, half)
 
         pending = {}
-        gather_words(0, 0, 2)
+        gather_words(0, 0, 4)
         gather_scales(0, 0, 1)
-        gather_words(1, 0, 1)
         gather_scales(1, 0, 1)
-        gather_scales(0, 1, 2)
-        gather_words(1, 1, 2)
+        gather_words(1, 0, 1)
         first_product(0)
+        gather_scales(0, 1, 2)
         gather_scales(1, 1, 2)
+        gather_words(1, 1, 2)
         first_product(1)
-        gather_words(0, 2, 4)
-        gather_scales(1, 2, 3)
         gather_scales(0, 2, 3)
+        gather_scales(1, 2, 3)
         gather_words(1, 2, 3)
+        first_product(2)
         gather_scales(0, 3, 4)
         gather_scales(1, 3, 4)
         gather_words(1, 3, 4)
-        first_product(2)
         turn_and_mask(0)
         first_product(3)
         turn_and_mask(1)
@@ -239,30 +245,31 @@ def tile_moe_adb_relu_kernel(
         turn_and_mask(2)
         turn_and_mask(3)
         second_product(0)
-        quantize(2)
         second_product(1)
-        base_to_sbuf(0, 1)
-        second_product(2)
+        quantize(2)
         quantize(3)
-        second_product(3)
-        base_to_sbuf(0, 0)
+        second_product(2)
         scatter(0, 0, 1)
-        base_to_sbuf(1, 1)
-        base_to_sbuf(1, 0)
-        base_to_sbuf(2, 0)
+        second_product(3)
         scatter(1, 0, 2)
+        scatter(2, 0, 2)
+        pending[0, 0] = base_product(0, 0)
+        pending[0, 1] = base_product(0, 1)
+        pending[1, 0] = base_product(1, 0)
+        pending[1, 1] = base_product(1, 1)
         scatter(0, 1, 4)
-        add_on_gpsimd(0, 0)
         scatter(1, 2, 4)
-        add_on_gpsimd(0, 1)
-        add_on_gpsimd(1, 0)
-        base_to_sbuf(2, 1)
+        add_on_vector(0, 0, pending[0, 0])
+        add_on_vector(0, 1, pending[0, 1])
+        pending[2, 0] = base_product(2, 0)
+        pending[2, 1] = base_product(2, 1)
+        scatter(2, 2, 4)
+        add_on_vector(1, 0, pending[1, 0])
+        add_on_vector(1, 1, pending[1, 1])
         pending[3, 0] = base_product(3, 0)
         pending[3, 1] = base_product(3, 1)
-        add_on_gpsimd(1, 1)
-        scatter(2, 0, 4)
-        add_on_gpsimd(2, 0)
         scatter(3, 0, 4)
-        add_on_gpsimd(2, 1)
+        add_on_vector(2, 0, pending[2, 0])
+        add_on_vector(2, 1, pending[2, 1])
         add_on_vector(3, 0, pending[3, 0])
         add_on_vector(3, 1, pending[3, 1])

@@ -19,9 +19,14 @@ ALU = mybir.AluOpType
 COPY = mybir.ActivationFunctionType.Copy
 
 P = 128
-PASSES = N // 512
+PACK = 4
+PASSES = N // (P * PACK)
 KT = K // P
 BANK = 512
+HALVES = T // BANK
+BANKS = 8
+LIST_ROWS = 16
+FP4_BYTES = 2
 
 
 def tile_moe_adb_relu_kernel(
@@ -32,26 +37,25 @@ def tile_moe_adb_relu_kernel(
         keep = ctx.enter_context(tc.tile_pool(name="keep", bufs=1))
         psum = ctx.enter_context(tc.psum_pool(name="psum", bufs=1))
 
-        offsets = keep.tile([P, S // 16], U16, name="offsets")
+        offsets = keep.tile([P, S // LIST_ROWS], U16, name="offsets")
         nc.sync.dma_start(offsets[:], offs)
 
-        def scale_plane(name, count, width):
-            plane = keep.tile([P, count, width], U8, name=name, align_bytes=64)
-            nc.vector.memset(plane[:].rearrange("p c w -> p (c w)").bitcast(I32), 0)
-            return plane
+        def zeroed_planes(name, count, width):
+            planes = keep.tile([P, count, width], U8, name=name, align_bytes=64)
+            nc.vector.memset(planes[:].rearrange("p c w -> p (c w)").bitcast(I32), 0)
+            return planes
 
-        def load_scales(plane, rows, queue):
+        def load_scales(planes, rows, queue):
             by_r = rows.bitcast(I32).rearrange("c (q r) w -> r q c w", r=4)
             for r in range(4):
-                queue.dma_start(plane[r:P:32, :, :].bitcast(I32), by_r[r])
+                queue.dma_start(planes[r:P:32, :, :].bitcast(I32), by_r[r])
 
-        dy_s = scale_plane("dy_s", PASSES, T)
-        wb_s = scale_plane("wb_s", E * PASSES, H)
-        wa_s = scale_plane("wa_s", E, K)
-        wt_s = scale_plane("wt_s", PASSES, K)
+        dy_s = zeroed_planes("dy_s", PASSES, T)
+        wb_s = zeroed_planes("wb_s", E * PASSES, H)
+        wa_s = zeroed_planes("wa_s", E, K)
+        wt_s = zeroed_planes("wt_s", PASSES, K)
         zero = keep.tile([P, 8], F32, name="zero")
         nc.vector.memset(zero[:], 0.0)
-
         g_row = keep.tile([P, S], F32, name="g_row")
         nc.vector.memset(g_row[:], 0.0)
 
@@ -63,12 +67,11 @@ def tile_moe_adb_relu_kernel(
             nc.scalar.activation(windows[kt][:], zero[:, 0:1].to_broadcast([P, T]), COPY)
 
         dy_w = [keep.tile([P, T], I32, name=f"dy_w{s}", align_bytes=64) for s in range(PASSES)]
-        wb_w = [keep.tile([P, PASSES, 2 * H], U8, name=f"wb_w{e}", align_bytes=64) for e in range(E)]
-        wa_w = [keep.tile([P, 2, 2 * K], U8, name=f"wa_w{i}", align_bytes=64) for i in range(E // 2)]
-        wt_w = keep.tile([P, PASSES, 2 * K], U8, name="wt_w", align_bytes=64)
-        a_sb = [keep.tile([P, 4, 2 * C], F32, name=f"a_sb{i}") for i in range(E // 2)]
+        wb_w = [keep.tile([P, PASSES, FP4_BYTES * H], U8, name=f"wb_w{e}", align_bytes=64) for e in range(E)]
+        wa_w = [keep.tile([P, 2, FP4_BYTES * K], U8, name=f"wa_w{pair}", align_bytes=64) for pair in range(E // 2)]
+        wt_w = keep.tile([P, PASSES, FP4_BYTES * K], U8, name="wt_w", align_bytes=64)
+        a_sb = [keep.tile([P, PACK, 2 * C], F32, name=f"a_sb{pair}") for pair in range(E // 2)]
         g_col = keep.tile([P, E], F32, name="g_col")
-        a_rows = a.rearrange("(p t) j -> p t j", t=4)
 
         def load_dy(s):
             nc.sync.dma_start(dy_w[s][:], dy_words[s].rearrange("p t d -> p (t d)").bitcast(I32))
@@ -76,86 +79,73 @@ def tile_moe_adb_relu_kernel(
         def load_wb(e):
             nc.sync.dma_start(wb_w[e][:].bitcast(I32), wbt_words[e].bitcast(I32).rearrange("s p w -> p s w"))
 
-        def load_a(i):
-            nc.sync.dma_start(a_sb[i][:], a_rows[:, :, 2 * i * C : 2 * (i + 1) * C])
-
-        def load_wa(i):
-            pair = wat_words[2 * i : 2 * (i + 1)].bitcast(I32).rearrange("e s p w -> p (e s) w")
-            nc.sync.dma_start(wa_w[i][:].bitcast(I32), pair)
-
-        def load_gate(queue):
-            queue.dma_start(g_row[0:1, :], gate[0:1, :])
-
-        def load_wt():
-            nc.sync.dma_start(wt_w[:].bitcast(I32), wt_words.bitcast(I32).rearrange("s p w -> p s w"))
-
-        wb_rows = wbt_scales.rearrange("e s b w -> (e s) b w")
-        wa_rows = wat_scales.rearrange("e s b w -> (e s) b w")
         load_dy(0)
         load_scales(dy_s, dy_scales, nc.sync)
         load_dy(1)
         load_wb(0)
-        load_scales(wb_s, wb_rows, nc.sync)
-        load_gate(nc.sync)
-        load_wb(1)
-        load_wb(2)
-        load_wb(3)
-        load_wa(0)
-        load_a(0)
-        load_scales(wa_s, wa_rows, nc.sync)
-        load_a(1)
+        load_scales(wb_s, wbt_scales.rearrange("e s b w -> (e s) b w"), nc.sync)
+        nc.sync.dma_start(g_row[0:1, :], gate[0:1, :])
+        load_scales(wa_s, wat_scales.rearrange("e s b w -> (e s) b w"), nc.gpsimd)
+        for e in range(1, E):
+            load_wb(e)
+        a_rows = a.rearrange("(p d) j -> p d j", d=PACK)
+        for pair in range(E // 2):
+            nc.sync.dma_start(a_sb[pair][:], a_rows[:, :, 2 * pair * C : 2 * (pair + 1) * C])
+        for pair in range(E // 2):
+            words = wat_words[2 * pair : 2 * (pair + 1)].bitcast(I32).rearrange("e s p w -> p (e s) w")
+            nc.sync.dma_start(wa_w[pair][:].bitcast(I32), words)
         load_scales(wt_s, wt_scales, nc.sync)
-        load_wt()
-        load_wa(1)
+        nc.sync.dma_start(wt_w[:].bitcast(I32), wt_words.bitcast(I32).rearrange("s p w -> p s w"))
 
-        g_ps = psum.tile([P, E, P], F32, name="g_ps", tag="chain", bufs=4)
+        g_ps = psum.tile([P, E, P], F32, name="g_ps", tag="bank", bufs=BANKS)
         for e in range(E):
             nc.tensor.transpose(g_ps[:, e, :], g_row[:, e * C : (e + 1) * C], ident[:])
         nc.scalar.copy(g_col[:], g_ps[:, :, 0])
 
         slot_s = keep.tile([P, PASSES, S], U8, name="slot_s", align_bytes=64)
         slot_w = keep.tile([P, PASSES, S], U32, name="slot_w", align_bytes=64)
-
-        def slot_offsets(e0, e1):
-            return offsets[:, e0 * C // 16 : e1 * C // 16]
-
-        def gather_words(s, e0, e1):
-            nc.vector.tensor_copy(slot_w[:, s, e0 * C : e1 * C], dy_w[s][:].bitcast(U32).indirect(slot_offsets(e0, e1)))
-
-        def gather_scales(s, e0, e1):
-            nc.vector.tensor_copy(slot_s[:, s, e0 * C : e1 * C], dy_s[:, s, :].indirect(slot_offsets(e0, e1)))
-
         dx = keep.tile([P, KT, S], F32, name="dx")
         h_sb, dh, dh_w, dh_s, result = {}, {}, {}, {}, {}
 
+        def slots(e0, e1):
+            return slice(e0 * C, e1 * C)
+
+        def slot_offsets(e0, e1):
+            return offsets[:, e0 * C // LIST_ROWS : e1 * C // LIST_ROWS]
+
+        def gather_words(s, e0, e1):
+            nc.vector.tensor_copy(slot_w[:, s, slots(e0, e1)], dy_w[s][:].bitcast(U32).indirect(slot_offsets(e0, e1)))
+
+        def gather_scales(s, e0, e1):
+            nc.vector.tensor_copy(slot_s[:, s, slots(e0, e1)], dy_s[:, s, :].indirect(slot_offsets(e0, e1)))
+
         def first_product(e):
-            cols = slice(e * C, (e + 1) * C)
-            h_ps = psum.tile([P, H], F32, name="h_ps", tag="chain", bufs=4)
+            h_ps = psum.tile([P, H], F32, name="h_ps", tag="bank", bufs=BANKS)
             for s in range(PASSES):
                 nc.tensor.matmul_mx(
                     out=h_ps[:],
-                    lhsT=slot_w[:, s, cols].bitcast(FP8X4),
-                    lhsT_scale=slot_s[:, s, cols],
+                    lhsT=slot_w[:, s, slots(e, e + 1)].bitcast(FP8X4),
+                    lhsT_scale=slot_s[:, s, slots(e, e + 1)],
                     rhs=wb_w[e][:, s, :].bitcast(FP4X4),
                     rhs_scale=wb_s[:, e * PASSES + s, :],
                     start=(s == 0),
                     stop=(s == PASSES - 1),
                 )
-            h_sb[e] = keep.tile([P, 4, P], F32, name=f"h_sb{e}")
+            h_sb[e] = keep.tile([P, PACK, P], F32, name=f"h_sb{e}")
             nc.scalar.activation(
-                h_sb[e][:], h_ps[:].rearrange("u (m t) -> u t m", t=4), COPY, scale=g_col[:, e : e + 1]
+                h_sb[e][:], h_ps[:].rearrange("u (m d) -> u d m", d=PACK), COPY, scale=g_col[:, e : e + 1]
             )
 
         def turn_and_mask(e):
-            turned = psum.tile([P, 4, C], F32, name="turned", tag="chain", bufs=4)
-            for t in range(4):
-                nc.tensor.transpose(turned[:, t, :], h_sb[e][:, t, :], ident[:])
-            dh[e] = keep.tile([P, C, 4], BF16, name=f"dh{e}", align_bytes=64)
+            turned = psum.tile([P, PACK, C], F32, name="turned", tag="bank", bufs=BANKS)
+            for d in range(PACK):
+                nc.tensor.transpose(turned[:, d, :], h_sb[e][:, d, :], ident[:])
+            dh[e] = keep.tile([P, C, PACK], BF16, name=f"dh{e}", align_bytes=64)
             nc.vector.scalar_tensor_tensor(
                 out=dh[e][:],
-                in0=a_sb[e // 2][:, :, (e % 2) * C : (e % 2 + 1) * C].rearrange("p t u -> p u t"),
+                in0=a_sb[e // 2][:, :, slots(e % 2, e % 2 + 1)].rearrange("p d u -> p u d"),
                 scalar=0.0,
-                in1=turned[:].rearrange("p t u -> p u t"),
+                in1=turned[:].rearrange("p d u -> p u d"),
                 op0=ALU.is_gt,
                 op1=ALU.mult,
             )
@@ -164,112 +154,87 @@ def tile_moe_adb_relu_kernel(
             dh_w[e] = keep.tile([P, C], U32, name=f"dh_w{e}", align_bytes=64)
             dh_s[e] = keep.tile([P, C], U8, name=f"dh_s{e}", align_bytes=64)
             nc.vector.quantize_mx(
-                out=dh_w[e][:].bitcast(FP8X4), scales=dh_s[e][:], in_=dh[e][:].rearrange("p u t -> p (u t)")
+                out=dh_w[e][:].bitcast(FP8X4), scales=dh_s[e][:], in_=dh[e][:].rearrange("p u d -> p (u d)")
             )
 
         def second_product(e):
-            dx_ps = psum.tile([P, KT, C], F32, name="dx_ps", tag="chain", bufs=4)
+            dx_ps = psum.tile([P, KT, C], F32, name="dx_ps", tag="bank", bufs=BANKS)
             for kt in range(KT):
                 nc.tensor.matmul_mx(
                     out=dx_ps[:, kt, :],
-                    lhsT=wa_w[e // 2][:, e % 2, 2 * kt * P : 2 * (kt + 1) * P].bitcast(FP4X4),
+                    lhsT=wa_w[e // 2][:, e % 2, FP4_BYTES * kt * P : FP4_BYTES * (kt + 1) * P].bitcast(FP4X4),
                     lhsT_scale=wa_s[:, e, kt * P : (kt + 1) * P],
                     rhs=dh_w[e][:].bitcast(FP8X4),
                     rhs_scale=dh_s[e][:],
                     start=True,
                     stop=True,
                 )
-            nc.scalar.copy(dx[:, :, e * C : (e + 1) * C], dx_ps[:])
+            nc.scalar.copy(dx[:, :, slots(e, e + 1)], dx_ps[:])
 
         def scatter(kt, e0, e1):
-            nc.vector.tensor_copy(
-                windows[kt][:].indirect(offsets[:, e0 * C // 16 : e1 * C // 16]), dx[:, kt, e0 * C : e1 * C]
-            )
+            nc.vector.tensor_copy(windows[kt][:].indirect(slot_offsets(e0, e1)), dx[:, kt, slots(e0, e1)])
+
+        def tokens(half):
+            return slice(half * BANK, (half + 1) * BANK)
 
         def base_product(kt, half):
-            tok = slice(half * BANK, (half + 1) * BANK)
-            base_ps = psum.tile([P, BANK], F32, name="base_ps", bufs=4)
+            base_ps = psum.tile([P, BANK], F32, name="base_ps", tag="bank", bufs=BANKS)
             for s in range(PASSES):
                 nc.tensor.matmul_mx(
                     out=base_ps[:],
-                    lhsT=wt_w[:, s, 2 * kt * P : 2 * (kt + 1) * P].bitcast(FP4X4),
+                    lhsT=wt_w[:, s, FP4_BYTES * kt * P : FP4_BYTES * (kt + 1) * P].bitcast(FP4X4),
                     lhsT_scale=wt_s[:, s, kt * P : (kt + 1) * P],
-                    rhs=dy_w[s][:, tok].bitcast(FP8X4),
-                    rhs_scale=dy_s[:, s, tok],
+                    rhs=dy_w[s][:, tokens(half)].bitcast(FP8X4),
+                    rhs_scale=dy_s[:, s, tokens(half)],
                     start=(s == 0),
                     stop=(s == PASSES - 1),
                 )
+            result[kt, half] = keep.tile([P, BANK], F32, name=f"result{kt}_{half}")
             return base_ps
 
-        def base_to_sbuf(kt, half):
-            result[kt, half] = keep.tile([P, BANK], F32, name=f"result{kt}_{half}")
-            nc.scalar.copy(result[kt, half][:], base_product(kt, half)[:])
-
         def store(kt, half):
-            nc.sync.dma_start(out[kt * P : (kt + 1) * P, half * BANK : (half + 1) * BANK], result[kt, half][:])
+            nc.sync.dma_start(out[kt * P : (kt + 1) * P, tokens(half)], result[kt, half][:])
 
-        def add_on_gpsimd(kt, half):
-            total = result[kt, half]
-            nc.gpsimd.tensor_tensor(total[:], total[:], windows[kt][:, half * BANK : (half + 1) * BANK], ALU.add)
-            store(kt, half)
+        gather_words(0, 0, E)
+        for e0 in range(0, E, 2):
+            for s in range(PASSES):
+                gather_scales(s, e0, e0 + 2)
+            gather_words(1, e0, e0 + 2)
+            first_product(e0)
+            if e0 == 0:
+                first_product(1)
 
-        def add_on_vector(kt, half, base_ps):
-            result[kt, half] = keep.tile([P, BANK], F32, name=f"result{kt}_{half}")
-            nc.vector.tensor_tensor(
-                result[kt, half][:], windows[kt][:, half * BANK : (half + 1) * BANK], base_ps[:], ALU.add
-            )
-            store(kt, half)
-
-        pending = {}
-        gather_words(0, 0, 4)
-        gather_scales(0, 0, 1)
-        gather_scales(1, 0, 1)
-        gather_words(1, 0, 1)
-        first_product(0)
-        gather_scales(0, 1, 2)
-        gather_scales(1, 1, 2)
-        gather_words(1, 1, 2)
-        first_product(1)
-        gather_scales(0, 2, 3)
-        gather_scales(1, 2, 3)
-        gather_words(1, 2, 3)
-        first_product(2)
-        gather_scales(0, 3, 4)
-        gather_scales(1, 3, 4)
-        gather_words(1, 3, 4)
         turn_and_mask(0)
         first_product(3)
-        turn_and_mask(1)
         quantize(0)
-        quantize(1)
+        turn_and_mask(1)
         turn_and_mask(2)
+        quantize(1)
         turn_and_mask(3)
-        second_product(0)
-        second_product(1)
         quantize(2)
+        second_product(0)
         quantize(3)
+        second_product(1)
+
+        early = [1, 2, 0, 0]
+        scatter(0, 0, early[0])
         second_product(2)
-        scatter(0, 0, 1)
         second_product(3)
-        scatter(1, 0, 2)
-        scatter(2, 0, 2)
-        pending[0, 0] = base_product(0, 0)
-        pending[0, 1] = base_product(0, 1)
-        pending[1, 0] = base_product(1, 0)
-        pending[1, 1] = base_product(1, 1)
-        scatter(0, 1, 4)
-        scatter(1, 2, 4)
-        add_on_vector(0, 0, pending[0, 0])
-        add_on_vector(0, 1, pending[0, 1])
-        pending[2, 0] = base_product(2, 0)
-        pending[2, 1] = base_product(2, 1)
-        scatter(2, 2, 4)
-        add_on_vector(1, 0, pending[1, 0])
-        add_on_vector(1, 1, pending[1, 1])
-        pending[3, 0] = base_product(3, 0)
-        pending[3, 1] = base_product(3, 1)
-        scatter(3, 0, 4)
-        add_on_vector(2, 0, pending[2, 0])
-        add_on_vector(2, 1, pending[2, 1])
-        add_on_vector(3, 0, pending[3, 0])
-        add_on_vector(3, 1, pending[3, 1])
+        scatter(1, 0, early[1])
+
+        for kt in range(KT):
+            on_gpsimd = kt < KT - 1
+            banks = []
+            for half in range(HALVES):
+                banks.append(base_product(kt, half))
+                if on_gpsimd:
+                    nc.scalar.copy(result[kt, half][:], banks[half][:])
+            scatter(kt, early[kt], E)
+            for half in range(HALVES):
+                total = result[kt, half]
+                scattered = windows[kt][:, tokens(half)]
+                if on_gpsimd:
+                    nc.gpsimd.tensor_tensor(total[:], total[:], scattered, ALU.add)
+                else:
+                    nc.vector.tensor_tensor(total[:], scattered, banks[half][:], ALU.add)
+                store(kt, half)

@@ -35,14 +35,18 @@ def tile_moe_adb_relu_kernel(
     nc = tc.nc
     with ExitStack() as ctx:
         keep = ctx.enter_context(tc.tile_pool(name="keep", bufs=1))
+        loads = ctx.enter_context(tc.tile_pool(name="loads", bufs=1))
         psum = ctx.enter_context(tc.psum_pool(name="psum", bufs=1))
 
         offsets = keep.tile([P, S // LIST_ROWS], U16, name="offsets")
         nc.sync.dma_start(offsets[:], offs)
 
-        def zeroed_planes(name, count, width):
-            planes = keep.tile([P, count, width], U8, name=name, align_bytes=64)
-            nc.vector.memset(planes[:].rearrange("p c w -> p (c w)").bitcast(I32), 0)
+        def zeroed_planes(name, count, width, engine):
+            if name in place:
+                planes = loads.tile([P, count, width], U8, name=name, offset=place[name], align_bytes=64)
+            else:
+                planes = keep.tile([P, count, width], U8, name=name, align_bytes=64)
+            engine.memset(planes[:].rearrange("p c w -> p (c w)").bitcast(I32), 0)
             return planes
 
         def load_scales(planes, rows, queue):
@@ -50,62 +54,84 @@ def tile_moe_adb_relu_kernel(
             for r in range(4):
                 queue.dma_start(planes[r:P:32, :, :].bitcast(I32), by_r[r])
 
-        dy_s = zeroed_planes("dy_s", PASSES, T)
-        wb_s = zeroed_planes("wb_s", E * PASSES, H)
-        wa_s = zeroed_planes("wa_s", E, K)
-        wt_s = zeroed_planes("wt_s", PASSES, K)
-        zero = keep.tile([P, 8], F32, name="zero")
-        nc.vector.memset(zero[:], 0.0)
-        g_row = keep.tile([P, S], F32, name="g_row")
-        nc.vector.memset(g_row[:], 0.0)
-
+        first_sizes = {"dy": 8 * T, "wb0": 4 * H}
+        later_sizes = {"wb1": 4 * H, "wb23": 8 * H, "wa0": 4 * K, "wa1": 4 * K, "wt": 4 * K, "a0": 8 * PACK * C, "a1": 8 * PACK * C,
+                       "wa_s": E * K, "wt_s": PASSES * K}
+        place, end = {}, 0
+        for name, size in list(first_sizes.items()) + list(later_sizes.items()):
+            place[name] = end
+            end = end + size
+        first_end = place["wb1"]
+        zero_first = loads.tile([P, first_end // 4], F32, name="zero_first", offset=0, align_bytes=64)
+        zero_later = loads.tile([P, (end - first_end) // 4], F32, name="zero_later", offset=first_end, align_bytes=64)
+        dy_s = zeroed_planes("dy_s", PASSES, T, nc.vector)
+        nc.gpsimd.memset(zero_first[:, 0:8], 0.0)
+        nc.gpsimd.memset(zero_later[:, 0:8], 0.0)
+        g_rows = keep.tile([P, C], F32, name="g_rows")
+        nc.vector.tensor_copy(g_rows[:], zero_first[:, 0:1].to_broadcast([P, C]))
+        wb_s = [zeroed_planes("wb_s0", 2 * PASSES, H, nc.vector), zeroed_planes("wb_s1", 2 * PASSES, H, nc.gpsimd)]
         ident = keep.tile([P, P], F32, name="ident")
         make_identity(nc, ident[:])
+        windows = {kt: keep.tile([P, T], F32, name=f"window{kt}") for kt in range(KT - 1)}
 
-        windows = [keep.tile([P, T], F32, name=f"window{kt}") for kt in range(KT)]
-        for kt in range(KT):
-            nc.scalar.activation(windows[kt][:], zero[:, 0:1].to_broadcast([P, T]), COPY)
+        def load_tile(name, shape, dtype):
+            return loads.tile(shape, dtype, name=name, offset=place[name], align_bytes=64)
 
-        dy_w = [keep.tile([P, T], I32, name=f"dy_w{s}", align_bytes=64) for s in range(PASSES)]
-        wb_w = [keep.tile([P, PASSES, FP4_BYTES * H], U8, name=f"wb_w{e}", align_bytes=64) for e in range(E)]
-        wa_w = [keep.tile([P, 2, FP4_BYTES * K], U8, name=f"wa_w{pair}", align_bytes=64) for pair in range(E // 2)]
-        wt_w = keep.tile([P, PASSES, FP4_BYTES * K], U8, name="wt_w", align_bytes=64)
-        a_sb = [keep.tile([P, PACK, 2 * C], F32, name=f"a_sb{pair}") for pair in range(E // 2)]
-        g_col = keep.tile([P, E], F32, name="g_col")
-
-        def load_dy(s):
-            nc.sync.dma_start(dy_w[s][:], dy_words[s].rearrange("p t d -> p (t d)").bitcast(I32))
+        dy_all = load_tile("dy", [P, PASSES, T], I32)
+        dy_w = [dy_all[:, s, :] for s in range(PASSES)]
+        wb_23 = load_tile("wb23", [P, 2 * PASSES, FP4_BYTES * H], U8)
+        wb_w = [load_tile(f"wb{e}", [P, PASSES, FP4_BYTES * H], U8)[:] for e in range(2)]
+        wb_w.extend([wb_23[:, 0:PASSES, :], wb_23[:, PASSES : 2 * PASSES, :]])
+        wa_w = [load_tile(f"wa{pair}", [P, 2, FP4_BYTES * K], U8) for pair in range(E // 2)]
+        wt_w = load_tile("wt", [P, PASSES, FP4_BYTES * K], U8)
+        a_sb = [load_tile(f"a{pair}", [P, PACK, 2 * C], F32) for pair in range(E // 2)]
+        g_col = keep.tile([P, 8], F32, name="g_col")
 
         def load_wb(e):
-            nc.sync.dma_start(wb_w[e][:].bitcast(I32), wbt_words[e].bitcast(I32).rearrange("s p w -> p s w"))
+            nc.sync.dma_start(wb_w[e].bitcast(I32), wbt_words[e].bitcast(I32).rearrange("s p w -> p s w"))
 
-        load_dy(0)
-        load_scales(dy_s, dy_scales, nc.sync)
-        load_dy(1)
-        load_wb(0)
-        load_scales(wb_s, wbt_scales.rearrange("e s b w -> (e s) b w"), nc.sync)
-        nc.sync.dma_start(g_row[0:1, :], gate[0:1, :])
-        load_scales(wa_s, wat_scales.rearrange("e s b w -> (e s) b w"), nc.gpsimd)
-        for e in range(1, E):
-            load_wb(e)
+        def load_wb_scales(pair, queue):
+            load_scales(wb_s[pair], wbt_scales[2 * pair : 2 * pair + 2].rearrange("e s b w -> (e s) b w"), queue)
+
         a_rows = a.rearrange("(p d) j -> p d j", d=PACK)
-        for pair in range(E // 2):
+
+        def load_a(pair):
             nc.sync.dma_start(a_sb[pair][:], a_rows[:, :, 2 * pair * C : 2 * (pair + 1) * C])
-        for pair in range(E // 2):
+
+        def load_wa(pair):
             words = wat_words[2 * pair : 2 * (pair + 1)].bitcast(I32).rearrange("e s p w -> p (e s) w")
             nc.sync.dma_start(wa_w[pair][:].bitcast(I32), words)
+
+        load_scales(dy_s, dy_scales, nc.sync)
+        nc.sync.dma_start(dy_all[:], dy_words.rearrange("s p t d -> p s (t d)").bitcast(I32))
+        load_wb(0)
+        nc.sync.dma_start(g_rows[0:E, :], gate[0:1, :].rearrange("o (e u) -> (o e) u", e=E))
+        load_wb_scales(0, nc.sync)
+        load_wb_scales(1, nc.gpsimd)
+        nc.scalar.activation(windows[0][:, 0:8], zero_later[:, 0:8], COPY)
+        wa_s = zeroed_planes("wa_s", E, K, nc.vector)
+        wt_s = zeroed_planes("wt_s", PASSES, K, nc.vector)
+        nc.scalar.activation(windows[0][:, 8:T], windows[0][:, 0:1].to_broadcast([P, T - 8]), COPY)
+        for kt in range(1, KT - 1):
+            nc.scalar.activation(windows[kt][:], windows[0][:, 0:1].to_broadcast([P, T]), COPY)
+        load_wb(1)
+        load_a(0)
+        load_wa(0)
+        load_scales(wa_s, wat_scales.rearrange("e s b w -> (e s) b w"), nc.sync)
+        load_a(1)
+        nc.sync.dma_start(wb_23[:].bitcast(I32), wbt_words[2:4].bitcast(I32).rearrange("e s p w -> p (e s) w"))
+        load_wa(1)
         load_scales(wt_s, wt_scales, nc.sync)
         nc.sync.dma_start(wt_w[:].bitcast(I32), wt_words.bitcast(I32).rearrange("s p w -> p s w"))
 
-        g_ps = psum.tile([P, E, P], F32, name="g_ps", tag="bank", bufs=BANKS)
-        for e in range(E):
-            nc.tensor.transpose(g_ps[:, e, :], g_row[:, e * C : (e + 1) * C], ident[:])
-        nc.scalar.copy(g_col[:], g_ps[:, :, 0])
+        g_ps = psum.tile([P, P], F32, name="g_ps", tag="bank_a")
+        nc.tensor.transpose(g_ps[:], g_rows[:], ident[:])
+        nc.scalar.copy(g_col[:, 0:E], g_ps[:, 0:E])
 
         slot_s = keep.tile([P, PASSES, S], U8, name="slot_s", align_bytes=64)
         slot_w = keep.tile([P, PASSES, S], U32, name="slot_w", align_bytes=64)
         dx = keep.tile([P, KT, S], F32, name="dx")
-        h_sb, dh, dh_w, dh_s, result = {}, {}, {}, {}, {}
+        mask, h_sb, dh, dh_w, dh_s, result = {}, {}, {}, {}, {}, {}
 
         def slots(e0, e1):
             return slice(e0 * C, e1 * C)
@@ -114,62 +140,79 @@ def tile_moe_adb_relu_kernel(
             return offsets[:, e0 * C // LIST_ROWS : e1 * C // LIST_ROWS]
 
         def gather_words(s, e0, e1):
-            nc.vector.tensor_copy(slot_w[:, s, slots(e0, e1)], dy_w[s][:].bitcast(U32).indirect(slot_offsets(e0, e1)))
+            nc.vector.tensor_copy(slot_w[:, s, slots(e0, e1)], dy_w[s].bitcast(U32).indirect(slot_offsets(e0, e1)))
 
         def gather_scales(s, e0, e1):
             nc.vector.tensor_copy(slot_s[:, s, slots(e0, e1)], dy_s[:, s, :].indirect(slot_offsets(e0, e1)))
 
+        def make_mask(pair):
+            mask[pair] = keep.tile([P, 2 * C, PACK], BF16, name=f"mask{pair}", tag=f"mask_slot{pair}", align_bytes=64)
+            nc.vector.tensor_scalar(
+                out=mask[pair][:],
+                in0=a_sb[pair][:].rearrange("p d u -> p u d"),
+                scalar1=0.0,
+                scalar2=None,
+                op0=ALU.is_gt,
+            )
+
         def first_product(e):
-            h_ps = psum.tile([P, H], F32, name="h_ps", tag="bank", bufs=BANKS)
+            h_ps = psum.tile([P, H], F32, name="h_ps", tag=["bank_b", "bank_c", "bank_e", "bank_c"][e])
             for s in range(PASSES):
                 nc.tensor.matmul_mx(
                     out=h_ps[:],
                     lhsT=slot_w[:, s, slots(e, e + 1)].bitcast(FP8X4),
                     lhsT_scale=slot_s[:, s, slots(e, e + 1)],
                     rhs=wb_w[e][:, s, :].bitcast(FP4X4),
-                    rhs_scale=wb_s[:, e * PASSES + s, :],
+                    rhs_scale=wb_s[e // 2][:, (e % 2) * PASSES + s, :],
                     start=(s == 0),
                     stop=(s == PASSES - 1),
                 )
-            h_sb[e] = keep.tile([P, PACK, P], F32, name=f"h_sb{e}")
+            h_sb[e] = keep.tile([P, 2, P, 2], BF16, name=f"h_sb{e}", tag=f"h_slot{e}")
             nc.scalar.activation(
-                h_sb[e][:], h_ps[:].rearrange("u (m d) -> u d m", d=PACK), COPY, scale=g_col[:, e : e + 1]
+                h_sb[e][:], h_ps[:].rearrange("u (m w t) -> u w m t", w=2, t=2), COPY, scale=g_col[:, e : e + 1]
             )
 
-        def turn_and_mask(e):
-            turned = psum.tile([P, PACK, C], F32, name="turned", tag="bank", bufs=BANKS)
-            for d in range(PACK):
-                nc.tensor.transpose(turned[:, d, :], h_sb[e][:, d, :], ident[:])
-            dh[e] = keep.tile([P, C, PACK], BF16, name=f"dh{e}", align_bytes=64)
-            nc.vector.scalar_tensor_tensor(
-                out=dh[e][:],
-                in0=a_sb[e // 2][:, :, slots(e % 2, e % 2 + 1)].rearrange("p d u -> p u d"),
-                scalar=0.0,
-                in1=turned[:].rearrange("p d u -> p u d"),
-                op0=ALU.is_gt,
-                op1=ALU.mult,
+        def turn_and_mask(e0, e1, bank):
+            count = e1 - e0
+            turned = psum.tile([P, 2, count * C], F32, name="turned", tag=bank)
+            for e in range(e0, e1):
+                pairs = h_sb[e][:].rearrange("u w m t -> u (w m t)").bitcast(F32)
+                for w in range(2):
+                    nc.tensor.transpose(turned[:, w, slots(e - e0, e - e0 + 1)], pairs[:, w * P : (w + 1) * P], ident[:])
+            slot = "mask_slot1" if e0 == 1 else f"dh_slot{e0}"
+            dh[e0] = keep.tile([P, count * C, 2, 2], BF16, name=f"dh{e0}", tag=slot, align_bytes=64)
+            values = turned[:].rearrange("p w u -> p (w u)").bitcast(BF16).rearrange("p (w u t) -> p u w t", w=2, t=2)
+            nc.vector.tensor_tensor(
+                dh[e0][:],
+                values,
+                mask[e0 // 2][:, slots(e0 % 2, e0 % 2 + count), :].rearrange("p u (w t) -> p u w t", w=2),
+                ALU.mult,
             )
 
-        def quantize(e):
-            dh_w[e] = keep.tile([P, C], U32, name=f"dh_w{e}", align_bytes=64)
-            dh_s[e] = keep.tile([P, C], U8, name=f"dh_s{e}", align_bytes=64)
+        def quantize(e0, e1):
+            count = e1 - e0
+            words = keep.tile([P, count * C], U32, name=f"dh_w{e0}", tag=f"words_slot{e0}", align_bytes=64)
+            scales = keep.tile([P, count * C], U8, name=f"dh_s{e0}", tag=f"scales_slot{e0}", align_bytes=64)
             nc.vector.quantize_mx(
-                out=dh_w[e][:].bitcast(FP8X4), scales=dh_s[e][:], in_=dh[e][:].rearrange("p u d -> p (u d)")
+                out=words[:].bitcast(FP8X4), scales=scales[:], in_=dh[e0][:].rearrange("p u w t -> p (u w t)")
             )
+            for e in range(e0, e1):
+                dh_w[e] = words[:, slots(e - e0, e - e0 + 1)]
+                dh_s[e] = scales[:, slots(e - e0, e - e0 + 1)]
 
-        def second_product(e):
-            dx_ps = psum.tile([P, KT, C], F32, name="dx_ps", tag="bank", bufs=BANKS)
-            for kt in range(KT):
+        def second_product(e, kt0, kt1, bank):
+            dx_ps = psum.tile([P, kt1 - kt0, C], F32, name="dx_ps", tag=bank)
+            for kt in range(kt0, kt1):
                 nc.tensor.matmul_mx(
-                    out=dx_ps[:, kt, :],
+                    out=dx_ps[:, kt - kt0, :],
                     lhsT=wa_w[e // 2][:, e % 2, FP4_BYTES * kt * P : FP4_BYTES * (kt + 1) * P].bitcast(FP4X4),
                     lhsT_scale=wa_s[:, e, kt * P : (kt + 1) * P],
-                    rhs=dh_w[e][:].bitcast(FP8X4),
-                    rhs_scale=dh_s[e][:],
+                    rhs=dh_w[e].bitcast(FP8X4),
+                    rhs_scale=dh_s[e],
                     start=True,
                     stop=True,
                 )
-            nc.scalar.copy(dx[:, :, slots(e, e + 1)], dx_ps[:])
+            nc.scalar.copy(dx[:, kt0:kt1, slots(e, e + 1)], dx_ps[:])
 
         def scatter(kt, e0, e1):
             nc.vector.tensor_copy(windows[kt][:].indirect(slot_offsets(e0, e1)), dx[:, kt, slots(e0, e1)])
@@ -178,7 +221,7 @@ def tile_moe_adb_relu_kernel(
             return slice(half * BANK, (half + 1) * BANK)
 
         def base_product(kt, half):
-            base_ps = psum.tile([P, BANK], F32, name="base_ps", tag="bank", bufs=BANKS)
+            base_ps = psum.tile([P, BANK], F32, name="base_ps", tag=[["bank_f", "bank_g"], ["bank_d", "bank_c"]][kt % 2][half])
             for s in range(PASSES):
                 nc.tensor.matmul_mx(
                     out=base_ps[:],
@@ -189,41 +232,49 @@ def tile_moe_adb_relu_kernel(
                     start=(s == 0),
                     stop=(s == PASSES - 1),
                 )
-            result[kt, half] = keep.tile([P, BANK], F32, name=f"result{kt}_{half}")
+            slot = ["words_slot2", "scales_slot2"][half] if kt == KT - 1 else f"result_slot{kt}_{half}"
+            result[kt, half] = keep.tile([P, BANK], F32, name=f"result{kt}_{half}", tag=slot, align_bytes=64)
             return base_ps
 
         def store(kt, half):
-            nc.sync.dma_start(out[kt * P : (kt + 1) * P, tokens(half)], result[kt, half][:])
+            queue = nc.scalar if kt == 0 else nc.sync
+            queue.dma_start(out[kt * P : (kt + 1) * P, tokens(half)], result[kt, half][:])
 
-        gather_words(0, 0, E)
+        for s in range(PASSES):
+            gather_scales(s, 0, E)
         for e0 in range(0, E, 2):
             for s in range(PASSES):
-                gather_scales(s, e0, e0 + 2)
-            gather_words(1, e0, e0 + 2)
-            first_product(e0)
+                gather_words(s, e0, e0 + 2)
             if e0 == 0:
+                first_product(0)
                 first_product(1)
-
-        turn_and_mask(0)
+        make_mask(0)
+        turn_and_mask(0, 1, "bank_d")
+        quantize(0, 1)
+        turn_and_mask(1, 2, "bank_a")
+        second_product(0, 0, 1, "bank_e")
+        second_product(0, 1, KT, "bank_c")
+        quantize(1, 2)
+        second_product(1, 0, KT, "bank_b")
+        make_mask(1)
+        first_product(2)
         first_product(3)
-        quantize(0)
-        turn_and_mask(1)
-        turn_and_mask(2)
-        quantize(1)
-        turn_and_mask(3)
-        quantize(2)
-        second_product(0)
-        quantize(3)
-        second_product(1)
+        scatter(0, 0, 1)
+        scatter(1, 0, 1)
+        scatter(2, 0, 2)
+        turn_and_mask(2, E, "bank_d")
+        windows[3] = keep.tile([P, T], F32, name="window3", tag="h_slot3")
+        nc.scalar.activation(windows[3][:], ident[:, 0:1].to_broadcast([P, T]), COPY, scale=0.0)
+        quantize(2, E)
+        second_product(2, 0, KT, "bank_f")
+        second_product(3, 0, KT, "bank_g")
+        scatter(3, 0, 2)
+        scatter(3, 2, 3)
 
-        early = [1, 2, 0, 0]
-        scatter(0, 0, early[0])
-        second_product(2)
-        second_product(3)
-        scatter(1, 0, early[1])
-
-        for kt in range(KT):
-            on_gpsimd = kt < KT - 1
+        early = [1, 1, 2, 3]
+        order = [3, 2, 1, 0]
+        for kt in order:
+            on_gpsimd = kt != order[-1]
             banks = []
             for half in range(HALVES):
                 banks.append(base_product(kt, half))

@@ -54,8 +54,8 @@ def tile_moe_adb_relu_kernel(
             for r in range(4):
                 queue.dma_start(planes[r:P:32, :, :].bitcast(I32), by_r[r])
 
-        first_sizes = {"dy": 8 * T, "wb0": 4 * H}
-        later_sizes = {"wb1": 4 * H, "wb23": 8 * H, "wa0": 4 * K, "wa1": 4 * K, "wt": 4 * K, "a0": 8 * PACK * C, "a1": 8 * PACK * C,
+        first_sizes = {"dy1": 4 * T, "wb0": 4 * H}
+        later_sizes = {"wb1": 4 * H, "wb2": 4 * H, "wb3": 4 * H, "wa0": 4 * K, "wa1": 4 * K, "wt": 4 * K, "a0": 8 * PACK * C, "a1": 8 * PACK * C,
                        "wa_s": E * K, "wt_s": PASSES * K}
         place, end = {}, 0
         for name, size in list(first_sizes.items()) + list(later_sizes.items()):
@@ -67,21 +67,18 @@ def tile_moe_adb_relu_kernel(
         dy_s = zeroed_planes("dy_s", PASSES, T, nc.vector)
         nc.gpsimd.memset(zero_first[:, 0:8], 0.0)
         nc.gpsimd.memset(zero_later[:, 0:8], 0.0)
-        g_rows = keep.tile([P, C], F32, name="g_rows")
+        g_rows = keep.tile([P, C], F32, name="g_rows", tag="gate_slot", align_bytes=64)
         nc.vector.tensor_copy(g_rows[:], zero_first[:, 0:1].to_broadcast([P, C]))
         wb_s = [zeroed_planes("wb_s0", 2 * PASSES, H, nc.vector), zeroed_planes("wb_s1", 2 * PASSES, H, nc.gpsimd)]
         ident = keep.tile([P, P], F32, name="ident")
         make_identity(nc, ident[:])
-        windows = {kt: keep.tile([P, T], F32, name=f"window{kt}") for kt in range(KT - 1)}
+        windows = {kt: keep.tile([P, T], F32, name=f"window{kt}") for kt in range(KT)}
 
         def load_tile(name, shape, dtype):
             return loads.tile(shape, dtype, name=name, offset=place[name], align_bytes=64)
 
-        dy_all = load_tile("dy", [P, PASSES, T], I32)
-        dy_w = [dy_all[:, s, :] for s in range(PASSES)]
-        wb_23 = load_tile("wb23", [P, 2 * PASSES, FP4_BYTES * H], U8)
-        wb_w = [load_tile(f"wb{e}", [P, PASSES, FP4_BYTES * H], U8)[:] for e in range(2)]
-        wb_w.extend([wb_23[:, 0:PASSES, :], wb_23[:, PASSES : 2 * PASSES, :]])
+        dy_w = [keep.tile([P, T], I32, name="dy0", align_bytes=64)[:], load_tile("dy1", [P, T], I32)[:]]
+        wb_w = [load_tile(f"wb{e}", [P, PASSES, FP4_BYTES * H], U8)[:] for e in range(E)]
         wa_w = [load_tile(f"wa{pair}", [P, 2, FP4_BYTES * K], U8) for pair in range(E // 2)]
         wt_w = load_tile("wt", [P, PASSES, FP4_BYTES * K], U8)
         a_sb = [load_tile(f"a{pair}", [P, PACK, 2 * C], F32) for pair in range(E // 2)]
@@ -102,8 +99,9 @@ def tile_moe_adb_relu_kernel(
             words = wat_words[2 * pair : 2 * (pair + 1)].bitcast(I32).rearrange("e s p w -> p (e s) w")
             nc.sync.dma_start(wa_w[pair][:].bitcast(I32), words)
 
+        nc.sync.dma_start(dy_w[0], dy_words[0].rearrange("p t d -> p (t d)").bitcast(I32))
         load_scales(dy_s, dy_scales, nc.sync)
-        nc.sync.dma_start(dy_all[:], dy_words.rearrange("s p t d -> p s (t d)").bitcast(I32))
+        nc.sync.dma_start(dy_w[1], dy_words[1].rearrange("p t d -> p (t d)").bitcast(I32))
         load_wb(0)
         nc.sync.dma_start(g_rows[0:E, :], gate[0:1, :].rearrange("o (e u) -> (o e) u", e=E))
         load_wb_scales(0, nc.sync)
@@ -112,14 +110,15 @@ def tile_moe_adb_relu_kernel(
         wa_s = zeroed_planes("wa_s", E, K, nc.vector)
         wt_s = zeroed_planes("wt_s", PASSES, K, nc.vector)
         nc.scalar.activation(windows[0][:, 8:T], windows[0][:, 0:1].to_broadcast([P, T - 8]), COPY)
-        for kt in range(1, KT - 1):
+        for kt in range(1, KT):
             nc.scalar.activation(windows[kt][:], windows[0][:, 0:1].to_broadcast([P, T]), COPY)
         load_wb(1)
         load_a(0)
+        load_wb(2)
+        load_a(1)
         load_wa(0)
         load_scales(wa_s, wat_scales.rearrange("e s b w -> (e s) b w"), nc.sync)
-        load_a(1)
-        nc.sync.dma_start(wb_23[:].bitcast(I32), wbt_words[2:4].bitcast(I32).rearrange("e s p w -> p (e s) w"))
+        load_wb(3)
         load_wa(1)
         load_scales(wt_s, wt_scales, nc.sync)
         nc.sync.dma_start(wt_w[:].bitcast(I32), wt_words.bitcast(I32).rearrange("s p w -> p s w"))
@@ -128,7 +127,7 @@ def tile_moe_adb_relu_kernel(
         nc.tensor.transpose(g_ps[:], g_rows[:], ident[:])
         nc.scalar.copy(g_col[:, 0:E], g_ps[:, 0:E])
 
-        slot_s = keep.tile([P, PASSES, S], U8, name="slot_s", align_bytes=64)
+        slot_s = {(0, s): keep.tile([P, 2 * C], U8, name=f"slot_s0{s}", align_bytes=64)[:] for s in range(PASSES)}
         slot_w = keep.tile([P, PASSES, S], U32, name="slot_w", align_bytes=64)
         dx = keep.tile([P, KT, S], F32, name="dx")
         mask, h_sb, dh, dh_w, dh_s, result = {}, {}, {}, {}, {}, {}
@@ -143,31 +142,27 @@ def tile_moe_adb_relu_kernel(
             nc.vector.tensor_copy(slot_w[:, s, slots(e0, e1)], dy_w[s].bitcast(U32).indirect(slot_offsets(e0, e1)))
 
         def gather_scales(s, e0, e1):
-            nc.vector.tensor_copy(slot_s[:, s, slots(e0, e1)], dy_s[:, s, :].indirect(slot_offsets(e0, e1)))
+            nc.vector.tensor_copy(slot_s[e0 // 2, s], dy_s[:, s, :].indirect(slot_offsets(e0, e1)))
 
-        def make_mask(pair):
-            mask[pair] = keep.tile([P, 2 * C, PACK], BF16, name=f"mask{pair}", tag=f"mask_slot{pair}", align_bytes=64)
+        def make_mask(pair, slot):
+            mask[pair] = keep.tile([P, 2 * C, PACK], BF16, name=f"mask{pair}", tag=slot, align_bytes=64)
             nc.vector.tensor_scalar(
-                out=mask[pair][:],
-                in0=a_sb[pair][:].rearrange("p d u -> p u d"),
-                scalar1=0.0,
-                scalar2=None,
-                op0=ALU.is_gt,
+                out=mask[pair][:], in0=a_sb[pair][:].rearrange("p d u -> p u d"), scalar1=0.0, scalar2=None, op0=ALU.is_gt
             )
 
         def first_product(e):
-            h_ps = psum.tile([P, H], F32, name="h_ps", tag=["bank_b", "bank_c", "bank_e", "bank_c"][e])
+            h_ps = psum.tile([P, H], F32, name="h_ps", tag=["bank_b", "bank_c", "bank_b", "bank_e"][e])
             for s in range(PASSES):
                 nc.tensor.matmul_mx(
                     out=h_ps[:],
                     lhsT=slot_w[:, s, slots(e, e + 1)].bitcast(FP8X4),
-                    lhsT_scale=slot_s[:, s, slots(e, e + 1)],
+                    lhsT_scale=slot_s[e // 2, s][:, slots(e % 2, e % 2 + 1)],
                     rhs=wb_w[e][:, s, :].bitcast(FP4X4),
                     rhs_scale=wb_s[e // 2][:, (e % 2) * PASSES + s, :],
                     start=(s == 0),
                     stop=(s == PASSES - 1),
                 )
-            h_sb[e] = keep.tile([P, 2, P, 2], BF16, name=f"h_sb{e}", tag=f"h_slot{e}")
+            h_sb[e] = keep.tile([P, 2, P, 2], BF16, name=f"h_sb{e}", tag=f"h_slot{e}", align_bytes=64)
             nc.scalar.activation(
                 h_sb[e][:], h_ps[:].rearrange("u (m w t) -> u w m t", w=2, t=2), COPY, scale=g_col[:, e : e + 1]
             )
@@ -179,8 +174,7 @@ def tile_moe_adb_relu_kernel(
                 pairs = h_sb[e][:].rearrange("u w m t -> u (w m t)").bitcast(F32)
                 for w in range(2):
                     nc.tensor.transpose(turned[:, w, slots(e - e0, e - e0 + 1)], pairs[:, w * P : (w + 1) * P], ident[:])
-            slot = "mask_slot1" if e0 == 1 else f"dh_slot{e0}"
-            dh[e0] = keep.tile([P, count * C, 2, 2], BF16, name=f"dh{e0}", tag=slot, align_bytes=64)
+            dh[e0] = keep.tile([P, count * C, 2, 2], BF16, name=f"dh{e0}", tag=f"dh_slot{e0}", align_bytes=64)
             values = turned[:].rearrange("p w u -> p (w u)").bitcast(BF16).rearrange("p (w u t) -> p u w t", w=2, t=2)
             nc.vector.tensor_tensor(
                 dh[e0][:],
@@ -200,19 +194,25 @@ def tile_moe_adb_relu_kernel(
                 dh_w[e] = words[:, slots(e - e0, e - e0 + 1)]
                 dh_s[e] = scales[:, slots(e - e0, e - e0 + 1)]
 
-        def second_product(e, kt0, kt1, bank):
+        def second_product(e, kt, target):
+            nc.tensor.matmul_mx(
+                out=target,
+                lhsT=wa_w[e // 2][:, e % 2, FP4_BYTES * kt * P : FP4_BYTES * (kt + 1) * P].bitcast(FP4X4),
+                lhsT_scale=wa_s[:, e, kt * P : (kt + 1) * P],
+                rhs=dh_w[e].bitcast(FP8X4),
+                rhs_scale=dh_s[e],
+                start=True,
+                stop=True,
+            )
+
+        def dx_tiles(e, kt0, kt1, bank):
             dx_ps = psum.tile([P, kt1 - kt0, C], F32, name="dx_ps", tag=bank)
             for kt in range(kt0, kt1):
-                nc.tensor.matmul_mx(
-                    out=dx_ps[:, kt - kt0, :],
-                    lhsT=wa_w[e // 2][:, e % 2, FP4_BYTES * kt * P : FP4_BYTES * (kt + 1) * P].bitcast(FP4X4),
-                    lhsT_scale=wa_s[:, e, kt * P : (kt + 1) * P],
-                    rhs=dh_w[e].bitcast(FP8X4),
-                    rhs_scale=dh_s[e],
-                    start=True,
-                    stop=True,
-                )
+                second_product(e, kt, dx_ps[:, kt - kt0, :])
             nc.scalar.copy(dx[:, kt0:kt1, slots(e, e + 1)], dx_ps[:])
+
+        def scatter_from(source, kt, e):
+            nc.vector.tensor_copy(windows[kt][:].indirect(slot_offsets(e, e + 1)), source)
 
         def scatter(kt, e0, e1):
             nc.vector.tensor_copy(windows[kt][:].indirect(slot_offsets(e0, e1)), dx[:, kt, slots(e0, e1)])
@@ -221,7 +221,7 @@ def tile_moe_adb_relu_kernel(
             return slice(half * BANK, (half + 1) * BANK)
 
         def base_product(kt, half):
-            base_ps = psum.tile([P, BANK], F32, name="base_ps", tag=[["bank_f", "bank_g"], ["bank_d", "bank_c"]][kt % 2][half])
+            base_ps = psum.tile([P, BANK], F32, name="base_ps", tag="bank_c" if (kt, half) == (0, 0) else ["bank_a", "bank_f", "bank_g"][(HALVES * kt + half) % 3])
             for s in range(PASSES):
                 nc.tensor.matmul_mx(
                     out=base_ps[:],
@@ -232,47 +232,55 @@ def tile_moe_adb_relu_kernel(
                     start=(s == 0),
                     stop=(s == PASSES - 1),
                 )
-            slot = ["words_slot2", "scales_slot2"][half] if kt == KT - 1 else f"result_slot{kt}_{half}"
-            result[kt, half] = keep.tile([P, BANK], F32, name=f"result{kt}_{half}", tag=slot, align_bytes=64)
+            result[kt, half] = keep.tile([P, BANK], F32, name=f"result{kt}_{half}")
             return base_ps
 
-        def store(kt, half):
-            queue = nc.scalar if kt == 0 else nc.sync
-            queue.dma_start(out[kt * P : (kt + 1) * P, tokens(half)], result[kt, half][:])
+        def store(kt, half, c0, c1):
+            queue = nc.scalar if (kt, half) == (KT - 1, 0) else nc.sync
+            queue.dma_start(out[kt * P : (kt + 1) * P, half * BANK + c0 : half * BANK + c1], result[kt, half][:, c0:c1])
 
+        gather_words(0, 0, E)
         for s in range(PASSES):
-            gather_scales(s, 0, E)
-        for e0 in range(0, E, 2):
-            for s in range(PASSES):
-                gather_words(s, e0, e0 + 2)
-            if e0 == 0:
-                first_product(0)
-                first_product(1)
-        make_mask(0)
+            gather_scales(s, 0, 2)
+        gather_words(1, 0, 2)
+        first_product(0)
+        first_product(1)
+        gather_words(1, 2, E)
+        second_scales = keep.tile([P, PASSES, 2 * C], U8, name="second_scales", tag="gate_slot", align_bytes=64)
+        for s in range(PASSES):
+            slot_s[1, s] = second_scales[:, s, :]
+            gather_scales(s, 2, E)
+        make_mask(0, "mask_slot0")
         turn_and_mask(0, 1, "bank_d")
         quantize(0, 1)
         turn_and_mask(1, 2, "bank_a")
-        second_product(0, 0, 1, "bank_e")
-        second_product(0, 1, KT, "bank_c")
-        quantize(1, 2)
-        second_product(1, 0, KT, "bank_b")
-        make_mask(1)
+        make_mask(1, "h_slot1")
+        dx_tiles(0, 0, 1, "bank_e")
+        dx_tiles(0, 1, KT - 1, "bank_c")
+        kept = psum.tile([P, 2, C], F32, name="kept", tag="bank_d")
+        second_product(0, KT - 1, kept[:, 0, :])
         first_product(2)
+        quantize(1, 2)
         first_product(3)
-        scatter(0, 0, 1)
-        scatter(1, 0, 1)
-        scatter(2, 0, 2)
-        turn_and_mask(2, E, "bank_d")
-        windows[3] = keep.tile([P, T], F32, name="window3", tag="h_slot3")
-        nc.scalar.activation(windows[3][:], ident[:, 0:1].to_broadcast([P, T]), COPY, scale=0.0)
+        second_product(1, 0, kept[:, 1, :])
+        dx_tiles(1, 1, KT, "bank_h")
+        for kt in range(KT - 1):
+            scatter(kt, 0, 1)
+        turn_and_mask(2, E, "bank_e")
         quantize(2, E)
-        second_product(2, 0, KT, "bank_f")
-        second_product(3, 0, KT, "bank_g")
-        scatter(3, 0, 2)
-        scatter(3, 2, 3)
+        after_mask = keep.tile([P, 2, C], F32, name="after_mask", tag="h_slot1", align_bytes=64)
+        nc.scalar.copy(after_mask[:], kept[:])
+        scatter_from(after_mask[:, 1, :], 0, 1)
+        scatter_from(after_mask[:, 0, :], KT - 1, 0)
+        first_tile = psum.tile([P, 2, C], F32, name="first_tile", tag="bank_f")
+        for e in range(2, E):
+            second_product(e, 0, first_tile[:, e - 2, :])
+        nc.scalar.copy(dx[:, 0, slots(2, E)], first_tile[:].rearrange("p e u -> p (e u)"))
+        dx_tiles(2, 1, KT, "bank_g")
+        dx_tiles(3, 1, KT, "bank_a")
 
-        early = [1, 1, 2, 3]
-        order = [3, 2, 1, 0]
+        early = [2, 1, 1, 1]
+        order = [0, 1, 2, 3]
         for kt in order:
             on_gpsimd = kt != order[-1]
             banks = []
@@ -286,6 +294,7 @@ def tile_moe_adb_relu_kernel(
                 scattered = windows[kt][:, tokens(half)]
                 if on_gpsimd:
                     nc.gpsimd.tensor_tensor(total[:], total[:], scattered, ALU.add)
+                    store(kt, half, 0, BANK)
                 else:
                     nc.vector.tensor_tensor(total[:], scattered, banks[half][:], ALU.add)
-                store(kt, half)
+                    store(kt, half, 0, BANK)

@@ -144,28 +144,36 @@ def tile_moe_adb_relu_kernel(
         def gather_scales(s, e0, e1):
             nc.vector.tensor_copy(slot_s[e0 // 2, s], dy_s[:, s, :].indirect(slot_offsets(e0, e1)))
 
-        def make_mask(pair, slot):
-            mask[pair] = keep.tile([P, 2 * C, PACK], BF16, name=f"mask{pair}", tag=slot, align_bytes=64)
-            nc.vector.tensor_scalar(
-                out=mask[pair][:], in0=a_sb[pair][:].rearrange("p d u -> p u d"), scalar1=0.0, scalar2=None, op0=ALU.is_gt
-            )
+        def make_mask(e0, e1, slot):
+            tile = keep.tile([P, (e1 - e0) * C, PACK], BF16, name=f"mask{e0}", tag=slot, align_bytes=64)
+            values = a_sb[e0 // 2][:, :, slots(e0 % 2, e0 % 2 + e1 - e0)].rearrange("p d u -> p u d")
+            nc.vector.tensor_scalar(out=tile[:], in0=values, scalar1=0.0, scalar2=None, op0=ALU.is_gt)
+            mask[e0] = tile
 
-        def first_product(e):
-            h_ps = psum.tile([P, H], F32, name="h_ps", tag=["bank_b", "bank_c", "bank_b", "bank_e"][e])
-            for s in range(PASSES):
-                nc.tensor.matmul_mx(
-                    out=h_ps[:],
-                    lhsT=slot_w[:, s, slots(e, e + 1)].bitcast(FP8X4),
-                    lhsT_scale=slot_s[e // 2, s][:, slots(e % 2, e % 2 + 1)],
-                    rhs=wb_w[e][:, s, :].bitcast(FP4X4),
-                    rhs_scale=wb_s[e // 2][:, (e % 2) * PASSES + s, :],
-                    start=(s == 0),
-                    stop=(s == PASSES - 1),
-                )
+        def first_product(e, banks):
             h_sb[e] = keep.tile([P, 2, P, 2], BF16, name=f"h_sb{e}", tag=f"h_slot{e}", align_bytes=64)
-            nc.scalar.activation(
-                h_sb[e][:], h_ps[:].rearrange("u (m w t) -> u w m t", w=2, t=2), COPY, scale=g_col[:, e : e + 1]
-            )
+            part = H // len(banks)
+            width = H if len(banks) == 1 else C
+            for n, bank in enumerate(banks):
+                h_ps = psum.tile([P, part], F32, name="h_ps", tag=bank)
+                for c0 in range(0, part, width):
+                    i0 = n * part + c0
+                    for s in range(PASSES):
+                        nc.tensor.matmul_mx(
+                            out=h_ps[:, c0 : c0 + width],
+                            lhsT=slot_w[:, s, slots(e, e + 1)].bitcast(FP8X4),
+                            lhsT_scale=slot_s[e // 2, s][:, slots(e % 2, e % 2 + 1)],
+                            rhs=wb_w[e][:, s, FP4_BYTES * i0 : FP4_BYTES * (i0 + width)].bitcast(FP4X4),
+                            rhs_scale=wb_s[e // 2][:, (e % 2) * PASSES + s, i0 : i0 + width],
+                            start=(s == 0),
+                            stop=(s == PASSES - 1),
+                        )
+                nc.scalar.activation(
+                    h_sb[e][:, :, n * part // PACK : (n + 1) * part // PACK, :],
+                    h_ps[:].rearrange("u (m w t) -> u w m t", w=2, t=2),
+                    COPY,
+                    scale=g_col[:, e : e + 1],
+                )
 
         def turn_and_mask(e0, e1, bank):
             count = e1 - e0
@@ -179,7 +187,7 @@ def tile_moe_adb_relu_kernel(
             nc.vector.tensor_tensor(
                 dh[e0][:],
                 values,
-                mask[e0 // 2][:, slots(e0 % 2, e0 % 2 + count), :].rearrange("p u (w t) -> p u w t", w=2),
+                mask[e0][:].rearrange("p u (w t) -> p u w t", w=2),
                 ALU.mult,
             )
 
@@ -236,32 +244,33 @@ def tile_moe_adb_relu_kernel(
             return base_ps
 
         def store(kt, half, c0, c1):
-            queue = nc.scalar if (kt, half) == (KT - 1, 0) else nc.sync
+            queue = nc.scalar if kt == KT - 1 and c0 == 0 else nc.sync
             queue.dma_start(out[kt * P : (kt + 1) * P, half * BANK + c0 : half * BANK + c1], result[kt, half][:, c0:c1])
 
         gather_words(0, 0, E)
         for s in range(PASSES):
             gather_scales(s, 0, 2)
         gather_words(1, 0, 2)
-        first_product(0)
-        first_product(1)
+        first_product(0, ["bank_f", "bank_b"])
+        first_product(1, ["bank_c"])
         gather_words(1, 2, E)
         second_scales = keep.tile([P, PASSES, 2 * C], U8, name="second_scales", tag="gate_slot", align_bytes=64)
         for s in range(PASSES):
             slot_s[1, s] = second_scales[:, s, :]
             gather_scales(s, 2, E)
-        make_mask(0, "mask_slot0")
+        make_mask(0, 1, "mask_slot0")
         turn_and_mask(0, 1, "bank_d")
+        make_mask(1, 2, "h_slot0")
         quantize(0, 1)
         turn_and_mask(1, 2, "bank_a")
-        make_mask(1, "h_slot1")
+        make_mask(2, E, "h_slot1")
         dx_tiles(0, 0, 1, "bank_e")
         dx_tiles(0, 1, KT - 1, "bank_c")
         kept = psum.tile([P, 2, C], F32, name="kept", tag="bank_d")
         second_product(0, KT - 1, kept[:, 0, :])
-        first_product(2)
+        first_product(2, ["bank_b"])
         quantize(1, 2)
-        first_product(3)
+        first_product(3, ["bank_e"])
         second_product(1, 0, kept[:, 1, :])
         dx_tiles(1, 1, KT, "bank_h")
         for kt in range(KT - 1):
@@ -296,5 +305,7 @@ def tile_moe_adb_relu_kernel(
                     nc.gpsimd.tensor_tensor(total[:], total[:], scattered, ALU.add)
                     store(kt, half, 0, BANK)
                 else:
-                    nc.vector.tensor_tensor(total[:], scattered, banks[half][:], ALU.add)
-                    store(kt, half, 0, BANK)
+                    cuts = [0, BANK] if half == 0 else [0, BANK // 2, BANK]
+                    for c0, c1 in zip(cuts, cuts[1:]):
+                        nc.vector.tensor_tensor(total[:, c0:c1], scattered[:, c0:c1], banks[half][:, c0:c1], ALU.add)
+                        store(kt, half, c0, c1)

@@ -240,12 +240,11 @@ def tile_moe_adb_relu_kernel(
                     start=(s == 0),
                     stop=(s == PASSES - 1),
                 )
-            result[kt, half] = keep.tile([P, BANK], F32, name=f"result{kt}_{half}")
             return base_ps
 
-        def store(kt, half, c0, c1):
-            queue = nc.scalar if kt == KT - 1 and c0 == 0 else nc.sync
-            queue.dma_start(out[kt * P : (kt + 1) * P, half * BANK + c0 : half * BANK + c1], result[kt, half][:, c0:c1])
+        def store(kt, total, c0, c1):
+            queue = nc.scalar if kt == KT - 1 and c0 % BANK == 0 else nc.sync
+            queue.dma_start(out[kt * P : (kt + 1) * P, c0:c1], total[:, c0:c1])
 
         gather_words(0, 0, E)
         for s in range(PASSES):
@@ -275,6 +274,7 @@ def tile_moe_adb_relu_kernel(
         dx_tiles(1, 1, KT, "bank_h")
         for kt in range(KT - 1):
             scatter(kt, 0, 1)
+        scatter(1, 1, 2)
         turn_and_mask(2, E, "bank_e")
         quantize(2, E)
         after_mask = keep.tile([P, 2, C], F32, name="after_mask", tag="h_slot1", align_bytes=64)
@@ -288,24 +288,21 @@ def tile_moe_adb_relu_kernel(
         dx_tiles(2, 1, KT, "bank_g")
         dx_tiles(3, 1, KT, "bank_a")
 
-        early = [2, 1, 1, 1]
-        order = [0, 1, 2, 3]
-        for kt in order:
-            on_gpsimd = kt != order[-1]
+        early = [2, 2, 1, 1]
+        for kt in range(KT):
+            on_gpsimd = kt < KT - 1
+            total = keep.tile([P, T], F32, name=f"total{kt}", align_bytes=64)
             banks = []
             for half in range(HALVES):
                 banks.append(base_product(kt, half))
                 if on_gpsimd:
-                    nc.scalar.copy(result[kt, half][:], banks[half][:])
+                    nc.scalar.copy(total[:, tokens(half)], banks[half][:])
             scatter(kt, early[kt], E)
-            for half in range(HALVES):
-                total = result[kt, half]
-                scattered = windows[kt][:, tokens(half)]
+            cuts = [[0, BANK, T], [0, T], [0, BANK, T], [0, BANK, BANK + BANK // 2, T]][kt]
+            for c0, c1 in zip(cuts, cuts[1:]):
                 if on_gpsimd:
-                    nc.gpsimd.tensor_tensor(total[:], total[:], scattered, ALU.add)
-                    store(kt, half, 0, BANK)
+                    nc.gpsimd.tensor_tensor(total[:, c0:c1], total[:, c0:c1], windows[kt][:, c0:c1], ALU.add)
                 else:
-                    cuts = [0, BANK] if half == 0 else [0, BANK // 2, BANK]
-                    for c0, c1 in zip(cuts, cuts[1:]):
-                        nc.vector.tensor_tensor(total[:, c0:c1], scattered[:, c0:c1], banks[half][:, c0:c1], ALU.add)
-                        store(kt, half, c0, c1)
+                    bank = banks[c0 // BANK][:, c0 % BANK : c0 % BANK + c1 - c0]
+                    nc.vector.tensor_tensor(total[:, c0:c1], windows[kt][:, c0:c1], bank, ALU.add)
+                store(kt, total, c0, c1)

@@ -54,19 +54,22 @@ def tile_moe_adb_relu_kernel(
             for r in range(4):
                 queue.dma_start(planes[r:P:32, :, :].bitcast(I32), by_r[r])
 
-        first_sizes = {"dy1": 4 * T, "wb0": 4 * H}
-        later_sizes = {"wb1": 4 * H, "wb2": 4 * H, "wb3": 4 * H, "wa0": 4 * K, "wa1": 4 * K, "wt": 4 * K, "a0": 8 * PACK * C, "a1": 8 * PACK * C,
-                       "wa_s": E * K, "wt_s": PASSES * K}
+        first_sizes = {"dy1": 4 * T, "wb0": 8 * H}
+        later_sizes = {"wa0": 4 * K, "a0": 8 * PACK * C, "wa_s": E * K}
+        last_sizes = {"wb1": 8 * H, "a1": 8 * PACK * C, "wa1": 4 * K, "wt": 4 * K, "wt_s": PASSES * K}
         place, end = {}, 0
-        for name, size in list(first_sizes.items()) + list(later_sizes.items()):
+        for name, size in list(first_sizes.items()) + list(later_sizes.items()) + list(last_sizes.items()):
             place[name] = end
             end = end + size
-        first_end = place["wb1"]
+        first_end = place["wa0"]
         zero_first = loads.tile([P, first_end // 4], F32, name="zero_first", offset=0, align_bytes=64)
-        zero_later = loads.tile([P, (end - first_end) // 4], F32, name="zero_later", offset=first_end, align_bytes=64)
+        later_end = place["wb1"]
+        zero_later = loads.tile([P, (later_end - first_end) // 4], F32, name="zero_later", offset=first_end, align_bytes=64)
+        zero_last = loads.tile([P, (end - later_end) // 4], F32, name="zero_last", offset=later_end, align_bytes=64)
         dy_s = zeroed_planes("dy_s", PASSES, T, nc.vector)
         nc.gpsimd.memset(zero_first[:, 0:8], 0.0)
         nc.gpsimd.memset(zero_later[:, 0:8], 0.0)
+        nc.gpsimd.memset(zero_last[:, 0:8], 0.0)
         g_rows = keep.tile([P, C], F32, name="g_rows", tag="gate_slot", align_bytes=64)
         nc.vector.tensor_copy(g_rows[:], zero_first[:, 0:1].to_broadcast([P, C]))
         wb_s = [zeroed_planes("wb_s0", 2 * PASSES, H, nc.vector), zeroed_planes("wb_s1", 2 * PASSES, H, nc.gpsimd)]
@@ -78,14 +81,15 @@ def tile_moe_adb_relu_kernel(
             return loads.tile(shape, dtype, name=name, offset=place[name], align_bytes=64)
 
         dy_w = [keep.tile([P, T], I32, name="dy0", align_bytes=64)[:], load_tile("dy1", [P, T], I32)[:]]
-        wb_w = [load_tile(f"wb{e}", [P, PASSES, FP4_BYTES * H], U8)[:] for e in range(E)]
+        wb_w = [load_tile(f"wb{pair}", [P, 2 * PASSES, FP4_BYTES * H], U8) for pair in range(E // 2)]
         wa_w = [load_tile(f"wa{pair}", [P, 2, FP4_BYTES * K], U8) for pair in range(E // 2)]
         wt_w = load_tile("wt", [P, PASSES, FP4_BYTES * K], U8)
         a_sb = [load_tile(f"a{pair}", [P, PACK, 2 * C], F32) for pair in range(E // 2)]
         g_col = keep.tile([P, 8], F32, name="g_col")
 
-        def load_wb(e):
-            nc.sync.dma_start(wb_w[e].bitcast(I32), wbt_words[e].bitcast(I32).rearrange("s p w -> p s w"))
+        def load_wb(pair):
+            words = wbt_words[2 * pair : 2 * pair + 2].bitcast(I32).rearrange("e s p w -> p (e s) w")
+            nc.sync.dma_start(wb_w[pair][:].bitcast(I32), words)
 
         def load_wb_scales(pair, queue):
             load_scales(wb_s[pair], wbt_scales[2 * pair : 2 * pair + 2].rearrange("e s b w -> (e s) b w"), queue)
@@ -108,20 +112,18 @@ def tile_moe_adb_relu_kernel(
         load_wb_scales(1, nc.gpsimd)
         nc.scalar.activation(windows[0][:, 0:8], zero_later[:, 0:8], COPY)
         wa_s = zeroed_planes("wa_s", E, K, nc.vector)
+        nc.scalar.activation(windows[0][:, 8:T], zero_last[:, 0:1].to_broadcast([P, T - 8]), COPY)
         wt_s = zeroed_planes("wt_s", PASSES, K, nc.vector)
-        nc.scalar.activation(windows[0][:, 8:T], windows[0][:, 0:1].to_broadcast([P, T - 8]), COPY)
         for kt in range(1, KT):
             nc.scalar.activation(windows[kt][:], windows[0][:, 0:1].to_broadcast([P, T]), COPY)
-        load_wb(1)
         load_a(0)
-        load_wb(2)
-        load_a(1)
         load_wa(0)
         load_scales(wa_s, wat_scales.rearrange("e s b w -> (e s) b w"), nc.sync)
-        load_wb(3)
+        load_wb(1)
+        load_a(1)
         load_wa(1)
-        load_scales(wt_s, wt_scales, nc.sync)
         nc.sync.dma_start(wt_w[:].bitcast(I32), wt_words.bitcast(I32).rearrange("s p w -> p s w"))
+        load_scales(wt_s, wt_scales, nc.sync)
 
         g_ps = psum.tile([P, P], F32, name="g_ps", tag="bank_a")
         nc.tensor.transpose(g_ps[:], g_rows[:], ident[:])
@@ -146,9 +148,9 @@ def tile_moe_adb_relu_kernel(
 
         def make_mask(e0, e1, slot):
             tile = keep.tile([P, (e1 - e0) * C, PACK], BF16, name=f"mask{e0}", tag=slot, align_bytes=64)
-            values = a_sb[e0 // 2][:, :, slots(e0 % 2, e0 % 2 + e1 - e0)].rearrange("p d u -> p u d")
-            nc.vector.tensor_scalar(out=tile[:], in0=values, scalar1=0.0, scalar2=None, op0=ALU.is_gt)
-            mask[e0] = tile
+            values = a_sb[e0 // 2][:, :, slots(e0 % 2, e0 % 2 + e1 - e0)].rearrange("p d (c i) -> p c d i", i=4)
+            nc.vector.tensor_scalar(out=tile[:].rearrange("p (c i) d -> p c d i", i=4), in0=values, scalar1=0.0, scalar2=None, op0=ALU.is_gt)
+            mask[e0 // 2] = tile
 
         def first_product(e, banks):
             h_sb[e] = keep.tile([P, 2, P, 2], BF16, name=f"h_sb{e}", tag=f"h_slot{e}", align_bytes=64)
@@ -163,7 +165,7 @@ def tile_moe_adb_relu_kernel(
                             out=h_ps[:, c0 : c0 + width],
                             lhsT=slot_w[:, s, slots(e, e + 1)].bitcast(FP8X4),
                             lhsT_scale=slot_s[e // 2, s][:, slots(e % 2, e % 2 + 1)],
-                            rhs=wb_w[e][:, s, FP4_BYTES * i0 : FP4_BYTES * (i0 + width)].bitcast(FP4X4),
+                            rhs=wb_w[e // 2][:, (e % 2) * PASSES + s, FP4_BYTES * i0 : FP4_BYTES * (i0 + width)].bitcast(FP4X4),
                             rhs_scale=wb_s[e // 2][:, (e % 2) * PASSES + s, i0 : i0 + width],
                             start=(s == 0),
                             stop=(s == PASSES - 1),
@@ -177,17 +179,17 @@ def tile_moe_adb_relu_kernel(
 
         def turn_and_mask(e0, e1, bank):
             count = e1 - e0
-            turned = psum.tile([P, 2, count * C], F32, name="turned", tag=bank)
+            turned = psum.tile([P, count * C, 2], F32, name="turned", tag=bank)
             for e in range(e0, e1):
                 pairs = h_sb[e][:].rearrange("u w m t -> u (w m t)").bitcast(F32)
                 for w in range(2):
-                    nc.tensor.transpose(turned[:, w, slots(e - e0, e - e0 + 1)], pairs[:, w * P : (w + 1) * P], ident[:])
+                    nc.tensor.transpose(turned[:, slots(e - e0, e - e0 + 1), w], pairs[:, w * P : (w + 1) * P], ident[:])
             dh[e0] = keep.tile([P, count * C, 2, 2], BF16, name=f"dh{e0}", tag=f"dh_slot{e0}", align_bytes=64)
-            values = turned[:].rearrange("p w u -> p (w u)").bitcast(BF16).rearrange("p (w u t) -> p u w t", w=2, t=2)
+            values = turned[:].rearrange("p u w -> p (u w)").bitcast(BF16).rearrange("p (u w t) -> p u w t", w=2, t=2)
             nc.vector.tensor_tensor(
                 dh[e0][:],
                 values,
-                mask[e0][:].rearrange("p u (w t) -> p u w t", w=2),
+                mask[e0 // 2][:, slots(e0 % 2, e0 % 2 + count), :].rearrange("p u (w t) -> p u w t", w=2),
                 ALU.mult,
             )
 
@@ -229,7 +231,7 @@ def tile_moe_adb_relu_kernel(
             return slice(half * BANK, (half + 1) * BANK)
 
         def base_product(kt, half):
-            base_ps = psum.tile([P, BANK], F32, name="base_ps", tag="bank_c" if (kt, half) == (0, 0) else ["bank_a", "bank_f", "bank_g"][(HALVES * kt + half) % 3])
+            base_ps = psum.tile([P, BANK], F32, name="base_ps", tag=["bank_f", "bank_g"][half])
             for s in range(PASSES):
                 nc.tensor.matmul_mx(
                     out=base_ps[:],
@@ -257,38 +259,36 @@ def tile_moe_adb_relu_kernel(
         for s in range(PASSES):
             slot_s[1, s] = second_scales[:, s, :]
             gather_scales(s, 2, E)
-        make_mask(0, 1, "mask_slot0")
+        make_mask(0, 2, "mask_slot0")
         turn_and_mask(0, 1, "bank_d")
-        make_mask(1, 2, "h_slot0")
         quantize(0, 1)
         turn_and_mask(1, 2, "bank_a")
-        make_mask(2, E, "h_slot1")
         dx_tiles(0, 0, 1, "bank_e")
-        dx_tiles(0, 1, KT - 1, "bank_c")
-        kept = psum.tile([P, 2, C], F32, name="kept", tag="bank_d")
-        second_product(0, KT - 1, kept[:, 0, :])
-        first_product(2, ["bank_b"])
+        dx_tiles(0, 1, 3, "bank_h")
+        first_product(2, ["bank_e"])
         quantize(1, 2)
-        first_product(3, ["bank_e"])
-        second_product(1, 0, kept[:, 1, :])
-        dx_tiles(1, 1, KT, "bank_h")
-        for kt in range(KT - 1):
+        first_product(3, ["bank_h"])
+        kept = psum.tile([P, 2, C], F32, name="kept", tag="bank_d")
+        dx_tiles(1, 0, 1, "bank_g")
+        second_product(1, 1, kept[:, 0, :])
+        second_product(1, 2, kept[:, 1, :])
+        for kt in range(3):
             scatter(kt, 0, 1)
-        scatter(1, 1, 2)
-        turn_and_mask(2, E, "bank_e")
+        scatter(0, 1, 2)
+        make_mask(2, E, "mask_slot1")
+        turn_and_mask(2, E, "bank_a")
         quantize(2, E)
-        after_mask = keep.tile([P, 2, C], F32, name="after_mask", tag="h_slot1", align_bytes=64)
+        after_mask = keep.tile([P, 2, C], F32, name="after_mask", tag="mask_slot1", align_bytes=64)
         nc.scalar.copy(after_mask[:], kept[:])
-        scatter_from(after_mask[:, 1, :], 0, 1)
-        scatter_from(after_mask[:, 0, :], KT - 1, 0)
-        first_tile = psum.tile([P, 2, C], F32, name="first_tile", tag="bank_f")
-        for e in range(2, E):
-            second_product(e, 0, first_tile[:, e - 2, :])
-        nc.scalar.copy(dx[:, 0, slots(2, E)], first_tile[:].rearrange("p e u -> p (e u)"))
-        dx_tiles(2, 1, KT, "bank_g")
-        dx_tiles(3, 1, KT, "bank_a")
+        scatter_from(after_mask[:, 0, :], 1, 1)
+        scatter_from(after_mask[:, 1, :], 2, 1)
+        early = [2, 2, 2, 0]
+        for kt, bank in enumerate(["bank_b", "bank_c", "bank_e", "bank_a"]):
+            dx_ps = psum.tile([P, E - early[kt], C], F32, name="dx_ps", tag=bank)
+            for e in range(early[kt], E):
+                second_product(e, kt, dx_ps[:, e - early[kt], :])
+            nc.scalar.copy(dx[:, kt, slots(early[kt], E)], dx_ps[:].rearrange("p e u -> p (e u)"))
 
-        early = [2, 2, 1, 1]
         for kt in range(KT):
             on_gpsimd = kt < KT - 1
             total = keep.tile([P, T], F32, name=f"total{kt}", align_bytes=64)

@@ -244,6 +244,19 @@ def tile_moe_adb_relu_kernel(
                 )
             return base_ps
 
+        def warm_up(passes, bank):
+            warm = psum.tile([P, BANK], F32, name="warm", tag=bank)
+            for n in range(passes):
+                nc.tensor.matmul_mx(
+                    out=warm[:],
+                    lhsT=dy_w[1][:, 0:P].bitcast(FP8X4),
+                    lhsT_scale=dy_s[:, 1, 0:P],
+                    rhs=dy_w[1][:, 0 : BANK // 2].bitcast(U8).bitcast(FP4X4),
+                    rhs_scale=dy_s[:, 1, 0:BANK],
+                    start=True,
+                    stop=True,
+                )
+
         def store(kt, total, c0, c1):
             queue = nc.scalar if kt == KT - 1 and c0 % BANK == 0 else nc.sync
             queue.dma_start(out[kt * P : (kt + 1) * P, c0:c1], total[:, c0:c1])
@@ -252,6 +265,7 @@ def tile_moe_adb_relu_kernel(
         for s in range(PASSES):
             gather_scales(s, 0, 2)
         gather_words(1, 0, 2)
+        warm_up(3, "bank_g")
         first_product(0, ["bank_f", "bank_b"])
         first_product(1, ["bank_c"])
         gather_words(1, 2, E)
@@ -261,6 +275,7 @@ def tile_moe_adb_relu_kernel(
             gather_scales(s, 2, E)
         make_mask(0, 2, "mask_slot0")
         turn_and_mask(0, 1, "bank_d")
+        warm_up(2, "bank_b")
         quantize(0, 1)
         turn_and_mask(1, 2, "bank_a")
         dx_tiles(0, 0, 1, "bank_e")

@@ -26,6 +26,7 @@ BANK = 512
 HALVES = T // BANK
 BANKS = 8
 LIST_ROWS = 16
+BASE_BANKS = [["bank_h", "bank_h"], ["bank_a", "bank_h"], ["bank_a", "bank_h"], ["bank_a", "bank_h"]]
 FP4_BYTES = 2
 
 
@@ -121,9 +122,9 @@ def tile_moe_adb_relu_kernel(
         load_scales(wa_s, wat_scales.rearrange("e s b w -> (e s) b w"), nc.sync)
         load_wb(1)
         load_a(1)
-        load_wa(1)
         nc.sync.dma_start(wt_w[:].bitcast(I32), wt_words.bitcast(I32).rearrange("s p w -> p s w"))
         load_scales(wt_s, wt_scales, nc.sync)
+        load_wa(1)
 
         g_ps = psum.tile([P, P], F32, name="g_ps", tag="bank_a")
         nc.tensor.transpose(g_ps[:], g_rows[:], ident[:])
@@ -193,12 +194,13 @@ def tile_moe_adb_relu_kernel(
                 ALU.mult,
             )
 
-        def quantize(e0, e1):
+        def quantize(e0, e1, source=None):
             count = e1 - e0
+            values = dh[e0][:] if source is None else dh[source][:, slots(e0 - source, e1 - source), :, :]
             words = keep.tile([P, count * C], U32, name=f"dh_w{e0}", tag=f"words_slot{e0}", align_bytes=64)
             scales = keep.tile([P, count * C], U8, name=f"dh_s{e0}", tag=f"scales_slot{e0}", align_bytes=64)
             nc.vector.quantize_mx(
-                out=words[:].bitcast(FP8X4), scales=scales[:], in_=dh[e0][:].rearrange("p u w t -> p (u w t)")
+                out=words[:].bitcast(FP8X4), scales=scales[:], in_=values.rearrange("p u w t -> p (u w t)")
             )
             for e in range(e0, e1):
                 dh_w[e] = words[:, slots(e - e0, e - e0 + 1)]
@@ -231,7 +233,7 @@ def tile_moe_adb_relu_kernel(
             return slice(half * BANK, (half + 1) * BANK)
 
         def base_product(kt, half):
-            base_ps = psum.tile([P, BANK], F32, name="base_ps", tag=["bank_f", "bank_g"][half])
+            base_ps = psum.tile([P, BANK], F32, name="base_ps", tag=BASE_BANKS[kt][half])
             for s in range(PASSES):
                 nc.tensor.matmul_mx(
                     out=base_ps[:],
@@ -258,7 +260,7 @@ def tile_moe_adb_relu_kernel(
                 )
 
         def store(kt, total, c0, c1):
-            queue = nc.scalar if kt == KT - 1 and c0 % BANK == 0 else nc.sync
+            queue = nc.scalar if kt == KT - 1 and c1 == T else nc.sync
             queue.dma_start(out[kt * P : (kt + 1) * P, c0:c1], total[:, c0:c1])
 
         gather_words(0, 0, E)
@@ -283,39 +285,47 @@ def tile_moe_adb_relu_kernel(
         first_product(2, ["bank_e"])
         quantize(1, 2)
         first_product(3, ["bank_h"])
-        kept = psum.tile([P, 2, C], F32, name="kept", tag="bank_d")
+        kept = psum.tile([P, C], F32, name="kept", tag="bank_d")
         dx_tiles(1, 0, 1, "bank_g")
-        second_product(1, 1, kept[:, 0, :])
-        second_product(1, 2, kept[:, 1, :])
+        second_product(1, 1, kept[:])
         for kt in range(3):
             scatter(kt, 0, 1)
         scatter(0, 1, 2)
         make_mask(2, E, "mask_slot1")
         turn_and_mask(2, E, "bank_a")
-        quantize(2, E)
-        after_mask = keep.tile([P, 2, C], F32, name="after_mask", tag="mask_slot1", align_bytes=64)
+        quantize(2, 3, 2)
+        quantize(3, E, 2)
+        after_mask = keep.tile([P, C], F32, name="after_mask", tag="mask_slot1", align_bytes=64)
         nc.scalar.copy(after_mask[:], kept[:])
-        scatter_from(after_mask[:, 0, :], 1, 1)
-        scatter_from(after_mask[:, 1, :], 2, 1)
-        early = [2, 2, 2, 0]
-        for kt, bank in enumerate(["bank_b", "bank_c", "bank_e", "bank_a"]):
+        scatter_from(after_mask[:], 1, 1)
+        dx_tiles(2, 0, 1, "bank_b")
+        scatter(0, 2, 3)
+        early = [3, 2, 1, 0]
+
+        def late_dx(kt, bank):
             dx_ps = psum.tile([P, E - early[kt], C], F32, name="dx_ps", tag=bank)
             for e in range(early[kt], E):
                 second_product(e, kt, dx_ps[:, e - early[kt], :])
             nc.scalar.copy(dx[:, kt, slots(early[kt], E)], dx_ps[:].rearrange("p e u -> p (e u)"))
 
+        for kt, bank in enumerate(["bank_c", "bank_e", "bank_f", "bank_g"]):
+            late_dx(kt, bank)
+
+        share = 256
         for kt in range(KT):
-            on_gpsimd = kt < KT - 1
+            last = kt == KT - 1
             total = keep.tile([P, T], F32, name=f"total{kt}", align_bytes=64)
             banks = []
             for half in range(HALVES):
                 banks.append(base_product(kt, half))
-                if on_gpsimd:
+                if not last:
                     nc.scalar.copy(total[:, tokens(half)], banks[half][:])
+            if last:
+                nc.scalar.copy(total[:, T - share : T], banks[1][:, BANK - share : BANK])
             scatter(kt, early[kt], E)
-            cuts = [[0, BANK, T], [0, T], [0, BANK, T], [0, BANK, BANK + BANK // 2, T]][kt]
+            cuts = [[0, T], [0, T], [0, BANK, T], [0, BANK // 2, BANK, T - share, T]][kt]
             for c0, c1 in zip(cuts, cuts[1:]):
-                if on_gpsimd:
+                if not last or c1 == T:
                     nc.gpsimd.tensor_tensor(total[:, c0:c1], total[:, c0:c1], windows[kt][:, c0:c1], ALU.add)
                 else:
                     bank = banks[c0 // BANK][:, c0 % BANK : c0 % BANK + c1 - c0]

@@ -24,10 +24,9 @@ PASSES = N // (P * PACK)
 KT = K // P
 BANK = 512
 HALVES = T // BANK
-BANKS = 8
 LIST_ROWS = 16
-BASE_BANKS = [["bank_h", "bank_h"], ["bank_a", "bank_h"], ["bank_a", "bank_h"], ["bank_a", "bank_h"]]
 FP4_BYTES = 2
+ZEROS = 8
 
 
 def tile_moe_adb_relu_kernel(
@@ -42,11 +41,26 @@ def tile_moe_adb_relu_kernel(
         offsets = keep.tile([P, S // LIST_ROWS], U16, name="offsets")
         nc.sync.dma_start(offsets[:], offs)
 
-        def zeroed_planes(name, count, width, engine):
+        groups = [
+            {"dy1": 4 * T, "wb": 16 * H},
+            {"a0": 8 * PACK * C, "wa": 8 * K, "a1": 8 * PACK * C},
+            {"wt": 4 * K, "wt_s": PASSES * K},
+        ]
+        place, zeros, end = {}, [], 0
+        for number, group in enumerate(groups):
+            start = end
+            for name, size in group.items():
+                place[name] = end
+                end = end + size
+            zeros.append(loads.tile([P, (end - start) // 4], F32, name=f"zeros{number}", offset=start, align_bytes=64))
+
+        def load_tile(name, shape, dtype):
             if name in place:
-                planes = loads.tile([P, count, width], U8, name=name, offset=place[name], align_bytes=64)
-            else:
-                planes = keep.tile([P, count, width], U8, name=name, align_bytes=64)
+                return loads.tile(shape, dtype, name=name, offset=place[name], align_bytes=64)
+            return keep.tile(shape, dtype, name=name, align_bytes=64)
+
+        def zeroed_planes(name, count, width, engine):
+            planes = load_tile(name, [P, count, width], U8)
             engine.memset(planes[:].rearrange("p c w -> p (c w)").bitcast(I32), 0)
             return planes
 
@@ -55,85 +69,59 @@ def tile_moe_adb_relu_kernel(
             for r in range(4):
                 queue.dma_start(planes[r:P:32, :, :].bitcast(I32), by_r[r])
 
-        first_sizes = {"dy1": 4 * T, "wb0": 8 * H}
-        later_sizes = {"wa0": 4 * K, "a0": 8 * PACK * C, "wa_s": E * K}
-        last_sizes = {"wb1": 8 * H, "a1": 8 * PACK * C, "wa1": 4 * K, "wt": 4 * K, "wt_s": PASSES * K}
-        place, end = {}, 0
-        for name, size in list(first_sizes.items()) + list(later_sizes.items()) + list(last_sizes.items()):
-            place[name] = end
-            end = end + size
-        first_end = place["wa0"]
-        zero_first = loads.tile([P, first_end // 4], F32, name="zero_first", offset=0, align_bytes=64)
-        later_end = place["wb1"]
-        zero_later = loads.tile([P, (later_end - first_end) // 4], F32, name="zero_later", offset=first_end, align_bytes=64)
-        zero_last = loads.tile([P, (end - later_end) // 4], F32, name="zero_last", offset=later_end, align_bytes=64)
         dy_s = zeroed_planes("dy_s", PASSES, T, nc.vector)
-        nc.gpsimd.memset(zero_first[:, 0:8], 0.0)
-        nc.gpsimd.memset(zero_later[:, 0:8], 0.0)
-        nc.gpsimd.memset(zero_last[:, 0:8], 0.0)
-        g_rows = keep.tile([P, C], F32, name="g_rows", tag="gate_slot", align_bytes=64)
-        nc.vector.tensor_copy(g_rows[:], zero_first[:, 0:1].to_broadcast([P, C]))
-        wb_s = [zeroed_planes("wb_s0", 2 * PASSES, H, nc.vector), zeroed_planes("wb_s1", 2 * PASSES, H, nc.gpsimd)]
+        for tile in zeros:
+            nc.gpsimd.memset(tile[:, 0:ZEROS], 0.0)
+        g_rows = keep.tile([P, C], F32, name="g_rows", align_bytes=64)
+        nc.vector.tensor_copy(g_rows[:], zeros[0][:, 0:1].to_broadcast([P, C]))
+        wb_s = zeroed_planes("wb_s", E * PASSES, H, nc.vector)
+        wa_s = zeroed_planes("wa_s", E, K, nc.gpsimd)
         ident = keep.tile([P, P], F32, name="ident")
         make_identity(nc, ident[:])
         windows = {kt: keep.tile([P, T], F32, name=f"window{kt}") for kt in range(KT)}
 
-        def load_tile(name, shape, dtype):
-            return loads.tile(shape, dtype, name=name, offset=place[name], align_bytes=64)
-
-        dy_w = [keep.tile([P, T], I32, name="dy0", align_bytes=64)[:], load_tile("dy1", [P, T], I32)[:]]
-        wb_w = [load_tile(f"wb{pair}", [P, 2 * PASSES, FP4_BYTES * H], U8) for pair in range(E // 2)]
-        wa_w = [load_tile(f"wa{pair}", [P, 2, FP4_BYTES * K], U8) for pair in range(E // 2)]
+        dy_w = [load_tile(f"dy{s}", [P, T], I32)[:] for s in range(PASSES)]
+        wb_w = load_tile("wb", [P, E * PASSES, FP4_BYTES * H], U8)
+        wa_w = load_tile("wa", [P, E, FP4_BYTES * K], U8)
         wt_w = load_tile("wt", [P, PASSES, FP4_BYTES * K], U8)
         a_sb = [load_tile(f"a{pair}", [P, PACK, 2 * C], F32) for pair in range(E // 2)]
-        g_col = keep.tile([P, 8], F32, name="g_col")
-
-        def load_wb(pair):
-            words = wbt_words[2 * pair : 2 * pair + 2].bitcast(I32).rearrange("e s p w -> p (e s) w")
-            nc.sync.dma_start(wb_w[pair][:].bitcast(I32), words)
-
-        def load_wb_scales(pair, queue):
-            load_scales(wb_s[pair], wbt_scales[2 * pair : 2 * pair + 2].rearrange("e s b w -> (e s) b w"), queue)
-
+        g_col = keep.tile([P, ZEROS], F32, name="g_col", tag="gate_slot", align_bytes=64)
         a_rows = a.rearrange("(p d) j -> p d j", d=PACK)
+
+        def load_dy(s):
+            nc.sync.dma_start(dy_w[s], dy_words[s].rearrange("p t d -> p (t d)").bitcast(I32))
+
+        def load_words(tile, words):
+            nc.sync.dma_start(tile[:].bitcast(I32), words.bitcast(I32).rearrange("e s p w -> p (e s) w"))
 
         def load_a(pair):
             nc.sync.dma_start(a_sb[pair][:], a_rows[:, :, 2 * pair * C : 2 * (pair + 1) * C])
 
-        def load_wa(pair):
-            words = wat_words[2 * pair : 2 * (pair + 1)].bitcast(I32).rearrange("e s p w -> p (e s) w")
-            nc.sync.dma_start(wa_w[pair][:].bitcast(I32), words)
-
-        nc.sync.dma_start(dy_w[0], dy_words[0].rearrange("p t d -> p (t d)").bitcast(I32))
+        load_dy(0)
         load_scales(dy_s, dy_scales, nc.sync)
-        nc.sync.dma_start(dy_w[1], dy_words[1].rearrange("p t d -> p (t d)").bitcast(I32))
-        load_wb(0)
+        load_dy(1)
+        load_words(wb_w, wbt_words)
         nc.sync.dma_start(g_rows[0:E, :], gate[0:1, :].rearrange("o (e u) -> (o e) u", e=E))
-        load_wb_scales(0, nc.sync)
-        load_wb_scales(1, nc.gpsimd)
-        nc.scalar.activation(windows[0][:, 0:8], zero_later[:, 0:8], COPY)
-        wa_s = zeroed_planes("wa_s", E, K, nc.vector)
-        nc.scalar.activation(windows[0][:, 8:T], zero_last[:, 0:1].to_broadcast([P, T - 8]), COPY)
+        load_scales(wb_s, wbt_scales.rearrange("e s b w -> (e s) b w"), nc.sync)
+        load_scales(wa_s, wat_scales.rearrange("e s b w -> (e s) b w"), nc.gpsimd)
+        nc.scalar.activation(windows[0][:, 0:ZEROS], zeros[1][:, 0:ZEROS], COPY)
+        nc.scalar.activation(windows[0][:, ZEROS:T], zeros[2][:, 0:1].to_broadcast([P, T - ZEROS]), COPY)
         wt_s = zeroed_planes("wt_s", PASSES, K, nc.vector)
         for kt in range(1, KT):
             nc.scalar.activation(windows[kt][:], windows[0][:, 0:1].to_broadcast([P, T]), COPY)
         load_a(0)
-        load_wa(0)
-        load_scales(wa_s, wat_scales.rearrange("e s b w -> (e s) b w"), nc.sync)
-        load_wb(1)
+        load_words(wa_w, wat_words)
         load_a(1)
         nc.sync.dma_start(wt_w[:].bitcast(I32), wt_words.bitcast(I32).rearrange("s p w -> p s w"))
         load_scales(wt_s, wt_scales, nc.sync)
-        load_wa(1)
 
-        g_ps = psum.tile([P, P], F32, name="g_ps", tag="bank_a")
+        g_ps = psum.tile([P, P], F32, name="g_ps", tag="bank_e")
         nc.tensor.transpose(g_ps[:], g_rows[:], ident[:])
         nc.scalar.copy(g_col[:, 0:E], g_ps[:, 0:E])
 
-        slot_s = {(0, s): keep.tile([P, 2 * C], U8, name=f"slot_s0{s}", align_bytes=64)[:] for s in range(PASSES)}
         slot_w = keep.tile([P, PASSES, S], U32, name="slot_w", align_bytes=64)
-        dx = keep.tile([P, KT, S], F32, name="dx")
-        mask, h_sb, dh, dh_w, dh_s, result = {}, {}, {}, {}, {}, {}
+        slot_s = keep.tile([P, PASSES, S], U8, name="slot_s", align_bytes=64)
+        mask, h_sb, turned, dh, dh_w, dh_s, total, base_ps = {}, {}, {}, {}, {}, {}, {}, {}
 
         def slots(e0, e1):
             return slice(e0 * C, e1 * C)
@@ -141,42 +129,41 @@ def tile_moe_adb_relu_kernel(
         def slot_offsets(e0, e1):
             return offsets[:, e0 * C // LIST_ROWS : e1 * C // LIST_ROWS]
 
+        def tokens(half):
+            return slice(half * BANK, (half + 1) * BANK)
+
         def gather_words(s, e0, e1):
             nc.vector.tensor_copy(slot_w[:, s, slots(e0, e1)], dy_w[s].bitcast(U32).indirect(slot_offsets(e0, e1)))
 
         def gather_scales(s, e0, e1):
-            nc.vector.tensor_copy(slot_s[e0 // 2, s], dy_s[:, s, :].indirect(slot_offsets(e0, e1)))
+            nc.vector.tensor_copy(slot_s[:, s, slots(e0, e1)], dy_s[:, s, :].indirect(slot_offsets(e0, e1)))
 
-        def make_mask(e0, e1, slot):
-            tile = keep.tile([P, (e1 - e0) * C, PACK], BF16, name=f"mask{e0}", tag=slot, align_bytes=64)
-            values = a_sb[e0 // 2][:, :, slots(e0 % 2, e0 % 2 + e1 - e0)].rearrange("p d (c i) -> p c d i", i=4)
-            nc.vector.tensor_scalar(out=tile[:].rearrange("p (c i) d -> p c d i", i=4), in0=values, scalar1=0.0, scalar2=None, op0=ALU.is_gt)
-            mask[e0 // 2] = tile
+        def make_mask(pair):
+            mask[pair] = keep.tile([P, 2 * C, PACK], BF16, name=f"mask{pair}", align_bytes=64)
+            nc.vector.tensor_scalar(
+                out=mask[pair][:].rearrange("p (c i) d -> p c d i", i=4),
+                in0=a_sb[pair][:].rearrange("p d (c i) -> p c d i", i=4),
+                scalar1=0.0,
+                scalar2=None,
+                op0=ALU.is_gt,
+            )
 
-        def first_product(e, banks):
-            h_sb[e] = keep.tile([P, 2, P, 2], BF16, name=f"h_sb{e}", tag=f"h_slot{e}", align_bytes=64)
-            part = H // len(banks)
-            width = H if len(banks) == 1 else C
-            for n, bank in enumerate(banks):
-                h_ps = psum.tile([P, part], F32, name="h_ps", tag=bank)
-                for c0 in range(0, part, width):
-                    i0 = n * part + c0
-                    for s in range(PASSES):
-                        nc.tensor.matmul_mx(
-                            out=h_ps[:, c0 : c0 + width],
-                            lhsT=slot_w[:, s, slots(e, e + 1)].bitcast(FP8X4),
-                            lhsT_scale=slot_s[e // 2, s][:, slots(e % 2, e % 2 + 1)],
-                            rhs=wb_w[e // 2][:, (e % 2) * PASSES + s, FP4_BYTES * i0 : FP4_BYTES * (i0 + width)].bitcast(FP4X4),
-                            rhs_scale=wb_s[e // 2][:, (e % 2) * PASSES + s, i0 : i0 + width],
-                            start=(s == 0),
-                            stop=(s == PASSES - 1),
-                        )
-                nc.scalar.activation(
-                    h_sb[e][:, :, n * part // PACK : (n + 1) * part // PACK, :],
-                    h_ps[:].rearrange("u (m w t) -> u w m t", w=2, t=2),
-                    COPY,
-                    scale=g_col[:, e : e + 1],
+        def first_product(e, bank):
+            h_ps = psum.tile([P, H], F32, name="h_ps", tag=bank)
+            for s in range(PASSES):
+                nc.tensor.matmul_mx(
+                    out=h_ps[:],
+                    lhsT=slot_w[:, s, slots(e, e + 1)].bitcast(FP8X4),
+                    lhsT_scale=slot_s[:, s, slots(e, e + 1)],
+                    rhs=wb_w[:, e * PASSES + s, :].bitcast(FP4X4),
+                    rhs_scale=wb_s[:, e * PASSES + s, :],
+                    start=(s == 0),
+                    stop=(s == PASSES - 1),
                 )
+            h_sb[e] = keep.tile([P, 2, P, 2], BF16, name=f"h_sb{e}", align_bytes=64)
+            nc.scalar.activation(
+                h_sb[e][:], h_ps[:].rearrange("u (m w t) -> u w m t", w=2, t=2), COPY, scale=g_col[:, e : e + 1]
+            )
 
         def turn_and_mask(e0, e1, bank):
             count = e1 - e0
@@ -185,58 +172,50 @@ def tile_moe_adb_relu_kernel(
                 pairs = h_sb[e][:].rearrange("u w m t -> u (w m t)").bitcast(F32)
                 for w in range(2):
                     nc.tensor.transpose(turned[:, slots(e - e0, e - e0 + 1), w], pairs[:, w * P : (w + 1) * P], ident[:])
-            dh[e0] = keep.tile([P, count * C, 2, 2], BF16, name=f"dh{e0}", tag=f"dh_slot{e0}", align_bytes=64)
-            values = turned[:].rearrange("p u w -> p (u w)").bitcast(BF16).rearrange("p (u w t) -> p u w t", w=2, t=2)
+            dh[e0] = keep.tile([P, count * C * PACK], BF16, name=f"dh{e0}", tag=f"dh_slot{e0}", align_bytes=64)
             nc.vector.tensor_tensor(
                 dh[e0][:],
-                values,
-                mask[e0 // 2][:, slots(e0 % 2, e0 % 2 + count), :].rearrange("p u (w t) -> p u w t", w=2),
+                turned[:].rearrange("p u w -> p (u w)").bitcast(BF16),
+                mask[e0 // 2][:, slots(e0 % 2, e0 % 2 + count), :].rearrange("p u d -> p (u d)"),
                 ALU.mult,
             )
 
-        def quantize(e0, e1, source=None):
+        def quantize(e0, e1):
             count = e1 - e0
-            values = dh[e0][:] if source is None else dh[source][:, slots(e0 - source, e1 - source), :, :]
-            words = keep.tile([P, count * C], U32, name=f"dh_w{e0}", tag=f"words_slot{e0}", align_bytes=64)
-            scales = keep.tile([P, count * C], U8, name=f"dh_s{e0}", tag=f"scales_slot{e0}", align_bytes=64)
-            nc.vector.quantize_mx(
-                out=words[:].bitcast(FP8X4), scales=scales[:], in_=values.rearrange("p u w t -> p (u w t)")
-            )
+            words = keep.tile([P, count * C], U32, name=f"dh_w{e0}", align_bytes=64)
+            scales = keep.tile([P, count * C], U8, name=f"dh_s{e0}", align_bytes=64)
+            nc.vector.quantize_mx(out=words[:].bitcast(FP8X4), scales=scales[:], in_=dh[e0][:])
             for e in range(e0, e1):
                 dh_w[e] = words[:, slots(e - e0, e - e0 + 1)]
                 dh_s[e] = scales[:, slots(e - e0, e - e0 + 1)]
 
-        def second_product(e, kt, target):
-            nc.tensor.matmul_mx(
-                out=target,
-                lhsT=wa_w[e // 2][:, e % 2, FP4_BYTES * kt * P : FP4_BYTES * (kt + 1) * P].bitcast(FP4X4),
-                lhsT_scale=wa_s[:, e, kt * P : (kt + 1) * P],
-                rhs=dh_w[e].bitcast(FP8X4),
-                rhs_scale=dh_s[e],
-                start=True,
-                stop=True,
-            )
+        def dx_piece(kt, e0, e1, bank, copier, slot):
+            dx_ps = psum.tile([P, (e1 - e0) * C], F32, name="dx_ps", tag=bank)
+            for e in range(e0, e1):
+                nc.tensor.matmul_mx(
+                    out=dx_ps[:, slots(e - e0, e - e0 + 1)],
+                    lhsT=wa_w[:, e, FP4_BYTES * kt * P : FP4_BYTES * (kt + 1) * P].bitcast(FP4X4),
+                    lhsT_scale=wa_s[:, e, kt * P : (kt + 1) * P],
+                    rhs=dh_w[e].bitcast(FP8X4),
+                    rhs_scale=dh_s[e],
+                    start=True,
+                    stop=True,
+                )
+            piece = keep.tile([P, (e1 - e0) * C], F32, name=f"dx{kt}{e0}", tag=slot, align_bytes=64)
+            copier(piece[:], dx_ps[:])
+            return piece
 
-        def dx_tiles(e, kt0, kt1, bank):
-            dx_ps = psum.tile([P, kt1 - kt0, C], F32, name="dx_ps", tag=bank)
-            for kt in range(kt0, kt1):
-                second_product(e, kt, dx_ps[:, kt - kt0, :])
-            nc.scalar.copy(dx[:, kt0:kt1, slots(e, e + 1)], dx_ps[:])
+        def scatter_vector(kt, e0, e1, source):
+            nc.vector.tensor_copy(windows[kt][:].indirect(slot_offsets(e0, e1)), source)
 
-        def scatter_from(source, kt, e):
-            nc.vector.tensor_copy(windows[kt][:].indirect(slot_offsets(e, e + 1)), source)
+        def scatter_scalar(kt, e0, e1, source):
+            nc.scalar.activation(windows[kt][:].indirect(slot_offsets(e0, e1)), source, COPY)
 
-        def scatter(kt, e0, e1):
-            nc.vector.tensor_copy(windows[kt][:].indirect(slot_offsets(e0, e1)), dx[:, kt, slots(e0, e1)])
-
-        def tokens(half):
-            return slice(half * BANK, (half + 1) * BANK)
-
-        def base_product(kt, half):
-            base_ps = psum.tile([P, BANK], F32, name="base_ps", tag=BASE_BANKS[kt][half])
+        def base_product(kt, half, bank):
+            base_ps[kt, half] = psum.tile([P, BANK], F32, name="base_ps", tag=bank)
             for s in range(PASSES):
                 nc.tensor.matmul_mx(
-                    out=base_ps[:],
+                    out=base_ps[kt, half][:],
                     lhsT=wt_w[:, s, FP4_BYTES * kt * P : FP4_BYTES * (kt + 1) * P].bitcast(FP4X4),
                     lhsT_scale=wt_s[:, s, kt * P : (kt + 1) * P],
                     rhs=dy_w[s][:, tokens(half)].bitcast(FP8X4),
@@ -244,90 +223,64 @@ def tile_moe_adb_relu_kernel(
                     start=(s == 0),
                     stop=(s == PASSES - 1),
                 )
-            return base_ps
 
-        def warm_up(passes, bank):
-            warm = psum.tile([P, BANK], F32, name="warm", tag=bank)
-            for n in range(passes):
-                nc.tensor.matmul_mx(
-                    out=warm[:],
-                    lhsT=dy_w[1][:, 0:P].bitcast(FP8X4),
-                    lhsT_scale=dy_s[:, 1, 0:P],
-                    rhs=dy_w[1][:, 0 : BANK // 2].bitcast(U8).bitcast(FP4X4),
-                    rhs_scale=dy_s[:, 1, 0:BANK],
-                    start=True,
-                    stop=True,
-                )
+        def base_copy(kt, half):
+            nc.scalar.copy(total[kt][:, tokens(half)], base_ps[kt, half][:])
 
-        def store(kt, total, c0, c1):
-            queue = nc.scalar if kt == KT - 1 and c1 == T else nc.sync
-            queue.dma_start(out[kt * P : (kt + 1) * P, c0:c1], total[:, c0:c1])
+        def add_and_store(kt, c0, c1, from_psum, queue):
+            if from_psum:
+                bank = base_ps[kt, c0 // BANK][:, c0 % BANK : c0 % BANK + c1 - c0]
+                nc.vector.tensor_tensor(total[kt][:, c0:c1], windows[kt][:, c0:c1], bank, ALU.add)
+            else:
+                nc.gpsimd.tensor_tensor(total[kt][:, c0:c1], total[kt][:, c0:c1], windows[kt][:, c0:c1], ALU.add)
+            queue.dma_start(out[kt * P : (kt + 1) * P, c0:c1], total[kt][:, c0:c1])
+
+        for kt in range(KT):
+            total[kt] = keep.tile([P, T], F32, name=f"total{kt}", align_bytes=64)
 
         gather_words(0, 0, E)
         for s in range(PASSES):
             gather_scales(s, 0, 2)
         gather_words(1, 0, 2)
-        warm_up(3, "bank_g")
-        first_product(0, ["bank_f", "bank_b"])
-        first_product(1, ["bank_c"])
+        first_product(0, "bank_a")
+        first_product(1, "bank_b")
         gather_words(1, 2, E)
-        second_scales = keep.tile([P, PASSES, 2 * C], U8, name="second_scales", tag="gate_slot", align_bytes=64)
         for s in range(PASSES):
-            slot_s[1, s] = second_scales[:, s, :]
             gather_scales(s, 2, E)
-        make_mask(0, 2, "mask_slot0")
-        turn_and_mask(0, 1, "bank_d")
-        warm_up(2, "bank_b")
+        make_mask(0)
+        turn_and_mask(0, 1, "bank_e")
         quantize(0, 1)
-        turn_and_mask(1, 2, "bank_a")
-        dx_tiles(0, 0, 1, "bank_e")
-        dx_tiles(0, 1, 3, "bank_h")
-        first_product(2, ["bank_e"])
+        first_product(2, "bank_c")
+        turn_and_mask(1, 2, "bank_f")
         quantize(1, 2)
-        first_product(3, ["bank_h"])
-        kept = psum.tile([P, C], F32, name="kept", tag="bank_d")
-        dx_tiles(1, 0, 1, "bank_g")
-        second_product(1, 1, kept[:])
-        for kt in range(3):
-            scatter(kt, 0, 1)
-        scatter(0, 1, 2)
-        make_mask(2, E, "mask_slot1")
-        turn_and_mask(2, E, "bank_a")
-        quantize(2, 3, 2)
-        quantize(3, E, 2)
-        after_mask = keep.tile([P, C], F32, name="after_mask", tag="mask_slot1", align_bytes=64)
-        nc.scalar.copy(after_mask[:], kept[:])
-        scatter_from(after_mask[:], 1, 1)
-        dx_tiles(2, 0, 1, "bank_b")
-        scatter(0, 2, 3)
-        early = [3, 2, 1, 0]
+        first_product(3, "bank_d")
+        make_mask(1)
+        turn_and_mask(2, E, "bank_g")
+        quantize(2, E)
 
-        def late_dx(kt, bank):
-            dx_ps = psum.tile([P, E - early[kt], C], F32, name="dx_ps", tag=bank)
-            for e in range(early[kt], E):
-                second_product(e, kt, dx_ps[:, e - early[kt], :])
-            nc.scalar.copy(dx[:, kt, slots(early[kt], E)], dx_ps[:].rearrange("p e u -> p (e u)"))
-
-        for kt, bank in enumerate(["bank_c", "bank_e", "bank_f", "bank_g"]):
-            late_dx(kt, bank)
-
-        share = 256
-        for kt in range(KT):
-            last = kt == KT - 1
-            total = keep.tile([P, T], F32, name=f"total{kt}", align_bytes=64)
-            banks = []
-            for half in range(HALVES):
-                banks.append(base_product(kt, half))
-                if not last:
-                    nc.scalar.copy(total[:, tokens(half)], banks[half][:])
-            if last:
-                nc.scalar.copy(total[:, T - share : T], banks[1][:, BANK - share : BANK])
-            scatter(kt, early[kt], E)
-            cuts = [[0, T], [0, T], [0, BANK, T], [0, BANK // 2, BANK, T - share, T]][kt]
-            for c0, c1 in zip(cuts, cuts[1:]):
-                if not last or c1 == T:
-                    nc.gpsimd.tensor_tensor(total[:, c0:c1], total[:, c0:c1], windows[kt][:, c0:c1], ALU.add)
-                else:
-                    bank = banks[c0 // BANK][:, c0 % BANK : c0 % BANK + c1 - c0]
-                    nc.vector.tensor_tensor(total[:, c0:c1], windows[kt][:, c0:c1], bank, ALU.add)
-                store(kt, total, c0, c1)
+        scatter_scalar(0, 0, 2, dx_piece(0, 0, 2, "bank_e", nc.scalar.copy, "gate_slot")[:])
+        scatter_vector(1, 0, 2, dx_piece(1, 0, 2, "bank_f", nc.vector.tensor_copy, "dh_slot2")[:])
+        scatter_vector(1, 2, E, dx_piece(1, 2, E, "bank_a", nc.vector.tensor_copy, "dx12")[:])
+        dx0 = dx_piece(0, 2, E, "bank_h", nc.scalar.copy, "dx02")
+        for half, bank in enumerate(["bank_c", "bank_d"]):
+            base_product(0, half, bank)
+            base_copy(0, half)
+        scatter_scalar(0, 2, E, dx0[:])
+        dx2 = dx_piece(2, 0, E, "bank_b", nc.scalar.copy, "dx2")
+        dx3 = dx_piece(3, 0, E, "bank_g", nc.scalar.copy, "dx3")
+        for half in range(HALVES):
+            add_and_store(0, half * BANK, (half + 1) * BANK, False, nc.sync)
+        for half, bank in enumerate(["bank_e", "bank_f"]):
+            base_product(1, half, bank)
+            add_and_store(1, half * BANK, (half + 1) * BANK, True, nc.sync)
+        scatter_vector(2, 0, E, dx2[:])
+        base_product(3, 1, "bank_h")
+        base_copy(3, 1)
+        scatter_scalar(3, 0, 2, dx3[:, slots(0, 2)])
+        scatter_scalar(3, 2, E, dx3[:, slots(2, E)])
+        for half, bank in enumerate(["bank_c", "bank_d"]):
+            base_product(2, half, bank)
+            add_and_store(2, half * BANK, (half + 1) * BANK, True, nc.sync)
+        base_product(3, 0, "bank_a")
+        add_and_store(3, 0, BANK, True, nc.sync)
+        add_and_store(3, BANK, T, False, nc.sync)

@@ -42,9 +42,9 @@ def tile_moe_adb_relu_kernel(
         nc.sync.dma_start(offsets[:], offs)
 
         groups = [
-            {"dy1": 4 * T, "wb": 16 * H},
-            {"a0": 8 * PACK * C, "wa": 8 * K, "a1": 8 * PACK * C},
-            {"wt": 4 * K, "wt_s": PASSES * K},
+            {"dy0": 4 * T, "dy1": 4 * T, "wb0": 8 * H},
+            {"wb1": 8 * H, "a0": 8 * PACK * C, "wa0": 4 * K},
+            {"a1": 8 * PACK * C, "wa1": 4 * K, "wt": 4 * K, "wt_s": PASSES * K},
         ]
         place, zeros, end = {}, [], 0
         for number, group in enumerate(groups):
@@ -72,7 +72,7 @@ def tile_moe_adb_relu_kernel(
         dy_s = zeroed_planes("dy_s", PASSES, T, nc.vector)
         for tile in zeros:
             nc.gpsimd.memset(tile[:, 0:ZEROS], 0.0)
-        g_rows = keep.tile([P, C], F32, name="g_rows", align_bytes=64)
+        g_rows = keep.tile([P, C], F32, name="g_rows", tag="rows_slot", align_bytes=64)
         nc.vector.tensor_copy(g_rows[:], zeros[0][:, 0:1].to_broadcast([P, C]))
         wb_s = zeroed_planes("wb_s", E * PASSES, H, nc.vector)
         wa_s = zeroed_planes("wa_s", E, K, nc.gpsimd)
@@ -81,8 +81,8 @@ def tile_moe_adb_relu_kernel(
         windows = {kt: keep.tile([P, T], F32, name=f"window{kt}") for kt in range(KT)}
 
         dy_w = [load_tile(f"dy{s}", [P, T], I32)[:] for s in range(PASSES)]
-        wb_w = load_tile("wb", [P, E * PASSES, FP4_BYTES * H], U8)
-        wa_w = load_tile("wa", [P, E, FP4_BYTES * K], U8)
+        wb_w = [load_tile(f"wb{pair}", [P, 2 * PASSES, FP4_BYTES * H], U8) for pair in range(E // 2)]
+        wa_w = [load_tile(f"wa{pair}", [P, 2, FP4_BYTES * K], U8) for pair in range(E // 2)]
         wt_w = load_tile("wt", [P, PASSES, FP4_BYTES * K], U8)
         a_sb = [load_tile(f"a{pair}", [P, PACK, 2 * C], F32) for pair in range(E // 2)]
         g_col = keep.tile([P, ZEROS], F32, name="g_col", tag="gate_slot", align_bytes=64)
@@ -91,27 +91,32 @@ def tile_moe_adb_relu_kernel(
         def load_dy(s):
             nc.sync.dma_start(dy_w[s], dy_words[s].rearrange("p t d -> p (t d)").bitcast(I32))
 
-        def load_words(tile, words):
-            nc.sync.dma_start(tile[:].bitcast(I32), words.bitcast(I32).rearrange("e s p w -> p (e s) w"))
+        def load_pair(tile, words, pair):
+            nc.sync.dma_start(tile[:].bitcast(I32), words[2 * pair : 2 * pair + 2].bitcast(I32).rearrange("e s p w -> p (e s) w"))
 
         def load_a(pair):
             nc.sync.dma_start(a_sb[pair][:], a_rows[:, :, 2 * pair * C : 2 * (pair + 1) * C])
 
-        load_dy(0)
+        def zero_window(kt, c0, c1, group):
+            nc.scalar.activation(windows[kt][:, c0:c1], zeros[group][:, 0:1].to_broadcast([P, c1 - c0]), COPY)
+
         load_scales(dy_s, dy_scales, nc.sync)
+        load_dy(0)
         load_dy(1)
-        load_words(wb_w, wbt_words)
         nc.sync.dma_start(g_rows[0:E, :], gate[0:1, :].rearrange("o (e u) -> (o e) u", e=E))
+        load_pair(wb_w[0], wbt_words, 0)
         load_scales(wb_s, wbt_scales.rearrange("e s b w -> (e s) b w"), nc.sync)
         load_scales(wa_s, wat_scales.rearrange("e s b w -> (e s) b w"), nc.gpsimd)
-        nc.scalar.activation(windows[0][:, 0:ZEROS], zeros[1][:, 0:ZEROS], COPY)
-        nc.scalar.activation(windows[0][:, ZEROS:T], zeros[2][:, 0:1].to_broadcast([P, T - ZEROS]), COPY)
+        zero_window(0, 0, ZEROS, 1)
+        zero_window(0, ZEROS, T, 2)
         wt_s = zeroed_planes("wt_s", PASSES, K, nc.vector)
         for kt in range(1, KT):
             nc.scalar.activation(windows[kt][:], windows[0][:, 0:1].to_broadcast([P, T]), COPY)
+        load_pair(wb_w[1], wbt_words, 1)
         load_a(0)
-        load_words(wa_w, wat_words)
+        load_pair(wa_w[0], wat_words, 0)
         load_a(1)
+        load_pair(wa_w[1], wat_words, 1)
         nc.sync.dma_start(wt_w[:].bitcast(I32), wt_words.bitcast(I32).rearrange("s p w -> p s w"))
         load_scales(wt_s, wt_scales, nc.sync)
 
@@ -120,7 +125,10 @@ def tile_moe_adb_relu_kernel(
         nc.scalar.copy(g_col[:, 0:E], g_ps[:, 0:E])
 
         slot_w = keep.tile([P, PASSES, S], U32, name="slot_w", align_bytes=64)
-        slot_s = keep.tile([P, PASSES, S], U8, name="slot_s", align_bytes=64)
+        slot_s = [
+            keep.tile([P, PASSES, 2 * C], U8, name=f"slot_s{pair}", tag=slot, align_bytes=64)
+            for pair, slot in enumerate(["scales_slot", "rows_slot"])
+        ]
         mask, h_sb, turned, dh, dh_w, dh_s, total, base_ps = {}, {}, {}, {}, {}, {}, {}, {}
 
         def slots(e0, e1):
@@ -135,11 +143,11 @@ def tile_moe_adb_relu_kernel(
         def gather_words(s, e0, e1):
             nc.vector.tensor_copy(slot_w[:, s, slots(e0, e1)], dy_w[s].bitcast(U32).indirect(slot_offsets(e0, e1)))
 
-        def gather_scales(s, e0, e1):
-            nc.vector.tensor_copy(slot_s[:, s, slots(e0, e1)], dy_s[:, s, :].indirect(slot_offsets(e0, e1)))
+        def gather_scales(s, pair):
+            nc.vector.tensor_copy(slot_s[pair][:, s, :], dy_s[:, s, :].indirect(slot_offsets(2 * pair, 2 * pair + 2)))
 
-        def make_mask(pair):
-            mask[pair] = keep.tile([P, 2 * C, PACK], BF16, name=f"mask{pair}", align_bytes=64)
+        def make_mask(pair, slot):
+            mask[pair] = keep.tile([P, 2 * C, PACK], BF16, name=f"mask{pair}", tag=slot, align_bytes=64)
             nc.vector.tensor_scalar(
                 out=mask[pair][:].rearrange("p (c i) d -> p c d i", i=4),
                 in0=a_sb[pair][:].rearrange("p d (c i) -> p c d i", i=4),
@@ -154,8 +162,8 @@ def tile_moe_adb_relu_kernel(
                 nc.tensor.matmul_mx(
                     out=h_ps[:],
                     lhsT=slot_w[:, s, slots(e, e + 1)].bitcast(FP8X4),
-                    lhsT_scale=slot_s[:, s, slots(e, e + 1)],
-                    rhs=wb_w[:, e * PASSES + s, :].bitcast(FP4X4),
+                    lhsT_scale=slot_s[e // 2][:, s, slots(e % 2, e % 2 + 1)],
+                    rhs=wb_w[e // 2][:, (e % 2) * PASSES + s, :].bitcast(FP4X4),
                     rhs_scale=wb_s[:, e * PASSES + s, :],
                     start=(s == 0),
                     stop=(s == PASSES - 1),
@@ -189,19 +197,19 @@ def tile_moe_adb_relu_kernel(
                 dh_w[e] = words[:, slots(e - e0, e - e0 + 1)]
                 dh_s[e] = scales[:, slots(e - e0, e - e0 + 1)]
 
-        def dx_piece(kt, e0, e1, bank, copier, slot):
-            dx_ps = psum.tile([P, (e1 - e0) * C], F32, name="dx_ps", tag=bank)
-            for e in range(e0, e1):
+        def dx_piece(parts, bank, copier, slot):
+            dx_ps = psum.tile([P, len(parts) * C], F32, name="dx_ps", tag=bank)
+            for n, (kt, e) in enumerate(parts):
                 nc.tensor.matmul_mx(
-                    out=dx_ps[:, slots(e - e0, e - e0 + 1)],
-                    lhsT=wa_w[:, e, FP4_BYTES * kt * P : FP4_BYTES * (kt + 1) * P].bitcast(FP4X4),
+                    out=dx_ps[:, slots(n, n + 1)],
+                    lhsT=wa_w[e // 2][:, e % 2, FP4_BYTES * kt * P : FP4_BYTES * (kt + 1) * P].bitcast(FP4X4),
                     lhsT_scale=wa_s[:, e, kt * P : (kt + 1) * P],
                     rhs=dh_w[e].bitcast(FP8X4),
                     rhs_scale=dh_s[e],
                     start=True,
                     stop=True,
                 )
-            piece = keep.tile([P, (e1 - e0) * C], F32, name=f"dx{kt}{e0}", tag=slot, align_bytes=64)
+            piece = keep.tile([P, len(parts) * C], F32, name="dx_sb", tag=slot, align_bytes=64)
             copier(piece[:], dx_ps[:])
             return piece
 
@@ -238,49 +246,50 @@ def tile_moe_adb_relu_kernel(
         for kt in range(KT):
             total[kt] = keep.tile([P, T], F32, name=f"total{kt}", align_bytes=64)
 
-        gather_words(0, 0, E)
+        def row(kt, e0, e1):
+            return [(kt, e) for e in range(e0, e1)]
+
         for s in range(PASSES):
-            gather_scales(s, 0, 2)
-        gather_words(1, 0, 2)
+            gather_scales(s, 0)
+        for s in range(PASSES):
+            gather_words(s, 0, 2)
         first_product(0, "bank_a")
         first_product(1, "bank_b")
-        gather_words(1, 2, E)
         for s in range(PASSES):
-            gather_scales(s, 2, E)
-        make_mask(0)
+            gather_words(s, 2, E)
+        for s in range(PASSES):
+            gather_scales(s, 1)
+        make_mask(0, "mask_slot")
         turn_and_mask(0, 1, "bank_e")
         quantize(0, 1)
-        first_product(2, "bank_c")
-        turn_and_mask(1, 2, "bank_f")
-        quantize(1, 2)
+        first_product(2, "bank_a")
         first_product(3, "bank_d")
-        make_mask(1)
-        turn_and_mask(2, E, "bank_g")
-        quantize(2, E)
+        make_mask(1, "dh_slot0")
+        for e, bank in [(1, "bank_f"), (2, "bank_g"), (3, "bank_b")]:
+            turn_and_mask(e, e + 1, bank)
+            quantize(e, e + 1)
 
-        scatter_scalar(0, 0, 2, dx_piece(0, 0, 2, "bank_e", nc.scalar.copy, "gate_slot")[:])
-        scatter_vector(1, 0, 2, dx_piece(1, 0, 2, "bank_f", nc.vector.tensor_copy, "dh_slot2")[:])
-        scatter_vector(1, 2, E, dx_piece(1, 2, E, "bank_a", nc.vector.tensor_copy, "dx12")[:])
-        dx0 = dx_piece(0, 2, E, "bank_h", nc.scalar.copy, "dx02")
-        for half, bank in enumerate(["bank_c", "bank_d"]):
-            base_product(0, half, bank)
-            base_copy(0, half)
-        scatter_scalar(0, 2, E, dx0[:])
-        dx2 = dx_piece(2, 0, E, "bank_b", nc.scalar.copy, "dx2")
-        dx3 = dx_piece(3, 0, E, "bank_g", nc.scalar.copy, "dx3")
+        first = dx_piece([(0, 0), (3, 0)], "bank_e", nc.scalar.copy, "gate_slot")
+        scatter_scalar(0, 0, 1, first[:, slots(0, 1)])
+        scatter_scalar(3, 0, 1, first[:, slots(1, 2)])
+        scatter_vector(1, 0, 2, dx_piece(row(1, 0, 2), "bank_h", nc.vector.tensor_copy, "dh_slot3")[:])
+        scatter_vector(1, 2, E, dx_piece(row(1, 2, E), "bank_a", nc.vector.tensor_copy, "dx12")[:])
+        dx0 = dx_piece(row(0, 1, E), "bank_e", nc.scalar.copy, "dx0")
+        dx2 = dx_piece(row(2, 0, E), "bank_f", nc.scalar.copy, "dx2")
+        scatter_scalar(0, 1, E, dx0[:])
+        for kt, half, bank in [(0, 0, "bank_c"), (0, 1, "bank_d"), (3, 1, "bank_g")]:
+            base_product(kt, half, bank)
+            base_copy(kt, half)
+        for kt, half, bank in [(1, 0, "bank_b"), (1, 1, "bank_h"), (2, 0, "bank_a"), (2, 1, "bank_e"), (3, 0, "bank_f")]:
+            base_product(kt, half, bank)
+        dx3 = dx_piece(row(3, 1, E), "bank_c", nc.scalar.copy, "dx3")
         for half in range(HALVES):
             add_and_store(0, half * BANK, (half + 1) * BANK, False, nc.sync)
-        for half, bank in enumerate(["bank_e", "bank_f"]):
-            base_product(1, half, bank)
+        for half in range(HALVES):
             add_and_store(1, half * BANK, (half + 1) * BANK, True, nc.sync)
         scatter_vector(2, 0, E, dx2[:])
-        base_product(3, 1, "bank_h")
-        base_copy(3, 1)
-        scatter_scalar(3, 0, 2, dx3[:, slots(0, 2)])
-        scatter_scalar(3, 2, E, dx3[:, slots(2, E)])
-        for half, bank in enumerate(["bank_c", "bank_d"]):
-            base_product(2, half, bank)
+        scatter_scalar(3, 1, E, dx3[:])
+        for half in range(HALVES):
             add_and_store(2, half * BANK, (half + 1) * BANK, True, nc.sync)
-        base_product(3, 0, "bank_a")
         add_and_store(3, 0, BANK, True, nc.sync)
         add_and_store(3, BANK, T, False, nc.sync)

@@ -42,9 +42,8 @@ def tile_moe_adb_relu_kernel(
         nc.sync.dma_start(offsets[:], offs)
 
         groups = [
-            {"dy0": 4 * T, "dy1": 4 * T, "wb0": 8 * H},
-            {"wb1": 8 * H, "a0": 8 * PACK * C, "wa0": 4 * K},
-            {"a1": 8 * PACK * C, "wa1": 4 * K, "wt": 4 * K, "wt_s": PASSES * K},
+            {"dy1": 4 * T, "wb0": 8 * H},
+            {"a": 4 * PACK * S, "wb1": 8 * H, "wa0": 4 * K, "wa1": 4 * K, "wt": 4 * K, "wt_s": PASSES * K},
         ]
         place, zeros, end = {}, [], 0
         for number, group in enumerate(groups):
@@ -53,6 +52,10 @@ def tile_moe_adb_relu_kernel(
                 place[name] = end
                 end = end + size
             zeros.append(loads.tile([P, (end - start) // 4], F32, name=f"zeros{number}", offset=start, align_bytes=64))
+
+        place["slot_s1"] = end
+        place["g_rows"] = end + 2 * C
+        place["slot_w1_2"] = end + PASSES * 2 * C
 
         def load_tile(name, shape, dtype):
             if name in place:
@@ -64,29 +67,29 @@ def tile_moe_adb_relu_kernel(
             engine.memset(planes[:].rearrange("p c w -> p (c w)").bitcast(I32), 0)
             return planes
 
-        def load_scales(planes, rows, queue):
+        def load_scales(planes, rows, queues):
             by_r = rows.bitcast(I32).rearrange("c (q r) w -> r q c w", r=4)
-            for r in range(4):
+            for r, queue in enumerate(queues):
                 queue.dma_start(planes[r:P:32, :, :].bitcast(I32), by_r[r])
 
-        dy_s = zeroed_planes("dy_s", PASSES, T, nc.vector)
-        for tile in zeros:
+        windows = {kt: keep.tile([P, T], F32, name=f"window{kt}", align_bytes=64) for kt in range(KT)}
+        zero = keep.tile([P, ZEROS], F32, name="zero")
+        for tile in zeros + [zero]:
             nc.gpsimd.memset(tile[:, 0:ZEROS], 0.0)
-        g_rows = keep.tile([P, C], F32, name="g_rows", tag="rows_slot", align_bytes=64)
-        nc.vector.tensor_copy(g_rows[:], zeros[0][:, 0:1].to_broadcast([P, C]))
+        dy_s = zeroed_planes("dy_s", PASSES, T, nc.gpsimd)
+        nc.gpsimd.tensor_copy(windows[0][:, 0:ZEROS], zeros[0][:, 0:ZEROS])
+        g_rows = load_tile("g_rows", [P, C], F32)
+        nc.gpsimd.memset(g_rows[:], 0.0)
+        wa_s = zeroed_planes("wa_s", E, K, nc.vector)
         wb_s = zeroed_planes("wb_s", E * PASSES, H, nc.vector)
-        wa_s = zeroed_planes("wa_s", E, K, nc.gpsimd)
-        ident = keep.tile([P, P], F32, name="ident")
-        make_identity(nc, ident[:])
-        windows = {kt: keep.tile([P, T], F32, name=f"window{kt}") for kt in range(KT)}
+        nc.vector.tensor_copy(windows[1][:, 0:ZEROS], zeros[1][:, 0:ZEROS])
 
         dy_w = [load_tile(f"dy{s}", [P, T], I32)[:] for s in range(PASSES)]
         wb_w = [load_tile(f"wb{pair}", [P, 2 * PASSES, FP4_BYTES * H], U8) for pair in range(E // 2)]
         wa_w = [load_tile(f"wa{pair}", [P, 2, FP4_BYTES * K], U8) for pair in range(E // 2)]
         wt_w = load_tile("wt", [P, PASSES, FP4_BYTES * K], U8)
-        a_sb = [load_tile(f"a{pair}", [P, PACK, 2 * C], F32) for pair in range(E // 2)]
+        a_sb = load_tile("a", [P, PACK, S], F32)
         g_col = keep.tile([P, ZEROS], F32, name="g_col", tag="gate_slot", align_bytes=64)
-        a_rows = a.rearrange("(p d) j -> p d j", d=PACK)
 
         def load_dy(s):
             nc.sync.dma_start(dy_w[s], dy_words[s].rearrange("p t d -> p (t d)").bitcast(I32))
@@ -94,42 +97,36 @@ def tile_moe_adb_relu_kernel(
         def load_pair(tile, words, pair):
             nc.sync.dma_start(tile[:].bitcast(I32), words[2 * pair : 2 * pair + 2].bitcast(I32).rearrange("e s p w -> p (e s) w"))
 
-        def load_a(pair):
-            nc.sync.dma_start(a_sb[pair][:], a_rows[:, :, 2 * pair * C : 2 * (pair + 1) * C])
-
-        def zero_window(kt, c0, c1, group):
-            nc.scalar.activation(windows[kt][:, c0:c1], zeros[group][:, 0:1].to_broadcast([P, c1 - c0]), COPY)
-
-        load_scales(dy_s, dy_scales, nc.sync)
         load_dy(0)
+        load_scales(dy_s, dy_scales, [nc.sync] * 4)
         load_dy(1)
-        nc.sync.dma_start(g_rows[0:E, :], gate[0:1, :].rearrange("o (e u) -> (o e) u", e=E))
         load_pair(wb_w[0], wbt_words, 0)
-        load_scales(wb_s, wbt_scales.rearrange("e s b w -> (e s) b w"), nc.sync)
-        load_scales(wa_s, wat_scales.rearrange("e s b w -> (e s) b w"), nc.gpsimd)
-        zero_window(0, 0, ZEROS, 1)
-        zero_window(0, ZEROS, T, 2)
+        nc.sync.dma_start(g_rows[0:E, :], gate[0:1, :].rearrange("o (e u) -> (o e) u", e=E))
+        load_scales(wb_s, wbt_scales.rearrange("e s b w -> (e s) b w"), [nc.sync] * 4)
+        ident = keep.tile([P, P], F32, name="ident")
+        make_identity(nc, ident[:])
+        load_scales(wa_s, wat_scales.rearrange("e s b w -> (e s) b w"), [nc.gpsimd] * 4)
         wt_s = zeroed_planes("wt_s", PASSES, K, nc.vector)
-        for kt in range(1, KT):
-            nc.scalar.activation(windows[kt][:], windows[0][:, 0:1].to_broadcast([P, T]), COPY)
+        for kt in range(KT):
+            start = ZEROS if kt < len(zeros) else 0
+            nc.scalar.activation(windows[kt][:, start:T], zero[:, 0:1].to_broadcast([P, T - start]), COPY)
+        nc.sync.dma_start(a_sb[:], a.rearrange("(p d) j -> p d j", d=PACK))
         load_pair(wb_w[1], wbt_words, 1)
-        load_a(0)
         load_pair(wa_w[0], wat_words, 0)
-        load_a(1)
+        load_scales(wt_s, wt_scales, [nc.sync] * 4)
         load_pair(wa_w[1], wat_words, 1)
         nc.sync.dma_start(wt_w[:].bitcast(I32), wt_words.bitcast(I32).rearrange("s p w -> p s w"))
-        load_scales(wt_s, wt_scales, nc.sync)
 
         g_ps = psum.tile([P, P], F32, name="g_ps", tag="bank_e")
         nc.tensor.transpose(g_ps[:], g_rows[:], ident[:])
         nc.scalar.copy(g_col[:, 0:E], g_ps[:, 0:E])
 
-        slot_w = keep.tile([P, PASSES, S], U32, name="slot_w", align_bytes=64)
+        slot_w = {}
         slot_s = [
-            keep.tile([P, PASSES, 2 * C], U8, name=f"slot_s{pair}", tag=slot, align_bytes=64)
-            for pair, slot in enumerate(["scales_slot", "rows_slot"])
+            load_tile(f"slot_s{pair}", [P, PASSES, 2 * C], U8) for pair in range(E // 2)
         ]
-        mask, h_sb, turned, dh, dh_w, dh_s, total, base_ps = {}, {}, {}, {}, {}, {}, {}, {}
+        mask = {}
+        h_sb, dh, dh_w, dh_s, total, base_ps = {}, {}, {}, {}, {}, {}
 
         def slots(e0, e1):
             return slice(e0 * C, e1 * C)
@@ -141,7 +138,10 @@ def tile_moe_adb_relu_kernel(
             return slice(half * BANK, (half + 1) * BANK)
 
         def gather_words(s, e0, e1):
-            nc.vector.tensor_copy(slot_w[:, s, slots(e0, e1)], dy_w[s].bitcast(U32).indirect(slot_offsets(e0, e1)))
+            words = load_tile(f"slot_w{s}_{e0}", [P, (e1 - e0) * C], U32)
+            nc.vector.tensor_copy(words[:], dy_w[s].bitcast(U32).indirect(slot_offsets(e0, e1)))
+            for e in range(e0, e1):
+                slot_w[s, e] = words[:, slots(e - e0, e - e0 + 1)]
 
         def gather_scales(s, pair):
             nc.vector.tensor_copy(slot_s[pair][:, s, :], dy_s[:, s, :].indirect(slot_offsets(2 * pair, 2 * pair + 2)))
@@ -150,7 +150,7 @@ def tile_moe_adb_relu_kernel(
             mask[pair] = keep.tile([P, 2 * C, PACK], BF16, name=f"mask{pair}", tag=slot, align_bytes=64)
             nc.vector.tensor_scalar(
                 out=mask[pair][:].rearrange("p (c i) d -> p c d i", i=4),
-                in0=a_sb[pair][:].rearrange("p d (c i) -> p c d i", i=4),
+                in0=a_sb[:, :, slots(2 * pair, 2 * pair + 2)].rearrange("p d (c i) -> p c d i", i=4),
                 scalar1=0.0,
                 scalar2=None,
                 op0=ALU.is_gt,
@@ -161,7 +161,7 @@ def tile_moe_adb_relu_kernel(
             for s in range(PASSES):
                 nc.tensor.matmul_mx(
                     out=h_ps[:],
-                    lhsT=slot_w[:, s, slots(e, e + 1)].bitcast(FP8X4),
+                    lhsT=slot_w[s, e].bitcast(FP8X4),
                     lhsT_scale=slot_s[e // 2][:, s, slots(e % 2, e % 2 + 1)],
                     rhs=wb_w[e // 2][:, (e % 2) * PASSES + s, :].bitcast(FP4X4),
                     rhs_scale=wb_s[:, e * PASSES + s, :],
@@ -249,14 +249,13 @@ def tile_moe_adb_relu_kernel(
         def row(kt, e0, e1):
             return [(kt, e) for e in range(e0, e1)]
 
+        gather_words(0, 0, E)
         for s in range(PASSES):
             gather_scales(s, 0)
-        for s in range(PASSES):
-            gather_words(s, 0, 2)
+        gather_words(1, 0, 2)
         first_product(0, "bank_a")
         first_product(1, "bank_b")
-        for s in range(PASSES):
-            gather_words(s, 2, E)
+        gather_words(1, 2, E)
         for s in range(PASSES):
             gather_scales(s, 1)
         make_mask(0, "mask_slot")

@@ -43,7 +43,7 @@ def tile_moe_adb_relu_kernel(
 
         groups = [
             {"dy1": 4 * T, "wb0": 8 * H},
-            {"a": 4 * PACK * S, "wb1": 8 * H, "wa0": 4 * K, "wa1": 4 * K, "wt": 4 * K, "wt_s": PASSES * K},
+            {"a0": 8 * PACK * C, "wb1": 8 * H, "a1": 8 * PACK * C, "wa0": 4 * K, "wa1": 4 * K, "wt": 4 * K, "wt_s": PASSES * K},
         ]
         place, zeros, end = {}, [], 0
         for number, group in enumerate(groups):
@@ -88,7 +88,8 @@ def tile_moe_adb_relu_kernel(
         wb_w = [load_tile(f"wb{pair}", [P, 2 * PASSES, FP4_BYTES * H], U8) for pair in range(E // 2)]
         wa_w = [load_tile(f"wa{pair}", [P, 2, FP4_BYTES * K], U8) for pair in range(E // 2)]
         wt_w = load_tile("wt", [P, PASSES, FP4_BYTES * K], U8)
-        a_sb = load_tile("a", [P, PACK, S], F32)
+        a_sb = [load_tile(f"a{pair}", [P, PACK, 2 * C], F32) for pair in range(E // 2)]
+        a_rows = a.rearrange("(p d) j -> p d j", d=PACK)
         g_col = keep.tile([P, ZEROS], F32, name="g_col", tag="gate_slot", align_bytes=64)
 
         def load_dy(s):
@@ -96,6 +97,9 @@ def tile_moe_adb_relu_kernel(
 
         def load_pair(tile, words, pair):
             nc.sync.dma_start(tile[:].bitcast(I32), words[2 * pair : 2 * pair + 2].bitcast(I32).rearrange("e s p w -> p (e s) w"))
+
+        def load_a(pair):
+            nc.sync.dma_start(a_sb[pair][:], a_rows[:, :, 2 * pair * C : 2 * (pair + 1) * C])
 
         load_dy(0)
         load_scales(dy_s, dy_scales, [nc.sync] * 4)
@@ -105,17 +109,18 @@ def tile_moe_adb_relu_kernel(
         load_scales(wb_s, wbt_scales.rearrange("e s b w -> (e s) b w"), [nc.sync] * 4)
         ident = keep.tile([P, P], F32, name="ident")
         make_identity(nc, ident[:])
-        load_scales(wa_s, wat_scales.rearrange("e s b w -> (e s) b w"), [nc.gpsimd] * 4)
         wt_s = zeroed_planes("wt_s", PASSES, K, nc.vector)
         for kt in range(KT):
             start = ZEROS if kt < len(zeros) else 0
             nc.scalar.activation(windows[kt][:, start:T], zero[:, 0:1].to_broadcast([P, T - start]), COPY)
-        nc.sync.dma_start(a_sb[:], a.rearrange("(p d) j -> p d j", d=PACK))
+        load_a(0)
         load_pair(wb_w[1], wbt_words, 1)
-        load_pair(wa_w[0], wat_words, 0)
-        load_scales(wt_s, wt_scales, [nc.sync] * 4)
-        load_pair(wa_w[1], wat_words, 1)
+        load_a(1)
+        load_scales(wa_s, wat_scales.rearrange("e s b w -> (e s) b w"), [nc.sync] * 4)
+        for pair in range(E // 2):
+            load_pair(wa_w[pair], wat_words, pair)
         nc.sync.dma_start(wt_w[:].bitcast(I32), wt_words.bitcast(I32).rearrange("s p w -> p s w"))
+        load_scales(wt_s, wt_scales, [nc.sync] * 4)
 
         g_ps = psum.tile([P, P], F32, name="g_ps", tag="bank_e")
         nc.tensor.transpose(g_ps[:], g_rows[:], ident[:])
@@ -150,7 +155,7 @@ def tile_moe_adb_relu_kernel(
             mask[pair] = keep.tile([P, 2 * C, PACK], BF16, name=f"mask{pair}", tag=slot, align_bytes=64)
             nc.vector.tensor_scalar(
                 out=mask[pair][:].rearrange("p (c i) d -> p c d i", i=4),
-                in0=a_sb[:, :, slots(2 * pair, 2 * pair + 2)].rearrange("p d (c i) -> p c d i", i=4),
+                in0=a_sb[pair][:].rearrange("p d (c i) -> p c d i", i=4),
                 scalar1=0.0,
                 scalar2=None,
                 op0=ALU.is_gt,

@@ -27,6 +27,7 @@ HALVES = T // BANK
 LIST_ROWS = 16
 FP4_BYTES = 2
 ZEROS = 8
+SHARE = 352
 
 
 def tile_moe_adb_relu_kernel(
@@ -113,9 +114,9 @@ def tile_moe_adb_relu_kernel(
         for kt in range(KT):
             start = ZEROS if kt < len(zeros) else 0
             nc.scalar.activation(windows[kt][:, start:T], zero[:, 0:1].to_broadcast([P, T - start]), COPY)
-        load_a(0)
         load_pair(wb_w[1], wbt_words, 1)
-        load_a(1)
+        for pair in range(E // 2):
+            load_a(pair)
         load_scales(wa_s, wat_scales.rearrange("e s b w -> (e s) b w"), [nc.sync] * 4)
         for pair in range(E // 2):
             load_pair(wa_w[pair], wat_words, pair)
@@ -237,8 +238,8 @@ def tile_moe_adb_relu_kernel(
                     stop=(s == PASSES - 1),
                 )
 
-        def base_copy(kt, half):
-            nc.scalar.copy(total[kt][:, tokens(half)], base_ps[kt, half][:])
+        def base_copy(kt, c0, c1):
+            nc.scalar.copy(total[kt][:, c0:c1], base_ps[kt, c0 // BANK][:, c0 % BANK : c0 % BANK + c1 - c0])
 
         def add_and_store(kt, c0, c1, from_psum, queue):
             if from_psum:
@@ -264,26 +265,28 @@ def tile_moe_adb_relu_kernel(
         for s in range(PASSES):
             gather_scales(s, 1)
         make_mask(0, "mask_slot")
-        turn_and_mask(0, 1, "bank_e")
-        quantize(0, 1)
+        turn_and_mask(0, 2, "bank_e")
         first_product(2, "bank_a")
-        first_product(3, "bank_d")
-        make_mask(1, "dh_slot0")
-        for e, bank in [(1, "bank_f"), (2, "bank_g"), (3, "bank_b")]:
-            turn_and_mask(e, e + 1, bank)
-            quantize(e, e + 1)
+        first_product(3, "bank_b")
+        make_mask(1, "mask_slot")
+        quantize(0, 2)
+        turn_and_mask(2, E, "bank_g")
+        dx1 = dx_piece(row(1, 0, 2), "bank_h", nc.vector.tensor_copy, "mask_slot")
+        quantize(2, E)
 
         first = dx_piece([(0, 0), (3, 0)], "bank_e", nc.scalar.copy, "gate_slot")
         scatter_scalar(0, 0, 1, first[:, slots(0, 1)])
         scatter_scalar(3, 0, 1, first[:, slots(1, 2)])
-        scatter_vector(1, 0, 2, dx_piece(row(1, 0, 2), "bank_h", nc.vector.tensor_copy, "dh_slot3")[:])
+        scatter_vector(1, 0, 2, dx1[:])
         scatter_vector(1, 2, E, dx_piece(row(1, 2, E), "bank_a", nc.vector.tensor_copy, "dx12")[:])
         dx0 = dx_piece(row(0, 1, E), "bank_e", nc.scalar.copy, "dx0")
-        dx2 = dx_piece(row(2, 0, E), "bank_f", nc.scalar.copy, "dx2")
+        dx2 = dx_piece(row(2, 0, E), "bank_f", nc.vector.tensor_copy, "dx2")
         scatter_scalar(0, 1, E, dx0[:])
-        for kt, half, bank in [(0, 0, "bank_c"), (0, 1, "bank_d"), (3, 1, "bank_g")]:
-            base_product(kt, half, bank)
-            base_copy(kt, half)
+        for half, bank in enumerate(["bank_c", "bank_d"]):
+            base_product(0, half, bank)
+            base_copy(0, half * BANK, (half + 1) * BANK)
+        base_product(3, 1, "bank_g")
+        base_copy(3, T - SHARE, T)
         for kt, half, bank in [(1, 0, "bank_b"), (1, 1, "bank_h"), (2, 0, "bank_a"), (2, 1, "bank_e"), (3, 0, "bank_f")]:
             base_product(kt, half, bank)
         dx3 = dx_piece(row(3, 1, E), "bank_c", nc.scalar.copy, "dx3")
@@ -296,4 +299,5 @@ def tile_moe_adb_relu_kernel(
         for half in range(HALVES):
             add_and_store(2, half * BANK, (half + 1) * BANK, True, nc.sync)
         add_and_store(3, 0, BANK, True, nc.sync)
-        add_and_store(3, BANK, T, False, nc.sync)
+        add_and_store(3, BANK, T - SHARE, True, nc.sync)
+        add_and_store(3, T - SHARE, T, False, nc.sync)

@@ -43,8 +43,8 @@ def tile_moe_adb_relu_kernel(
         nc.sync.dma_start(offsets[:], offs)
 
         groups = [
-            {"dy1": 4 * T, "wb0": 8 * H},
-            {"a0": 8 * PACK * C, "wb1": 8 * H, "a1": 8 * PACK * C, "wa0": 4 * K, "wa1": 4 * K, "wt": 4 * K, "wt_s": PASSES * K},
+            {"wb0": 8 * H, "wb1": 8 * H, "a0": 8 * PACK * C, "a1": 8 * PACK * C, "wa_s": E * K},
+            {"wa0": 4 * K, "wa1": 4 * K, "wt": 4 * K, "wt_s": PASSES * K},
         ]
         place, zeros, end = {}, [], 0
         for number, group in enumerate(groups):
@@ -78,11 +78,11 @@ def tile_moe_adb_relu_kernel(
         for tile in zeros + [zero]:
             nc.gpsimd.memset(tile[:, 0:ZEROS], 0.0)
         dy_s = zeroed_planes("dy_s", PASSES, T, nc.gpsimd)
-        nc.gpsimd.tensor_copy(windows[0][:, 0:ZEROS], zeros[0][:, 0:ZEROS])
         g_rows = load_tile("g_rows", [P, C], F32)
         nc.gpsimd.memset(g_rows[:], 0.0)
-        wa_s = zeroed_planes("wa_s", E, K, nc.vector)
         wb_s = zeroed_planes("wb_s", E * PASSES, H, nc.vector)
+        nc.vector.tensor_copy(windows[0][:, 0:ZEROS], zeros[0][:, 0:ZEROS])
+        wa_s = zeroed_planes("wa_s", E, K, nc.vector)
         nc.vector.tensor_copy(windows[1][:, 0:ZEROS], zeros[1][:, 0:ZEROS])
 
         dy_w = [load_tile(f"dy{s}", [P, T], I32)[:] for s in range(PASSES)]
@@ -103,11 +103,11 @@ def tile_moe_adb_relu_kernel(
             nc.sync.dma_start(a_sb[pair][:], a_rows[:, :, 2 * pair * C : 2 * (pair + 1) * C])
 
         load_dy(0)
-        load_scales(dy_s, dy_scales, [nc.sync] * 4)
         load_dy(1)
-        load_pair(wb_w[0], wbt_words, 0)
+        load_scales(dy_s, dy_scales, [nc.sync] * 4)
         nc.sync.dma_start(g_rows[0:E, :], gate[0:1, :].rearrange("o (e u) -> (o e) u", e=E))
         load_scales(wb_s, wbt_scales.rearrange("e s b w -> (e s) b w"), [nc.sync] * 4)
+        load_pair(wb_w[0], wbt_words, 0)
         ident = keep.tile([P, P], F32, name="ident")
         make_identity(nc, ident[:])
         wt_s = zeroed_planes("wt_s", PASSES, K, nc.vector)
@@ -256,9 +256,9 @@ def tile_moe_adb_relu_kernel(
             return [(kt, e) for e in range(e0, e1)]
 
         gather_words(0, 0, E)
+        gather_words(1, 0, 2)
         for s in range(PASSES):
             gather_scales(s, 0)
-        gather_words(1, 0, 2)
         first_product(0, "bank_a")
         first_product(1, "bank_b")
         gather_words(1, 2, E)

@@ -54,10 +54,6 @@ def tile_moe_adb_relu_kernel(
                 end = end + size
             zeros.append(loads.tile([P, (end - start) // 4], F32, name=f"zeros{number}", offset=start, align_bytes=64))
 
-        place["slot_s1"] = end
-        place["g_rows"] = end + 2 * C
-        place["slot_w1_2"] = end + PASSES * 2 * C
-
         def load_tile(name, shape, dtype):
             if name in place:
                 return loads.tile(shape, dtype, name=name, offset=place[name], align_bytes=64)
@@ -77,10 +73,10 @@ def tile_moe_adb_relu_kernel(
         zero = keep.tile([P, ZEROS], F32, name="zero")
         for tile in zeros + [zero]:
             nc.gpsimd.memset(tile[:, 0:ZEROS], 0.0)
-        dy_s = zeroed_planes("dy_s", PASSES, T, nc.gpsimd)
         g_rows = load_tile("g_rows", [P, C], F32)
         nc.gpsimd.memset(g_rows[:], 0.0)
         wb_s = zeroed_planes("wb_s", E * PASSES, H, nc.vector)
+        dy_s = zeroed_planes("dy_s", PASSES, T, nc.vector)
         nc.vector.tensor_copy(windows[0][:, 0:ZEROS], zeros[0][:, 0:ZEROS])
         wa_s = zeroed_planes("wa_s", E, K, nc.vector)
         nc.vector.tensor_copy(windows[1][:, 0:ZEROS], zeros[1][:, 0:ZEROS])
@@ -104,9 +100,9 @@ def tile_moe_adb_relu_kernel(
 
         load_dy(0)
         load_dy(1)
-        load_scales(dy_s, dy_scales, [nc.sync] * 4)
         nc.sync.dma_start(g_rows[0:E, :], gate[0:1, :].rearrange("o (e u) -> (o e) u", e=E))
         load_scales(wb_s, wbt_scales.rearrange("e s b w -> (e s) b w"), [nc.sync] * 4)
+        load_scales(dy_s, dy_scales, [nc.sync] * 4)
         load_pair(wb_w[0], wbt_words, 0)
         ident = keep.tile([P, P], F32, name="ident")
         make_identity(nc, ident[:])
@@ -255,13 +251,12 @@ def tile_moe_adb_relu_kernel(
         def row(kt, e0, e1):
             return [(kt, e) for e in range(e0, e1)]
 
-        gather_words(0, 0, E)
-        gather_words(1, 0, 2)
+        for s in range(PASSES):
+            gather_words(s, 0, E)
         for s in range(PASSES):
             gather_scales(s, 0)
         first_product(0, "bank_a")
         first_product(1, "bank_b")
-        gather_words(1, 2, E)
         for s in range(PASSES):
             gather_scales(s, 1)
         make_mask(0, "mask_slot")

@@ -23,11 +23,10 @@ PACK = 4
 PASSES = N // (P * PACK)
 KT = K // P
 BANK = 512
-HALVES = T // BANK
 LIST_ROWS = 16
 FP4_BYTES = 2
 ZEROS = 8
-SHARE = 352
+SHARE = 256
 
 
 def tile_moe_adb_relu_kernel(
@@ -43,8 +42,8 @@ def tile_moe_adb_relu_kernel(
         nc.sync.dma_start(offsets[:], offs)
 
         groups = [
-            {"wb0": 8 * H, "wb1": 8 * H, "a0": 8 * PACK * C, "a1": 8 * PACK * C, "wa_s": E * K},
-            {"wa0": 4 * K, "wa1": 4 * K, "wt": 4 * K, "wt_s": PASSES * K},
+            {"wb0": 4 * H, "wb1": 4 * H, "a0": 8 * PACK * C, "wb2": 8 * H, "wa_s": E * K},
+            {"wa0": 4 * K, "a1": 8 * PACK * C, "wa1": 4 * K, "wt": 4 * K, "wt_s": PASSES * K},
         ]
         place, zeros, end = {}, [], 0
         for number, group in enumerate(groups):
@@ -64,71 +63,71 @@ def tile_moe_adb_relu_kernel(
             engine.memset(planes[:].rearrange("p c w -> p (c w)").bitcast(I32), 0)
             return planes
 
-        def load_scales(planes, rows, queues):
+        def load_scales(planes, rows):
             by_r = rows.bitcast(I32).rearrange("c (q r) w -> r q c w", r=4)
-            for r, queue in enumerate(queues):
-                queue.dma_start(planes[r:P:32, :, :].bitcast(I32), by_r[r])
+            for r in range(4):
+                nc.sync.dma_start(planes[r:P:32, :, :].bitcast(I32), by_r[r])
 
         windows = {kt: keep.tile([P, T], F32, name=f"window{kt}", align_bytes=64) for kt in range(KT)}
         zero = keep.tile([P, ZEROS], F32, name="zero")
+        dy_s = zeroed_planes("dy_s", PASSES, T, nc.gpsimd)
         for tile in zeros + [zero]:
             nc.gpsimd.memset(tile[:, 0:ZEROS], 0.0)
-        g_rows = load_tile("g_rows", [P, C], F32)
-        nc.gpsimd.memset(g_rows[:], 0.0)
         wb_s = zeroed_planes("wb_s", E * PASSES, H, nc.vector)
-        dy_s = zeroed_planes("dy_s", PASSES, T, nc.vector)
+        g_rows = load_tile("g_rows", [P, C], F32)
+        nc.vector.memset(g_rows[:], 0.0)
         nc.vector.tensor_copy(windows[0][:, 0:ZEROS], zeros[0][:, 0:ZEROS])
         wa_s = zeroed_planes("wa_s", E, K, nc.vector)
         nc.vector.tensor_copy(windows[1][:, 0:ZEROS], zeros[1][:, 0:ZEROS])
+        wt_s = zeroed_planes("wt_s", PASSES, K, nc.vector)
+        ident = keep.tile([P, P], F32, name="ident")
+        make_identity(nc, ident[:])
+        for kt in range(KT):
+            start = ZEROS if kt < len(zeros) else 0
+            nc.scalar.activation(windows[kt][:, start:T], zero[:, 0:1].to_broadcast([P, T - start]), COPY)
 
-        dy_w = [load_tile(f"dy{s}", [P, T], I32)[:] for s in range(PASSES)]
-        wb_w = [load_tile(f"wb{pair}", [P, 2 * PASSES, FP4_BYTES * H], U8) for pair in range(E // 2)]
-        wa_w = [load_tile(f"wa{pair}", [P, 2, FP4_BYTES * K], U8) for pair in range(E // 2)]
-        wt_w = load_tile("wt", [P, PASSES, FP4_BYTES * K], U8)
-        a_sb = [load_tile(f"a{pair}", [P, PACK, 2 * C], F32) for pair in range(E // 2)]
+        dy_w, wb_w, wa_w, a_sb = {}, {}, {}, {}
         a_rows = a.rearrange("(p d) j -> p d j", d=PACK)
-        g_col = keep.tile([P, ZEROS], F32, name="g_col", tag="gate_slot", align_bytes=64)
 
         def load_dy(s):
+            dy_w[s] = load_tile(f"dy{s}", [P, T], I32)[:]
             nc.sync.dma_start(dy_w[s], dy_words[s].rearrange("p t d -> p (t d)").bitcast(I32))
 
-        def load_pair(tile, words, pair):
-            nc.sync.dma_start(tile[:].bitcast(I32), words[2 * pair : 2 * pair + 2].bitcast(I32).rearrange("e s p w -> p (e s) w"))
+        def load_adapters(name, words, e0, e1):
+            passes, width = words.shape[1], words.shape[3]
+            tile = load_tile(name, [P, (e1 - e0) * passes, width], U8)
+            nc.sync.dma_start(tile[:].bitcast(I32), words[e0:e1].bitcast(I32).rearrange("e s p w -> p (e s) w"))
+            return {e: tile[:, (e - e0) * passes : (e - e0 + 1) * passes, :] for e in range(e0, e1)}
 
         def load_a(pair):
+            a_sb[pair] = load_tile(f"a{pair}", [P, PACK, 2 * C], F32)
             nc.sync.dma_start(a_sb[pair][:], a_rows[:, :, 2 * pair * C : 2 * (pair + 1) * C])
 
         load_dy(0)
         load_dy(1)
+        load_scales(dy_s, dy_scales)
+        load_scales(wb_s, wbt_scales.rearrange("e s b w -> (e s) b w"))
         nc.sync.dma_start(g_rows[0:E, :], gate[0:1, :].rearrange("o (e u) -> (o e) u", e=E))
-        load_scales(wb_s, wbt_scales.rearrange("e s b w -> (e s) b w"), [nc.sync] * 4)
-        load_scales(dy_s, dy_scales, [nc.sync] * 4)
-        load_pair(wb_w[0], wbt_words, 0)
-        ident = keep.tile([P, P], F32, name="ident")
-        make_identity(nc, ident[:])
-        wt_s = zeroed_planes("wt_s", PASSES, K, nc.vector)
-        for kt in range(KT):
-            start = ZEROS if kt < len(zeros) else 0
-            nc.scalar.activation(windows[kt][:, start:T], zero[:, 0:1].to_broadcast([P, T - start]), COPY)
-        load_pair(wb_w[1], wbt_words, 1)
-        for pair in range(E // 2):
-            load_a(pair)
-        load_scales(wa_s, wat_scales.rearrange("e s b w -> (e s) b w"), [nc.sync] * 4)
-        for pair in range(E // 2):
-            load_pair(wa_w[pair], wat_words, pair)
+        wb_w.update(load_adapters("wb0", wbt_words, 0, 1))
+        wb_w.update(load_adapters("wb1", wbt_words, 1, 2))
+        load_a(0)
+        wb_w.update(load_adapters("wb2", wbt_words, 2, E))
+        load_scales(wa_s, wat_scales.rearrange("e s b w -> (e s) b w"))
+        wa_w.update(load_adapters("wa0", wat_words, 0, 2))
+        load_a(1)
+        wa_w.update(load_adapters("wa1", wat_words, 2, E))
+        wt_w = load_tile("wt", [P, PASSES, FP4_BYTES * K], U8)
         nc.sync.dma_start(wt_w[:].bitcast(I32), wt_words.bitcast(I32).rearrange("s p w -> p s w"))
-        load_scales(wt_s, wt_scales, [nc.sync] * 4)
+        load_scales(wt_s, wt_scales)
 
-        g_ps = psum.tile([P, P], F32, name="g_ps", tag="bank_e")
+        g_col = keep.tile([P, ZEROS], F32, name="g_col", tag="gate_slot", align_bytes=64)
+        g_ps = psum.tile([P, P], F32, name="g_ps", tag="bank_d")
         nc.tensor.transpose(g_ps[:], g_rows[:], ident[:])
         nc.scalar.copy(g_col[:, 0:E], g_ps[:, 0:E])
 
-        slot_w = {}
-        slot_s = [
-            load_tile(f"slot_s{pair}", [P, PASSES, 2 * C], U8) for pair in range(E // 2)
-        ]
-        mask = {}
-        h_sb, dh, dh_w, dh_s, total, base_ps = {}, {}, {}, {}, {}, {}
+        slot_w = [keep.tile([P, S], U32, name=f"slot_w{s}", align_bytes=64) for s in range(PASSES)]
+        slot_s = [keep.tile([P, PASSES, 2 * C], U8, name=f"slot_s{pair}", align_bytes=64) for pair in range(E // 2)]
+        mask, h_sb, dh, dh_w, dh_s = {}, {}, {}, {}, {}
 
         def slots(e0, e1):
             return slice(e0 * C, e1 * C)
@@ -136,20 +135,14 @@ def tile_moe_adb_relu_kernel(
         def slot_offsets(e0, e1):
             return offsets[:, e0 * C // LIST_ROWS : e1 * C // LIST_ROWS]
 
-        def tokens(half):
-            return slice(half * BANK, (half + 1) * BANK)
-
-        def gather_words(s, e0, e1):
-            words = load_tile(f"slot_w{s}_{e0}", [P, (e1 - e0) * C], U32)
-            nc.vector.tensor_copy(words[:], dy_w[s].bitcast(U32).indirect(slot_offsets(e0, e1)))
-            for e in range(e0, e1):
-                slot_w[s, e] = words[:, slots(e - e0, e - e0 + 1)]
+        def gather_words(s):
+            nc.vector.tensor_copy(slot_w[s][:], dy_w[s].bitcast(U32).indirect(offsets[:]))
 
         def gather_scales(s, pair):
             nc.vector.tensor_copy(slot_s[pair][:, s, :], dy_s[:, s, :].indirect(slot_offsets(2 * pair, 2 * pair + 2)))
 
-        def make_mask(pair, slot):
-            mask[pair] = keep.tile([P, 2 * C, PACK], BF16, name=f"mask{pair}", tag=slot, align_bytes=64)
+        def make_mask(pair):
+            mask[pair] = keep.tile([P, 2 * C, PACK], BF16, name=f"mask{pair}", tag="mask_slot", align_bytes=64)
             nc.vector.tensor_scalar(
                 out=mask[pair][:].rearrange("p (c i) d -> p c d i", i=4),
                 in0=a_sb[pair][:].rearrange("p d (c i) -> p c d i", i=4),
@@ -163,9 +156,9 @@ def tile_moe_adb_relu_kernel(
             for s in range(PASSES):
                 nc.tensor.matmul_mx(
                     out=h_ps[:],
-                    lhsT=slot_w[s, e].bitcast(FP8X4),
+                    lhsT=slot_w[s][:, slots(e, e + 1)].bitcast(FP8X4),
                     lhsT_scale=slot_s[e // 2][:, s, slots(e % 2, e % 2 + 1)],
-                    rhs=wb_w[e // 2][:, (e % 2) * PASSES + s, :].bitcast(FP4X4),
+                    rhs=wb_w[e][:, s, :].bitcast(FP4X4),
                     rhs_scale=wb_s[:, e * PASSES + s, :],
                     start=(s == 0),
                     stop=(s == PASSES - 1),
@@ -175,45 +168,44 @@ def tile_moe_adb_relu_kernel(
                 h_sb[e][:], h_ps[:].rearrange("u (m w t) -> u w m t", w=2, t=2), COPY, scale=g_col[:, e : e + 1]
             )
 
-        def turn_and_mask(e0, e1, bank):
-            count = e1 - e0
-            turned = psum.tile([P, count * C, 2], F32, name="turned", tag=bank)
-            for e in range(e0, e1):
-                pairs = h_sb[e][:].rearrange("u w m t -> u (w m t)").bitcast(F32)
+        def turn_and_mask(pair, bank):
+            turned = psum.tile([P, 2 * C, 2], F32, name="turned", tag=bank)
+            for n in range(2):
+                words = h_sb[2 * pair + n][:].rearrange("u w m t -> u (w m t)").bitcast(F32)
                 for w in range(2):
-                    nc.tensor.transpose(turned[:, slots(e - e0, e - e0 + 1), w], pairs[:, w * P : (w + 1) * P], ident[:])
-            dh[e0] = keep.tile([P, count * C * PACK], BF16, name=f"dh{e0}", tag=f"dh_slot{e0}", align_bytes=64)
+                    nc.tensor.transpose(turned[:, slots(n, n + 1), w], words[:, w * P : (w + 1) * P], ident[:])
+            dh[pair] = keep.tile([P, 2 * C * PACK], BF16, name=f"dh{pair}", align_bytes=64)
             nc.vector.tensor_tensor(
-                dh[e0][:],
+                dh[pair][:],
                 turned[:].rearrange("p u w -> p (u w)").bitcast(BF16),
-                mask[e0 // 2][:, slots(e0 % 2, e0 % 2 + count), :].rearrange("p u d -> p (u d)"),
+                mask[pair][:].rearrange("p u d -> p (u d)"),
                 ALU.mult,
             )
 
-        def quantize(e0, e1):
-            count = e1 - e0
-            words = keep.tile([P, count * C], U32, name=f"dh_w{e0}", align_bytes=64)
-            scales = keep.tile([P, count * C], U8, name=f"dh_s{e0}", align_bytes=64)
-            nc.vector.quantize_mx(out=words[:].bitcast(FP8X4), scales=scales[:], in_=dh[e0][:])
-            for e in range(e0, e1):
-                dh_w[e] = words[:, slots(e - e0, e - e0 + 1)]
-                dh_s[e] = scales[:, slots(e - e0, e - e0 + 1)]
+        def quantize(pair):
+            words = keep.tile([P, 2 * C], U32, name=f"dh_w{pair}", align_bytes=64)
+            scales = keep.tile([P, 2 * C], U8, name=f"dh_s{pair}", align_bytes=64)
+            nc.vector.quantize_mx(out=words[:].bitcast(FP8X4), scales=scales[:], in_=dh[pair][:])
+            for n in range(2):
+                dh_w[2 * pair + n] = words[:, slots(n, n + 1)]
+                dh_s[2 * pair + n] = scales[:, slots(n, n + 1)]
 
-        def dx_piece(parts, bank, copier, slot):
+        def second_products(parts, bank):
             dx_ps = psum.tile([P, len(parts) * C], F32, name="dx_ps", tag=bank)
             for n, (kt, e) in enumerate(parts):
                 nc.tensor.matmul_mx(
                     out=dx_ps[:, slots(n, n + 1)],
-                    lhsT=wa_w[e // 2][:, e % 2, FP4_BYTES * kt * P : FP4_BYTES * (kt + 1) * P].bitcast(FP4X4),
+                    lhsT=wa_w[e][:, 0, FP4_BYTES * kt * P : FP4_BYTES * (kt + 1) * P].bitcast(FP4X4),
                     lhsT_scale=wa_s[:, e, kt * P : (kt + 1) * P],
                     rhs=dh_w[e].bitcast(FP8X4),
                     rhs_scale=dh_s[e],
                     start=True,
                     stop=True,
                 )
-            piece = keep.tile([P, len(parts) * C], F32, name="dx_sb", tag=slot, align_bytes=64)
-            copier(piece[:], dx_ps[:])
-            return piece
+            return dx_ps
+
+        def row(kt, e0, e1):
+            return [(kt, e) for e in range(e0, e1)]
 
         def scatter_vector(kt, e0, e1, source):
             nc.vector.tensor_copy(windows[kt][:].indirect(slot_offsets(e0, e1)), source)
@@ -221,78 +213,94 @@ def tile_moe_adb_relu_kernel(
         def scatter_scalar(kt, e0, e1, source):
             nc.scalar.activation(windows[kt][:].indirect(slot_offsets(e0, e1)), source, COPY)
 
-        def base_product(kt, half, bank):
-            base_ps[kt, half] = psum.tile([P, BANK], F32, name="base_ps", tag=bank)
+        def base_product(kt, c0, c1, bank):
+            base_ps = psum.tile([P, c1 - c0], F32, name="base_ps", tag=bank)
             for s in range(PASSES):
                 nc.tensor.matmul_mx(
-                    out=base_ps[kt, half][:],
+                    out=base_ps[:],
                     lhsT=wt_w[:, s, FP4_BYTES * kt * P : FP4_BYTES * (kt + 1) * P].bitcast(FP4X4),
                     lhsT_scale=wt_s[:, s, kt * P : (kt + 1) * P],
-                    rhs=dy_w[s][:, tokens(half)].bitcast(FP8X4),
-                    rhs_scale=dy_s[:, s, tokens(half)],
+                    rhs=dy_w[s][:, c0:c1].bitcast(FP8X4),
+                    rhs_scale=dy_s[:, s, c0:c1],
                     start=(s == 0),
                     stop=(s == PASSES - 1),
                 )
+            return base_ps
 
-        def base_copy(kt, c0, c1):
-            nc.scalar.copy(total[kt][:, c0:c1], base_ps[kt, c0 // BANK][:, c0 % BANK : c0 % BANK + c1 - c0])
+        total = {}
 
-        def add_and_store(kt, c0, c1, from_psum, queue):
-            if from_psum:
-                bank = base_ps[kt, c0 // BANK][:, c0 % BANK : c0 % BANK + c1 - c0]
-                nc.vector.tensor_tensor(total[kt][:, c0:c1], windows[kt][:, c0:c1], bank, ALU.add)
-            else:
-                nc.gpsimd.tensor_tensor(total[kt][:, c0:c1], total[kt][:, c0:c1], windows[kt][:, c0:c1], ALU.add)
+        def store(kt, c0, c1, queue):
             queue.dma_start(out[kt * P : (kt + 1) * P, c0:c1], total[kt][:, c0:c1])
 
-        for kt in range(KT):
-            total[kt] = keep.tile([P, T], F32, name=f"total{kt}", align_bytes=64)
+        def add_gpsimd(kt, c0, c1, base_sb, queue):
+            nc.gpsimd.tensor_tensor(total[kt][:, c0:c1], base_sb, windows[kt][:, c0:c1], ALU.add)
+            store(kt, c0, c1, queue)
 
-        def row(kt, e0, e1):
-            return [(kt, e) for e in range(e0, e1)]
+        def add_vector(kt, c0, c1, base_ps):
+            nc.vector.tensor_tensor(total[kt][:, c0:c1], windows[kt][:, c0:c1], base_ps[:], ALU.add)
+            store(kt, c0, c1, nc.sync)
 
         for s in range(PASSES):
-            gather_words(s, 0, E)
-        for s in range(PASSES):
-            gather_scales(s, 0)
+            gather_words(s)
+        for pair in range(E // 2):
+            for s in range(PASSES):
+                gather_scales(s, pair)
         first_product(0, "bank_a")
         first_product(1, "bank_b")
-        for s in range(PASSES):
-            gather_scales(s, 1)
-        make_mask(0, "mask_slot")
-        turn_and_mask(0, 2, "bank_e")
-        first_product(2, "bank_a")
-        first_product(3, "bank_b")
-        make_mask(1, "mask_slot")
-        quantize(0, 2)
-        turn_and_mask(2, E, "bank_g")
-        dx1 = dx_piece(row(1, 0, 2), "bank_h", nc.vector.tensor_copy, "mask_slot")
-        quantize(2, E)
+        make_mask(0)
+        turn_and_mask(0, "bank_c")
+        first_product(2, "bank_b")
+        first_product(3, "bank_c")
+        quantize(0)
 
-        first = dx_piece([(0, 0), (3, 0)], "bank_e", nc.scalar.copy, "gate_slot")
-        scatter_scalar(0, 0, 1, first[:, slots(0, 1)])
-        scatter_scalar(3, 0, 1, first[:, slots(1, 2)])
-        scatter_vector(1, 0, 2, dx1[:])
-        scatter_vector(1, 2, E, dx_piece(row(1, 2, E), "bank_a", nc.vector.tensor_copy, "dx12")[:])
-        dx0 = dx_piece(row(0, 1, E), "bank_e", nc.scalar.copy, "dx0")
-        dx2 = dx_piece(row(2, 0, E), "bank_f", nc.vector.tensor_copy, "dx2")
-        scatter_scalar(0, 1, E, dx0[:])
-        for half, bank in enumerate(["bank_c", "bank_d"]):
-            base_product(0, half, bank)
-            base_copy(0, half * BANK, (half + 1) * BANK)
-        base_product(3, 1, "bank_g")
-        base_copy(3, T - SHARE, T)
-        for kt, half, bank in [(1, 0, "bank_b"), (1, 1, "bank_h"), (2, 0, "bank_a"), (2, 1, "bank_e"), (3, 0, "bank_f")]:
-            base_product(kt, half, bank)
-        dx3 = dx_piece(row(3, 1, E), "bank_c", nc.scalar.copy, "dx3")
-        for half in range(HALVES):
-            add_and_store(0, half * BANK, (half + 1) * BANK, False, nc.sync)
-        for half in range(HALVES):
-            add_and_store(1, half * BANK, (half + 1) * BANK, True, nc.sync)
-        scatter_vector(2, 0, E, dx2[:])
-        scatter_scalar(3, 1, E, dx3[:])
-        for half in range(HALVES):
-            add_and_store(2, half * BANK, (half + 1) * BANK, True, nc.sync)
-        add_and_store(3, 0, BANK, True, nc.sync)
-        add_and_store(3, BANK, T - SHARE, True, nc.sync)
-        add_and_store(3, T - SHARE, T, False, nc.sync)
+        early = keep.tile([P, 2 * C + S], F32, name="early", tag="gate_slot", align_bytes=64)
+        dx0_first, dx3 = early[:, slots(0, 2)], early[:, slots(2, 2 + E)]
+        dx2 = keep.tile([P, S], F32, name="dx2", align_bytes=64)
+        ps = second_products(row(0, 0, 2) + row(3, 0, 2), "bank_d")
+        nc.scalar.copy(dx0_first, ps[:, slots(0, 2)])
+        nc.scalar.copy(dx3[:, slots(0, 2)], ps[:, slots(2, E)])
+        nc.vector.tensor_copy(dx2[:, slots(0, 2)], second_products(row(2, 0, 2), "bank_a")[:])
+        ps1 = second_products(row(1, 0, 2), "bank_e")
+        scatter_scalar(0, 0, 2, dx0_first)
+        make_mask(1)
+        turn_and_mask(1, "bank_a")
+        dx1_first = loads.tile([P, 2 * C], F32, name="dx1_first", offset=place["a1"], align_bytes=64)
+        nc.vector.tensor_copy(dx1_first[:], ps1[:])
+        quantize(1)
+        scatter_vector(1, 0, 2, dx1_first[:])
+        scatter_scalar(3, 0, 1, dx3[:, slots(0, 1)])
+
+        dx0_second = keep.tile([P, 2 * C], F32, name="dx0_second", align_bytes=64)
+        nc.scalar.copy(dx0_second[:], second_products(row(0, 2, E), "bank_b")[:])
+        dx1_second = keep.tile([P, 2 * C], F32, name="dx1_second", align_bytes=64)
+        ps = second_products(row(1, 2, E) + row(2, 2, 3), "bank_c")
+        nc.vector.tensor_copy(dx1_second[:], ps[:, slots(0, 2)])
+        nc.vector.tensor_copy(dx2[:, slots(2, 3)], ps[:, slots(2, 3)])
+        scatter_vector(1, 2, E, dx1_second[:])
+        scatter_vector(2, 0, 3, dx2[:, slots(0, 3)])
+
+        base0 = keep.tile([P, T], F32, name="base0", tag="base_slot", align_bytes=64)
+        base2 = keep.tile([P, SHARE], F32, name="base2", align_bytes=64)
+        nc.scalar.copy(base0[:, 0:BANK], base_product(0, 0, BANK, "bank_a")[:])
+        scatter_scalar(0, 2, E, dx0_second[:])
+        shared = base_product(2, T - SHARE, T, "bank_e")
+        nc.scalar.copy(base0[:, BANK:T], base_product(0, BANK, T, "bank_d")[:])
+        nc.scalar.copy(base2[:], shared[:])
+        for kt in (0, 2, 3):
+            total[kt] = keep.tile([P, T], F32, name=f"total{kt}", align_bytes=64)
+        add_gpsimd(0, 0, BANK, base0[:, 0:BANK], nc.sync)
+        add_gpsimd(0, BANK, T, base0[:, BANK:T], nc.sync)
+        total[1] = keep.tile([P, T], F32, name="total1", tag="base_slot", align_bytes=64)
+        add_vector(1, 0, BANK, base_product(1, 0, BANK, "bank_b"))
+        add_vector(1, BANK, T, base_product(1, BANK, T, "bank_c"))
+
+        ps = second_products(row(3, 2, E) + row(2, 3, E), "bank_a")
+        nc.scalar.copy(dx3[:, slots(2, E)], ps[:, slots(0, 2)])
+        nc.scalar.copy(dx2[:, slots(3, E)], ps[:, slots(2, 3)])
+        scatter_scalar(3, 1, E, dx3[:, slots(1, E)])
+        scatter_scalar(2, 3, E, dx2[:, slots(3, E)])
+        add_vector(3, 0, BANK, base_product(3, 0, BANK, "bank_d"))
+        add_vector(3, BANK, T, base_product(3, BANK, T, "bank_e"))
+        add_vector(2, 0, BANK, base_product(2, 0, BANK, "bank_a"))
+        add_vector(2, BANK, T - SHARE, base_product(2, BANK, T - SHARE, "bank_b"))
+        add_gpsimd(2, T - SHARE, T, base2[:], nc.scalar)

@@ -26,6 +26,7 @@ BANK = 512
 LIST_ROWS = 16
 FP4_BYTES = 2
 ZEROS = 8
+SPLIT = 288
 SHARE = 256
 
 
@@ -43,7 +44,7 @@ def tile_moe_adb_relu_kernel(
 
         groups = [
             {"wb0": 4 * H, "wb1": 4 * H, "a0": 8 * PACK * C, "wb2": 8 * H, "wa_s": E * K},
-            {"wa0": 4 * K, "a1": 8 * PACK * C, "wa1": 4 * K, "wt": 4 * K, "wt_s": PASSES * K},
+            {"wa0": 4 * K, "a1": 8 * PACK * C, "wa1": 4 * K, "wt": 3 * K, "wt_s": PASSES * (K - P)},
         ]
         place, zeros, end = {}, [], 0
         for number, group in enumerate(groups):
@@ -79,7 +80,8 @@ def tile_moe_adb_relu_kernel(
         nc.vector.tensor_copy(windows[0][:, 0:ZEROS], zeros[0][:, 0:ZEROS])
         wa_s = zeroed_planes("wa_s", E, K, nc.vector)
         nc.vector.tensor_copy(windows[1][:, 0:ZEROS], zeros[1][:, 0:ZEROS])
-        wt_s = zeroed_planes("wt_s", PASSES, K, nc.vector)
+        wt_s = zeroed_planes("wt_s", PASSES, K - P, nc.vector)
+        wt0_s = zeroed_planes("wt0_s", PASSES, P, nc.vector)
         ident = keep.tile([P, P], F32, name="ident")
         make_identity(nc, ident[:])
         for kt in range(KT):
@@ -103,6 +105,15 @@ def tile_moe_adb_relu_kernel(
             a_sb[pair] = load_tile(f"a{pair}", [P, PACK, 2 * C], F32)
             nc.sync.dma_start(a_sb[pair][:], a_rows[:, :, 2 * pair * C : 2 * (pair + 1) * C])
 
+        wt0_rows = keep.tile([P, PASSES, 4, P // 4], I32, name="wt0_rows", align_bytes=64)
+        nc.sync.dma_start(
+            wt0_rows[0:4].rearrange("r s q w -> r (s q) w"),
+            wt_scales[:, :, 0:P].bitcast(I32).rearrange("s (q r) w -> r (s q) w", r=4),
+        )
+        wt0_w = keep.tile([P, PASSES, FP4_BYTES * P], U8, name="wt0", align_bytes=64)
+        nc.sync.dma_start(wt0_w[:].bitcast(I32), wt_words[:, :, 0 : FP4_BYTES * P].bitcast(I32).rearrange("s p w -> p s w"))
+        for q in range(4):
+            nc.vector.tensor_copy(wt0_s[32 * q : 32 * q + 4].bitcast(I32), wt0_rows[0:4, :, q, :])
         load_dy(0)
         load_dy(1)
         load_scales(dy_s, dy_scales)
@@ -116,9 +127,12 @@ def tile_moe_adb_relu_kernel(
         wa_w.update(load_adapters("wa0", wat_words, 0, 2))
         load_a(1)
         wa_w.update(load_adapters("wa1", wat_words, 2, E))
-        wt_w = load_tile("wt", [P, PASSES, FP4_BYTES * K], U8)
-        nc.sync.dma_start(wt_w[:].bitcast(I32), wt_words.bitcast(I32).rearrange("s p w -> p s w"))
-        load_scales(wt_s, wt_scales)
+        wt_w = load_tile("wt", [P, PASSES, FP4_BYTES * (K - P)], U8)
+        nc.sync.dma_start(wt_w[:].bitcast(I32), wt_words[:, :, FP4_BYTES * P :].bitcast(I32).rearrange("s p w -> p s w"))
+        load_scales(wt_s, wt_scales[:, :, P:K])
+        wt_tile = {0: (wt0_w[:], wt0_s[:])}
+        for kt in range(1, KT):
+            wt_tile[kt] = (wt_w[:, :, FP4_BYTES * (kt - 1) * P : FP4_BYTES * kt * P], wt_s[:, :, (kt - 1) * P : kt * P])
 
         g_col = keep.tile([P, ZEROS], F32, name="g_col", tag="gate_slot", align_bytes=64)
         g_ps = psum.tile([P, P], F32, name="g_ps", tag="bank_d")
@@ -132,14 +146,14 @@ def tile_moe_adb_relu_kernel(
         def slots(e0, e1):
             return slice(e0 * C, e1 * C)
 
-        def slot_offsets(e0, e1):
-            return offsets[:, e0 * C // LIST_ROWS : e1 * C // LIST_ROWS]
+        def entries(part):
+            return offsets[:, part.start // LIST_ROWS : part.stop // LIST_ROWS]
 
         def gather_words(s):
             nc.vector.tensor_copy(slot_w[s][:], dy_w[s].bitcast(U32).indirect(offsets[:]))
 
         def gather_scales(s, pair):
-            nc.vector.tensor_copy(slot_s[pair][:, s, :], dy_s[:, s, :].indirect(slot_offsets(2 * pair, 2 * pair + 2)))
+            nc.vector.tensor_copy(slot_s[pair][:, s, :], dy_s[:, s, :].indirect(entries(slots(2 * pair, 2 * pair + 2))))
 
         def make_mask(pair):
             mask[pair] = keep.tile([P, 2 * C, PACK], BF16, name=f"mask{pair}", tag="mask_slot", align_bytes=64)
@@ -207,19 +221,19 @@ def tile_moe_adb_relu_kernel(
         def row(kt, e0, e1):
             return [(kt, e) for e in range(e0, e1)]
 
-        def scatter_vector(kt, e0, e1, source):
-            nc.vector.tensor_copy(windows[kt][:].indirect(slot_offsets(e0, e1)), source)
+        def scatter_vector(kt, part, source):
+            nc.vector.tensor_copy(windows[kt][:].indirect(entries(part)), source)
 
-        def scatter_scalar(kt, e0, e1, source):
-            nc.scalar.activation(windows[kt][:].indirect(slot_offsets(e0, e1)), source, COPY)
+        def scatter_scalar(kt, part, source):
+            nc.scalar.activation(windows[kt][:].indirect(entries(part)), source, COPY)
 
         def base_product(kt, c0, c1, bank):
             base_ps = psum.tile([P, c1 - c0], F32, name="base_ps", tag=bank)
             for s in range(PASSES):
                 nc.tensor.matmul_mx(
                     out=base_ps[:],
-                    lhsT=wt_w[:, s, FP4_BYTES * kt * P : FP4_BYTES * (kt + 1) * P].bitcast(FP4X4),
-                    lhsT_scale=wt_s[:, s, kt * P : (kt + 1) * P],
+                    lhsT=wt_tile[kt][0][:, s, :].bitcast(FP4X4),
+                    lhsT_scale=wt_tile[kt][1][:, s, :],
                     rhs=dy_w[s][:, c0:c1].bitcast(FP8X4),
                     rhs_scale=dy_s[:, s, c0:c1],
                     start=(s == 0),
@@ -240,6 +254,9 @@ def tile_moe_adb_relu_kernel(
             nc.vector.tensor_tensor(total[kt][:, c0:c1], windows[kt][:, c0:c1], base_ps[:], ALU.add)
             store(kt, c0, c1, nc.sync)
 
+        base0 = keep.tile([P, T], F32, name="base0", tag="base_slot", align_bytes=64)
+        nc.scalar.copy(base0[:, 0:BANK], base_product(0, 0, BANK, "bank_f")[:])
+        nc.scalar.copy(base0[:, BANK:T], base_product(0, BANK, T, "bank_g")[:])
         for s in range(PASSES):
             gather_words(s)
         for pair in range(E // 2):
@@ -261,14 +278,14 @@ def tile_moe_adb_relu_kernel(
         nc.scalar.copy(dx3[:, slots(0, 2)], ps[:, slots(2, E)])
         nc.vector.tensor_copy(dx2[:, slots(0, 2)], second_products(row(2, 0, 2), "bank_a")[:])
         ps1 = second_products(row(1, 0, 2), "bank_e")
-        scatter_scalar(0, 0, 2, dx0_first)
+        scatter_scalar(0, slots(0, 2), dx0_first)
         make_mask(1)
         turn_and_mask(1, "bank_a")
         dx1_first = loads.tile([P, 2 * C], F32, name="dx1_first", offset=place["a1"], align_bytes=64)
         nc.vector.tensor_copy(dx1_first[:], ps1[:])
         quantize(1)
-        scatter_vector(1, 0, 2, dx1_first[:])
-        scatter_scalar(3, 0, 1, dx3[:, slots(0, 1)])
+        scatter_vector(1, slots(0, 2), dx1_first[:])
+        scatter_scalar(3, slots(0, 1), dx3[:, slots(0, 1)])
 
         dx0_second = keep.tile([P, 2 * C], F32, name="dx0_second", align_bytes=64)
         nc.scalar.copy(dx0_second[:], second_products(row(0, 2, E), "bank_b")[:])
@@ -276,16 +293,17 @@ def tile_moe_adb_relu_kernel(
         ps = second_products(row(1, 2, E) + row(2, 2, 3), "bank_c")
         nc.vector.tensor_copy(dx1_second[:], ps[:, slots(0, 2)])
         nc.vector.tensor_copy(dx2[:, slots(2, 3)], ps[:, slots(2, 3)])
-        scatter_vector(1, 2, E, dx1_second[:])
-        scatter_vector(2, 0, 3, dx2[:, slots(0, 3)])
-
-        base0 = keep.tile([P, T], F32, name="base0", tag="base_slot", align_bytes=64)
+        scatter_vector(1, slots(2, E), dx1_second[:])
+        scatter_vector(2, slice(0, SPLIT), dx2[:, 0:SPLIT])
+        ps = second_products(row(3, 2, E) + row(2, 3, E), "bank_a")
+        nc.scalar.copy(dx3[:, slots(2, E)], ps[:, slots(0, 2)])
+        scatter_scalar(0, slots(2, E), dx0_second[:])
+        nc.scalar.copy(dx2[:, slots(3, E)], ps[:, slots(2, 3)])
+        scatter_scalar(3, slots(1, E), dx3[:, slots(1, E)])
         base2 = keep.tile([P, SHARE], F32, name="base2", align_bytes=64)
-        nc.scalar.copy(base0[:, 0:BANK], base_product(0, 0, BANK, "bank_a")[:])
-        scatter_scalar(0, 2, E, dx0_second[:])
-        shared = base_product(2, T - SHARE, T, "bank_e")
-        nc.scalar.copy(base0[:, BANK:T], base_product(0, BANK, T, "bank_d")[:])
-        nc.scalar.copy(base2[:], shared[:])
+        nc.scalar.copy(base2[:], base_product(2, T - SHARE, T, "bank_e")[:])
+        scatter_scalar(2, slice(SPLIT, S), dx2[:, SPLIT:S])
+
         for kt in (0, 2, 3):
             total[kt] = keep.tile([P, T], F32, name=f"total{kt}", align_bytes=64)
         add_gpsimd(0, 0, BANK, base0[:, 0:BANK], nc.sync)
@@ -293,14 +311,8 @@ def tile_moe_adb_relu_kernel(
         total[1] = keep.tile([P, T], F32, name="total1", tag="base_slot", align_bytes=64)
         add_vector(1, 0, BANK, base_product(1, 0, BANK, "bank_b"))
         add_vector(1, BANK, T, base_product(1, BANK, T, "bank_c"))
-
-        ps = second_products(row(3, 2, E) + row(2, 3, E), "bank_a")
-        nc.scalar.copy(dx3[:, slots(2, E)], ps[:, slots(0, 2)])
-        nc.scalar.copy(dx2[:, slots(3, E)], ps[:, slots(2, 3)])
-        scatter_scalar(3, 1, E, dx3[:, slots(1, E)])
-        scatter_scalar(2, 3, E, dx2[:, slots(3, E)])
         add_vector(3, 0, BANK, base_product(3, 0, BANK, "bank_d"))
-        add_vector(3, BANK, T, base_product(3, BANK, T, "bank_e"))
+        add_vector(3, BANK, T, base_product(3, BANK, T, "bank_f"))
         add_vector(2, 0, BANK, base_product(2, 0, BANK, "bank_a"))
         add_vector(2, BANK, T - SHARE, base_product(2, BANK, T - SHARE, "bank_b"))
         add_gpsimd(2, T - SHARE, T, base2[:], nc.scalar)

@@ -26,7 +26,6 @@ BANK = 512
 LIST_ROWS = 16
 FP4_BYTES = 2
 ZEROS = 8
-SPLIT = 288
 SHARE = 256
 
 
@@ -40,11 +39,10 @@ def tile_moe_adb_relu_kernel(
         psum = ctx.enter_context(tc.psum_pool(name="psum", bufs=1))
 
         offsets = keep.tile([P, S // LIST_ROWS], U16, name="offsets")
-        nc.sync.dma_start(offsets[:], offs)
 
         groups = [
-            {"wb0": 4 * H, "wb1": 4 * H, "a0": 8 * PACK * C, "wb2": 8 * H, "wa_s": E * K},
-            {"wa0": 4 * K, "a1": 8 * PACK * C, "wa1": 4 * K, "wt": 3 * K, "wt_s": PASSES * (K - P)},
+            {"wb0": 4 * H, "wb1": 4 * H, "a0": 8 * PACK * C, "wb2": 8 * H, "wa_s0": 2 * K},
+            {"wa0": 4 * K, "a1": 8 * PACK * C, "wa_s1": 2 * K, "wa1": 4 * K, "wt": 3 * K, "wt_s": PASSES * (K - P)},
         ]
         place, zeros, end = {}, [], 0
         for number, group in enumerate(groups):
@@ -78,8 +76,9 @@ def tile_moe_adb_relu_kernel(
         g_rows = load_tile("g_rows", [P, C], F32)
         nc.vector.memset(g_rows[:], 0.0)
         nc.vector.tensor_copy(windows[0][:, 0:ZEROS], zeros[0][:, 0:ZEROS])
-        wa_s = zeroed_planes("wa_s", E, K, nc.vector)
+        wa_s = [zeroed_planes("wa_s0", 2, K, nc.vector)]
         nc.vector.tensor_copy(windows[1][:, 0:ZEROS], zeros[1][:, 0:ZEROS])
+        wa_s.append(zeroed_planes("wa_s1", 2, K, nc.vector))
         wt_s = zeroed_planes("wt_s", PASSES, K - P, nc.vector)
         wt0_s = zeroed_planes("wt0_s", PASSES, P, nc.vector)
         ident = keep.tile([P, P], F32, name="ident")
@@ -105,6 +104,8 @@ def tile_moe_adb_relu_kernel(
             a_sb[pair] = load_tile(f"a{pair}", [P, PACK, 2 * C], F32)
             nc.sync.dma_start(a_sb[pair][:], a_rows[:, :, 2 * pair * C : 2 * (pair + 1) * C])
 
+        load_dy(0)
+        nc.sync.dma_start(offsets[:], offs)
         wt0_rows = keep.tile([P, PASSES, 4, P // 4], I32, name="wt0_rows", align_bytes=64)
         nc.sync.dma_start(
             wt0_rows[0:4].rearrange("r s q w -> r (s q) w"),
@@ -114,7 +115,6 @@ def tile_moe_adb_relu_kernel(
         nc.sync.dma_start(wt0_w[:].bitcast(I32), wt_words[:, :, 0 : FP4_BYTES * P].bitcast(I32).rearrange("s p w -> p s w"))
         for q in range(4):
             nc.vector.tensor_copy(wt0_s[32 * q : 32 * q + 4].bitcast(I32), wt0_rows[0:4, :, q, :])
-        load_dy(0)
         load_dy(1)
         load_scales(dy_s, dy_scales)
         load_scales(wb_s, wbt_scales.rearrange("e s b w -> (e s) b w"))
@@ -123,9 +123,11 @@ def tile_moe_adb_relu_kernel(
         wb_w.update(load_adapters("wb1", wbt_words, 1, 2))
         load_a(0)
         wb_w.update(load_adapters("wb2", wbt_words, 2, E))
-        load_scales(wa_s, wat_scales.rearrange("e s b w -> (e s) b w"))
+        wa_rows = wat_scales.rearrange("e s b w -> (e s) b w")
+        load_scales(wa_s[0], wa_rows[0:2])
         wa_w.update(load_adapters("wa0", wat_words, 0, 2))
         load_a(1)
+        load_scales(wa_s[1], wa_rows[2:E])
         wa_w.update(load_adapters("wa1", wat_words, 2, E))
         wt_w = load_tile("wt", [P, PASSES, FP4_BYTES * (K - P)], U8)
         nc.sync.dma_start(wt_w[:].bitcast(I32), wt_words[:, :, FP4_BYTES * P :].bitcast(I32).rearrange("s p w -> p s w"))
@@ -134,7 +136,7 @@ def tile_moe_adb_relu_kernel(
         for kt in range(1, KT):
             wt_tile[kt] = (wt_w[:, :, FP4_BYTES * (kt - 1) * P : FP4_BYTES * kt * P], wt_s[:, :, (kt - 1) * P : kt * P])
 
-        g_col = keep.tile([P, ZEROS], F32, name="g_col", tag="gate_slot", align_bytes=64)
+        g_col = keep.tile([P, ZEROS], F32, name="g_col", align_bytes=64)
         g_ps = psum.tile([P, P], F32, name="g_ps", tag="bank_d")
         nc.tensor.transpose(g_ps[:], g_rows[:], ident[:])
         nc.scalar.copy(g_col[:, 0:E], g_ps[:, 0:E])
@@ -165,7 +167,7 @@ def tile_moe_adb_relu_kernel(
                 op0=ALU.is_gt,
             )
 
-        def first_product(e, bank):
+        def first_product(e, bank, on_vector=False):
             h_ps = psum.tile([P, H], F32, name="h_ps", tag=bank)
             for s in range(PASSES):
                 nc.tensor.matmul_mx(
@@ -178,9 +180,12 @@ def tile_moe_adb_relu_kernel(
                     stop=(s == PASSES - 1),
                 )
             h_sb[e] = keep.tile([P, 2, P, 2], BF16, name=f"h_sb{e}", align_bytes=64)
-            nc.scalar.activation(
-                h_sb[e][:], h_ps[:].rearrange("u (m w t) -> u w m t", w=2, t=2), COPY, scale=g_col[:, e : e + 1]
-            )
+            by_word = h_ps[:].rearrange("u (m w t) -> u w m t", w=2, t=2)
+            if on_vector:
+                return lambda: nc.vector.tensor_scalar(
+                    out=h_sb[e][:], in0=by_word, scalar1=g_col[:, e : e + 1], scalar2=None, op0=ALU.mult
+                )
+            nc.scalar.activation(h_sb[e][:], by_word, COPY, scale=g_col[:, e : e + 1])
 
         def turn_and_mask(pair, bank):
             turned = psum.tile([P, 2 * C, 2], F32, name="turned", tag=bank)
@@ -210,7 +215,7 @@ def tile_moe_adb_relu_kernel(
                 nc.tensor.matmul_mx(
                     out=dx_ps[:, slots(n, n + 1)],
                     lhsT=wa_w[e][:, 0, FP4_BYTES * kt * P : FP4_BYTES * (kt + 1) * P].bitcast(FP4X4),
-                    lhsT_scale=wa_s[:, e, kt * P : (kt + 1) * P],
+                    lhsT_scale=wa_s[e // 2][:, e % 2, kt * P : (kt + 1) * P],
                     rhs=dh_w[e].bitcast(FP8X4),
                     rhs_scale=dh_s[e],
                     start=True,
@@ -254,9 +259,10 @@ def tile_moe_adb_relu_kernel(
             nc.vector.tensor_tensor(total[kt][:, c0:c1], windows[kt][:, c0:c1], base_ps[:], ALU.add)
             store(kt, c0, c1, nc.sync)
 
-        base0 = keep.tile([P, T], F32, name="base0", tag="base_slot", align_bytes=64)
-        nc.scalar.copy(base0[:, 0:BANK], base_product(0, 0, BANK, "bank_f")[:])
-        nc.scalar.copy(base0[:, BANK:T], base_product(0, BANK, T, "bank_g")[:])
+        base0 = keep.tile([P, BANK], F32, name="base0", tag="base_slot", align_bytes=64)
+        base0_rest = keep.tile([P, BANK], F32, name="base0_rest", align_bytes=64)
+        nc.scalar.copy(base0[:], base_product(0, 0, BANK, "bank_f")[:])
+        nc.scalar.copy(base0_rest[:], base_product(0, BANK, T, "bank_g")[:])
         for s in range(PASSES):
             gather_words(s)
         for pair in range(E // 2):
@@ -267,52 +273,48 @@ def tile_moe_adb_relu_kernel(
         make_mask(0)
         turn_and_mask(0, "bank_c")
         first_product(2, "bank_b")
-        first_product(3, "bank_c")
+        last_copy = first_product(3, "bank_c", True)
         quantize(0)
+        last_copy()
 
-        early = keep.tile([P, 2 * C + S], F32, name="early", tag="gate_slot", align_bytes=64)
-        dx0_first, dx3 = early[:, slots(0, 2)], early[:, slots(2, 2 + E)]
-        dx2 = keep.tile([P, S], F32, name="dx2", align_bytes=64)
+        dx = {kt: keep.tile([P, S], F32, name=f"dx{kt}", align_bytes=64) for kt in (0, 1, 3)}
         ps = second_products(row(0, 0, 2) + row(3, 0, 2), "bank_d")
-        nc.scalar.copy(dx0_first, ps[:, slots(0, 2)])
-        nc.scalar.copy(dx3[:, slots(0, 2)], ps[:, slots(2, E)])
-        nc.vector.tensor_copy(dx2[:, slots(0, 2)], second_products(row(2, 0, 2), "bank_a")[:])
-        ps1 = second_products(row(1, 0, 2), "bank_e")
-        scatter_scalar(0, slots(0, 2), dx0_first)
+        nc.scalar.copy(dx[0][:, slots(0, 2)], ps[:, slots(0, 2)])
+        nc.scalar.copy(dx[3][:, slots(0, 2)], ps[:, slots(2, E)])
+        nc.vector.tensor_copy(dx[1][:, slots(0, 2)], second_products(row(1, 0, 2), "bank_a")[:])
+        ps2 = second_products(row(2, 0, 2), "bank_e")
+        scatter_scalar(0, slots(0, 2), dx[0][:, slots(0, 2)])
         make_mask(1)
         turn_and_mask(1, "bank_a")
-        dx1_first = loads.tile([P, 2 * C], F32, name="dx1_first", offset=place["a1"], align_bytes=64)
-        nc.vector.tensor_copy(dx1_first[:], ps1[:])
+        dx2_first = loads.tile([P, 2 * C], F32, name="dx2_first", offset=place["a1"], align_bytes=64)
+        nc.vector.tensor_copy(dx2_first[:], ps2[:])
         quantize(1)
-        scatter_vector(1, slots(0, 2), dx1_first[:])
-        scatter_scalar(3, slots(0, 1), dx3[:, slots(0, 1)])
+        scatter_vector(2, slots(0, 2), dx2_first[:])
+        scatter_scalar(3, slots(0, 1), dx[3][:, slots(0, 1)])
 
-        dx0_second = keep.tile([P, 2 * C], F32, name="dx0_second", align_bytes=64)
-        nc.scalar.copy(dx0_second[:], second_products(row(0, 2, E), "bank_b")[:])
-        dx1_second = keep.tile([P, 2 * C], F32, name="dx1_second", align_bytes=64)
-        ps = second_products(row(1, 2, E) + row(2, 2, 3), "bank_c")
-        nc.vector.tensor_copy(dx1_second[:], ps[:, slots(0, 2)])
-        nc.vector.tensor_copy(dx2[:, slots(2, 3)], ps[:, slots(2, 3)])
-        scatter_vector(1, slots(2, E), dx1_second[:])
-        scatter_vector(2, slice(0, SPLIT), dx2[:, 0:SPLIT])
-        ps = second_products(row(3, 2, E) + row(2, 3, E), "bank_a")
-        nc.scalar.copy(dx3[:, slots(2, E)], ps[:, slots(0, 2)])
-        scatter_scalar(0, slots(2, E), dx0_second[:])
-        nc.scalar.copy(dx2[:, slots(3, E)], ps[:, slots(2, 3)])
-        scatter_scalar(3, slots(1, E), dx3[:, slots(1, E)])
-        base2 = keep.tile([P, SHARE], F32, name="base2", align_bytes=64)
-        nc.scalar.copy(base2[:], base_product(2, T - SHARE, T, "bank_e")[:])
-        scatter_scalar(2, slice(SPLIT, S), dx2[:, SPLIT:S])
+        dx2_second = keep.tile([P, 2 * C], F32, name="dx2_second", align_bytes=64)
+        nc.scalar.copy(dx[0][:, slots(2, E)], second_products(row(0, 2, E), "bank_b")[:])
+        nc.vector.tensor_copy(dx[1][:, slots(2, E)], second_products(row(1, 2, E), "bank_c")[:])
+        ps = second_products(row(2, 2, E) + row(3, 2, E), "bank_a")
+        nc.scalar.copy(dx2_second[:], ps[:, slots(0, 2)])
+        scatter_scalar(0, slots(2, E), dx[0][:, slots(2, E)])
+        nc.scalar.copy(dx[3][:, slots(2, E)], ps[:, slots(2, E)])
+        scatter_scalar(2, slots(2, E), dx2_second[:])
+        scatter_scalar(3, slots(1, E), dx[3][:, slots(1, E)])
+        base3 = keep.tile([P, SHARE], F32, name="base3", align_bytes=64)
+        nc.vector.tensor_copy(base3[:], base_product(3, T - SHARE, T, "bank_e")[:])
+        scatter_vector(1, slots(0, E), dx[1][:])
 
-        for kt in (0, 2, 3):
+        for kt in (0, 3):
             total[kt] = keep.tile([P, T], F32, name=f"total{kt}", align_bytes=64)
-        add_gpsimd(0, 0, BANK, base0[:, 0:BANK], nc.sync)
-        add_gpsimd(0, BANK, T, base0[:, BANK:T], nc.sync)
-        total[1] = keep.tile([P, T], F32, name="total1", tag="base_slot", align_bytes=64)
-        add_vector(1, 0, BANK, base_product(1, 0, BANK, "bank_b"))
-        add_vector(1, BANK, T, base_product(1, BANK, T, "bank_c"))
-        add_vector(3, 0, BANK, base_product(3, 0, BANK, "bank_d"))
-        add_vector(3, BANK, T, base_product(3, BANK, T, "bank_f"))
-        add_vector(2, 0, BANK, base_product(2, 0, BANK, "bank_a"))
-        add_vector(2, BANK, T - SHARE, base_product(2, BANK, T - SHARE, "bank_b"))
-        add_gpsimd(2, T - SHARE, T, base2[:], nc.scalar)
+        add_gpsimd(0, 0, BANK, base0[:], nc.sync)
+        add_gpsimd(0, BANK, T, base0_rest[:], nc.sync)
+        later = keep.tile([P, 2 * T], F32, name="later", tag="base_slot", align_bytes=64)
+        total[1], total[2] = later[:, 0:T], later[:, T : 2 * T]
+        add_vector(2, 0, BANK, base_product(2, 0, BANK, "bank_b"))
+        add_vector(2, BANK, T, base_product(2, BANK, T, "bank_c"))
+        add_vector(1, 0, BANK, base_product(1, 0, BANK, "bank_d"))
+        add_vector(1, BANK, T, base_product(1, BANK, T, "bank_f"))
+        add_vector(3, 0, BANK, base_product(3, 0, BANK, "bank_a"))
+        add_vector(3, BANK, T - SHARE, base_product(3, BANK, T - SHARE, "bank_e"))
+        add_gpsimd(3, T - SHARE, T, base3[:], nc.scalar)

@@ -136,7 +136,7 @@ def tile_moe_adb_relu_kernel(
         for kt in range(1, KT):
             wt_tile[kt] = (wt_w[:, :, FP4_BYTES * (kt - 1) * P : FP4_BYTES * kt * P], wt_s[:, :, (kt - 1) * P : kt * P])
 
-        g_col = keep.tile([P, ZEROS], F32, name="g_col", align_bytes=64)
+        g_col = keep.tile([P, ZEROS], F32, name="g_col", tag="gate_slot", align_bytes=64)
         g_ps = psum.tile([P, P], F32, name="g_ps", tag="bank_d")
         nc.tensor.transpose(g_ps[:], g_rows[:], ident[:])
         nc.scalar.copy(g_col[:, 0:E], g_ps[:, 0:E])
@@ -167,7 +167,7 @@ def tile_moe_adb_relu_kernel(
                 op0=ALU.is_gt,
             )
 
-        def first_product(e, bank, on_vector=False):
+        def first_product(e, bank):
             h_ps = psum.tile([P, H], F32, name="h_ps", tag=bank)
             for s in range(PASSES):
                 nc.tensor.matmul_mx(
@@ -181,10 +181,6 @@ def tile_moe_adb_relu_kernel(
                 )
             h_sb[e] = keep.tile([P, 2, P, 2], BF16, name=f"h_sb{e}", align_bytes=64)
             by_word = h_ps[:].rearrange("u (m w t) -> u w m t", w=2, t=2)
-            if on_vector:
-                return lambda: nc.vector.tensor_scalar(
-                    out=h_sb[e][:], in0=by_word, scalar1=g_col[:, e : e + 1], scalar2=None, op0=ALU.mult
-                )
             nc.scalar.activation(h_sb[e][:], by_word, COPY, scale=g_col[:, e : e + 1])
 
         def turn_and_mask(pair, bank):
@@ -273,11 +269,11 @@ def tile_moe_adb_relu_kernel(
         make_mask(0)
         turn_and_mask(0, "bank_c")
         first_product(2, "bank_b")
-        last_copy = first_product(3, "bank_c", True)
+        first_product(3, "bank_h")
         quantize(0)
-        last_copy()
 
-        dx = {kt: keep.tile([P, S], F32, name=f"dx{kt}", align_bytes=64) for kt in (0, 1, 3)}
+        both = keep.tile([P, 2 * S], F32, name="both", tag="gate_slot", align_bytes=64)
+        dx = {0: both[:, 0:S], 3: both[:, S : 2 * S], 1: keep.tile([P, S], F32, name="dx1", align_bytes=64)[:]}
         ps = second_products(row(0, 0, 2) + row(3, 0, 2), "bank_d")
         nc.scalar.copy(dx[0][:, slots(0, 2)], ps[:, slots(0, 2)])
         nc.scalar.copy(dx[3][:, slots(0, 2)], ps[:, slots(2, E)])
@@ -303,7 +299,7 @@ def tile_moe_adb_relu_kernel(
         scatter_scalar(3, slots(1, E), dx[3][:, slots(1, E)])
         base3 = keep.tile([P, SHARE], F32, name="base3", align_bytes=64)
         nc.vector.tensor_copy(base3[:], base_product(3, T - SHARE, T, "bank_e")[:])
-        scatter_vector(1, slots(0, E), dx[1][:])
+        scatter_vector(1, slots(0, E), dx[1])
 
         for kt in (0, 3):
             total[kt] = keep.tile([P, T], F32, name=f"total{kt}", align_bytes=64)

@@ -41,7 +41,7 @@ def tile_moe_adb_relu_kernel(
         offsets = keep.tile([P, S // LIST_ROWS], U16, name="offsets")
 
         groups = [
-            {"wb0": 4 * H, "wb1": 4 * H, "a0": 8 * PACK * C, "wb2": 8 * H, "wa_s0": 2 * K},
+            {"dy1": 4 * T, "wb0": 4 * H, "wb1": 4 * H, "a0": 8 * PACK * C, "wb2": 8 * H, "wa_s0": 2 * K},
             {"wa0": 4 * K, "a1": 8 * PACK * C, "wa_s1": 2 * K, "wa1": 4 * K, "wt": 3 * K, "wt_s": PASSES * (K - P)},
         ]
         place, zeros, end = {}, [], 0
@@ -71,16 +71,16 @@ def tile_moe_adb_relu_kernel(
         zero = keep.tile([P, ZEROS], F32, name="zero")
         dy_s = zeroed_planes("dy_s", PASSES, T, nc.gpsimd)
         for tile in zeros + [zero]:
-            nc.gpsimd.memset(tile[:, 0:ZEROS], 0.0)
+            nc.vector.memset(tile[:, 0:ZEROS], 0.0)
+        wt0_s = zeroed_planes("wt0_s", PASSES, P, nc.vector)
+        nc.vector.tensor_copy(windows[0][:, 0:ZEROS], zeros[0][:, 0:ZEROS])
         wb_s = zeroed_planes("wb_s", E * PASSES, H, nc.vector)
         g_rows = load_tile("g_rows", [P, C], F32)
         nc.vector.memset(g_rows[:], 0.0)
-        nc.vector.tensor_copy(windows[0][:, 0:ZEROS], zeros[0][:, 0:ZEROS])
         wa_s = [zeroed_planes("wa_s0", 2, K, nc.vector)]
         nc.vector.tensor_copy(windows[1][:, 0:ZEROS], zeros[1][:, 0:ZEROS])
         wa_s.append(zeroed_planes("wa_s1", 2, K, nc.vector))
         wt_s = zeroed_planes("wt_s", PASSES, K - P, nc.vector)
-        wt0_s = zeroed_planes("wt0_s", PASSES, P, nc.vector)
         ident = keep.tile([P, P], F32, name="ident")
         make_identity(nc, ident[:])
         for kt in range(KT):
@@ -104,19 +104,19 @@ def tile_moe_adb_relu_kernel(
             a_sb[pair] = load_tile(f"a{pair}", [P, PACK, 2 * C], F32)
             nc.sync.dma_start(a_sb[pair][:], a_rows[:, :, 2 * pair * C : 2 * (pair + 1) * C])
 
-        load_dy(0)
         nc.sync.dma_start(offsets[:], offs)
         wt0_rows = keep.tile([P, PASSES, 4, P // 4], I32, name="wt0_rows", align_bytes=64)
         nc.sync.dma_start(
             wt0_rows[0:4].rearrange("r s q w -> r (s q) w"),
             wt_scales[:, :, 0:P].bitcast(I32).rearrange("s (q r) w -> r (s q) w", r=4),
         )
-        wt0_w = keep.tile([P, PASSES, FP4_BYTES * P], U8, name="wt0", align_bytes=64)
+        load_dy(0)
+        wt0_w = keep.tile([P, PASSES, FP4_BYTES * P], U8, name="wt0", tag="wt0_slot", align_bytes=64)
         nc.sync.dma_start(wt0_w[:].bitcast(I32), wt_words[:, :, 0 : FP4_BYTES * P].bitcast(I32).rearrange("s p w -> p s w"))
         for q in range(4):
             nc.vector.tensor_copy(wt0_s[32 * q : 32 * q + 4].bitcast(I32), wt0_rows[0:4, :, q, :])
-        load_dy(1)
         load_scales(dy_s, dy_scales)
+        load_dy(1)
         load_scales(wb_s, wbt_scales.rearrange("e s b w -> (e s) b w"))
         nc.sync.dma_start(g_rows[0:E, :], gate[0:1, :].rearrange("o (e u) -> (o e) u", e=E))
         wb_w.update(load_adapters("wb0", wbt_words, 0, 1))
@@ -142,7 +142,7 @@ def tile_moe_adb_relu_kernel(
         nc.scalar.copy(g_col[:, 0:E], g_ps[:, 0:E])
 
         slot_w = [keep.tile([P, S], U32, name=f"slot_w{s}", align_bytes=64) for s in range(PASSES)]
-        slot_s = [keep.tile([P, PASSES, 2 * C], U8, name=f"slot_s{pair}", align_bytes=64) for pair in range(E // 2)]
+        slot_s = {}
         mask, h_sb, dh, dh_w, dh_s = {}, {}, {}, {}, {}
 
         def slots(e0, e1):
@@ -228,18 +228,21 @@ def tile_moe_adb_relu_kernel(
         def scatter_scalar(kt, part, source):
             nc.scalar.activation(windows[kt][:].indirect(entries(part)), source, COPY)
 
+        def base_pass(kt, c0, c1, s, base_ps):
+            nc.tensor.matmul_mx(
+                out=base_ps[:],
+                lhsT=wt_tile[kt][0][:, s, :].bitcast(FP4X4),
+                lhsT_scale=wt_tile[kt][1][:, s, :],
+                rhs=dy_w[s][:, c0:c1].bitcast(FP8X4),
+                rhs_scale=dy_s[:, s, c0:c1],
+                start=(s == 0),
+                stop=(s == PASSES - 1),
+            )
+
         def base_product(kt, c0, c1, bank):
             base_ps = psum.tile([P, c1 - c0], F32, name="base_ps", tag=bank)
             for s in range(PASSES):
-                nc.tensor.matmul_mx(
-                    out=base_ps[:],
-                    lhsT=wt_tile[kt][0][:, s, :].bitcast(FP4X4),
-                    lhsT_scale=wt_tile[kt][1][:, s, :],
-                    rhs=dy_w[s][:, c0:c1].bitcast(FP8X4),
-                    rhs_scale=dy_s[:, s, c0:c1],
-                    start=(s == 0),
-                    stop=(s == PASSES - 1),
-                )
+                base_pass(kt, c0, c1, s, base_ps)
             return base_ps
 
         total = {}
@@ -257,13 +260,20 @@ def tile_moe_adb_relu_kernel(
 
         base0 = keep.tile([P, BANK], F32, name="base0", tag="base_slot", align_bytes=64)
         base0_rest = keep.tile([P, BANK], F32, name="base0_rest", align_bytes=64)
-        nc.scalar.copy(base0[:], base_product(0, 0, BANK, "bank_f")[:])
-        nc.scalar.copy(base0_rest[:], base_product(0, BANK, T, "bank_g")[:])
+        first_ps = [psum.tile([P, BANK], F32, name="first_ps", tag=bank) for bank in ("bank_f", "bank_g")]
         for s in range(PASSES):
-            gather_words(s)
-        for pair in range(E // 2):
-            for s in range(PASSES):
-                gather_scales(s, pair)
+            for half in range(2):
+                base_pass(0, half * BANK, (half + 1) * BANK, s, first_ps[half])
+        nc.scalar.copy(base0[:], first_ps[0][:])
+        nc.scalar.copy(base0_rest[:], first_ps[1][:])
+        slot_s[0] = keep.tile([P, PASSES, 2 * C], U8, name="slot_s0", align_bytes=64)
+        slot_s[1] = keep.tile([P, PASSES, 2 * C], U8, name="slot_s1", tag="wt0_slot", align_bytes=64)
+        gather_words(0)
+        for s in range(PASSES):
+            gather_scales(s, 0)
+        gather_words(1)
+        for s in range(PASSES):
+            gather_scales(s, 1)
         first_product(0, "bank_a")
         first_product(1, "bank_b")
         make_mask(0)
@@ -273,16 +283,17 @@ def tile_moe_adb_relu_kernel(
         quantize(0)
 
         both = keep.tile([P, 2 * S], F32, name="both", tag="gate_slot", align_bytes=64)
-        dx = {0: both[:, 0:S], 3: both[:, S : 2 * S], 1: keep.tile([P, S], F32, name="dx1", align_bytes=64)[:]}
-        ps = second_products(row(0, 0, 2) + row(3, 0, 2), "bank_d")
-        nc.scalar.copy(dx[0][:, slots(0, 2)], ps[:, slots(0, 2)])
-        nc.scalar.copy(dx[3][:, slots(0, 2)], ps[:, slots(2, E)])
-        nc.vector.tensor_copy(dx[1][:, slots(0, 2)], second_products(row(1, 0, 2), "bank_a")[:])
+        dx = {0: both[:, 0:S], 3: both[:, S : 2 * S]}
+        nc.scalar.copy(dx[0][:, slots(0, 2)], second_products(row(0, 0, 2), "bank_d")[:])
+        nc.scalar.copy(dx[3][:, slots(0, 2)], second_products(row(3, 0, 2), "bank_g")[:])
+        ps1 = second_products(row(1, 0, 2), "bank_a")
         ps2 = second_products(row(2, 0, 2), "bank_e")
         scatter_scalar(0, slots(0, 2), dx[0][:, slots(0, 2)])
         make_mask(1)
-        turn_and_mask(1, "bank_a")
-        dx2_first = loads.tile([P, 2 * C], F32, name="dx2_first", offset=place["a1"], align_bytes=64)
+        dx[1] = loads.tile([P, S], F32, name="dx1", offset=place["a1"], align_bytes=64)[:]
+        nc.vector.tensor_copy(dx[1][:, slots(0, 2)], ps1[:])
+        turn_and_mask(1, "bank_d")
+        dx2_first = loads.tile([P, 2 * C], F32, name="dx2_first", offset=place["a1"] + 4 * S, align_bytes=64)
         nc.vector.tensor_copy(dx2_first[:], ps2[:])
         quantize(1)
         scatter_vector(2, slots(0, 2), dx2_first[:])

@@ -167,33 +167,38 @@ def tile_moe_adb_relu_kernel(
                 op0=ALU.is_gt,
             )
 
-        def first_product(e, bank):
-            h_ps = psum.tile([P, H], F32, name="h_ps", tag=bank)
-            for s in range(PASSES):
-                nc.tensor.matmul_mx(
-                    out=h_ps[:],
-                    lhsT=slot_w[s][:, slots(e, e + 1)].bitcast(FP8X4),
-                    lhsT_scale=slot_s[e // 2][:, s, slots(e % 2, e % 2 + 1)],
-                    rhs=wb_w[e][:, s, :].bitcast(FP4X4),
-                    rhs_scale=wb_s[:, e * PASSES + s, :],
-                    start=(s == 0),
-                    stop=(s == PASSES - 1),
-                )
+        def first_product(e, banks):
             h_sb[e] = keep.tile([P, 2, P, 2], BF16, name=f"h_sb{e}", align_bytes=64)
-            by_word = h_ps[:].rearrange("u (m w t) -> u w m t", w=2, t=2)
-            nc.scalar.activation(h_sb[e][:], by_word, COPY, scale=g_col[:, e : e + 1])
+            width = H // len(banks)
+            for half, bank in enumerate(banks):
+                c0, c1 = half * width, (half + 1) * width
+                h_ps = psum.tile([P, width], F32, name="h_ps", tag=bank)
+                for s in range(PASSES):
+                    nc.tensor.matmul_mx(
+                        out=h_ps[:],
+                        lhsT=slot_w[s][:, slots(e, e + 1)].bitcast(FP8X4),
+                        lhsT_scale=slot_s[e // 2][:, s, slots(e % 2, e % 2 + 1)],
+                        rhs=wb_w[e][:, s, FP4_BYTES * c0 : FP4_BYTES * c1].bitcast(FP4X4),
+                        rhs_scale=wb_s[:, e * PASSES + s, c0:c1],
+                        start=(s == 0),
+                        stop=(s == PASSES - 1),
+                    )
+                by_word = h_ps[:].rearrange("u (m w t) -> u w m t", w=2, t=2)
+                nc.scalar.activation(
+                    h_sb[e][:, :, c0 // PACK : c1 // PACK, :], by_word, COPY, scale=g_col[:, e : e + 1]
+                )
 
         def turn_and_mask(pair, bank):
-            turned = psum.tile([P, 2 * C, 2], F32, name="turned", tag=bank)
+            turned = psum.tile([P, 2, 2 * C], F32, name="turned", tag=bank)
             for n in range(2):
                 words = h_sb[2 * pair + n][:].rearrange("u w m t -> u (w m t)").bitcast(F32)
                 for w in range(2):
-                    nc.tensor.transpose(turned[:, slots(n, n + 1), w], words[:, w * P : (w + 1) * P], ident[:])
+                    nc.tensor.transpose(turned[:, w, slots(n, n + 1)], words[:, w * P : (w + 1) * P], ident[:])
             dh[pair] = keep.tile([P, 2 * C * PACK], BF16, name=f"dh{pair}", align_bytes=64)
             nc.vector.tensor_tensor(
-                dh[pair][:],
-                turned[:].rearrange("p u w -> p (u w)").bitcast(BF16),
-                mask[pair][:].rearrange("p u d -> p (u d)"),
+                dh[pair][:].rearrange("p (u w t) -> p u w t", w=2, t=2),
+                turned[:].bitcast(BF16).rearrange("p w (u t) -> p u w t", t=2),
+                mask[pair][:].rearrange("p u (w t) -> p u w t", t=2),
                 ALU.mult,
             )
 
@@ -274,12 +279,12 @@ def tile_moe_adb_relu_kernel(
         gather_words(1)
         for s in range(PASSES):
             gather_scales(s, 1)
-        first_product(0, "bank_a")
-        first_product(1, "bank_b")
+        first_product(0, ("bank_a", "bank_e"))
+        first_product(1, ("bank_b", "bank_h"))
         make_mask(0)
         turn_and_mask(0, "bank_c")
-        first_product(2, "bank_b")
-        first_product(3, "bank_h")
+        first_product(2, ("bank_h", "bank_b"))
+        first_product(3, ("bank_f", "bank_g"))
         quantize(0)
 
         both = keep.tile([P, 2 * S], F32, name="both", tag="gate_slot", align_bytes=64)

from contextlib import ExitStack

import concourse.mybir as mybir
from concourse.masks import make_identity

K, T, E, C, H, N = 512, 1024, 4, 128, 512, 1024
S = E * C
FLOPS = 2 * N * K * T + 2 * N * H * S + 2 * H * K * S

F32 = mybir.dt.float32
BF16 = mybir.dt.bfloat16
I32 = mybir.dt.int32
U32 = mybir.dt.uint32
U16 = mybir.dt.uint16
U8 = mybir.dt.uint8
FP8X4 = mybir.dt.float8_e4m3fn_x4
FP4X4 = mybir.dt.float4_e2m1fn_x4
ALU = mybir.AluOpType
COPY = mybir.ActivationFunctionType.Copy

P = 128
PACK = 4
PASSES = N // (P * PACK)
KT = K // P
BANK = 512
LIST_ROWS = 16
FP4_BYTES = 2
ZEROS = 8
SHARE = 256


def tile_moe_adb_relu_kernel(
    tc, dy_words, dy_scales, wt_words, wt_scales, wbt_words, wbt_scales, wat_words, wat_scales, a, gate, offs, out
):
    nc = tc.nc
    with ExitStack() as ctx:
        keep = ctx.enter_context(tc.tile_pool(name="keep", bufs=1))
        loads = ctx.enter_context(tc.tile_pool(name="loads", bufs=1))
        psum = ctx.enter_context(tc.psum_pool(name="psum", bufs=1))

        offsets = keep.tile([P, S // LIST_ROWS], U16, name="offsets")

        groups = [
            {"dy1": 4 * T, "wb0": 4 * H, "wb1": 4 * H, "a0": 8 * PACK * C, "wb2": 8 * H, "wa_s0": 2 * K},
            {"wa0": 4 * K, "a1": 8 * PACK * C, "wa_s1": 2 * K, "wa1": 4 * K, "wt": 3 * K, "wt_s": PASSES * (K - P)},
        ]
        place, zeros, end = {}, [], 0
        for number, group in enumerate(groups):
            start = end
            for name, size in group.items():
                place[name] = end
                end = end + size
            zeros.append(loads.tile([P, (end - start) // 4], F32, name=f"zeros{number}", offset=start, align_bytes=64))

        def load_tile(name, shape, dtype):
            if name in place:
                return loads.tile(shape, dtype, name=name, offset=place[name], align_bytes=64)
            return keep.tile(shape, dtype, name=name, align_bytes=64)

        def zeroed_planes(name, count, width, engine):
            planes = load_tile(name, [P, count, width], U8)
            engine.memset(planes[:].rearrange("p c w -> p (c w)").bitcast(I32), 0)
            return planes

        def load_scales(planes, rows):
            by_r = rows.bitcast(I32).rearrange("c (q r) w -> r q c w", r=4)
            for r in range(4):
                nc.sync.dma_start(planes[r:P:32, :, :].bitcast(I32), by_r[r])

        windows = {kt: keep.tile([P, T], F32, name=f"window{kt}", align_bytes=64) for kt in range(KT)}
        zero = keep.tile([P, ZEROS], F32, name="zero")
        dy_s = zeroed_planes("dy_s", PASSES, T, nc.gpsimd)
        for tile in zeros + [zero]:
            nc.vector.memset(tile[:, 0:ZEROS], 0.0)
        wt0_s = zeroed_planes("wt0_s", PASSES, P, nc.vector)
        nc.vector.tensor_copy(windows[0][:, 0:ZEROS], zeros[0][:, 0:ZEROS])
        wb_s = zeroed_planes("wb_s", E * PASSES, H, nc.vector)
        g_rows = load_tile("g_rows", [P, C], F32)
        nc.vector.memset(g_rows[:], 0.0)
        wa_s = [zeroed_planes("wa_s0", 2, K, nc.vector)]
        nc.vector.tensor_copy(windows[1][:, 0:ZEROS], zeros[1][:, 0:ZEROS])
        wa_s.append(zeroed_planes("wa_s1", 2, K, nc.vector))
        wt_s = zeroed_planes("wt_s", PASSES, K - P, nc.vector)
        ident = keep.tile([P, P], F32, name="ident")
        make_identity(nc, ident[:])
        for kt in range(KT):
            start = ZEROS if kt < len(zeros) else 0
            nc.scalar.activation(windows[kt][:, start:T], zero[:, 0:1].to_broadcast([P, T - start]), COPY)

        dy_w, wb_w, wa_w, a_sb = {}, {}, {}, {}
        a_rows = a.rearrange("(p d) j -> p d j", d=PACK)

        def load_dy(s):
            dy_w[s] = load_tile(f"dy{s}", [P, T], I32)[:]
            nc.sync.dma_start(dy_w[s], dy_words[s].rearrange("p t d -> p (t d)").bitcast(I32))

        def load_adapters(name, words, e0, e1):
            passes, width = words.shape[1], words.shape[3]
            tile = load_tile(name, [P, (e1 - e0) * passes, width], U8)
            nc.sync.dma_start(tile[:].bitcast(I32), words[e0:e1].bitcast(I32).rearrange("e s p w -> p (e s) w"))
            return {e: tile[:, (e - e0) * passes : (e - e0 + 1) * passes, :] for e in range(e0, e1)}

        def load_a(pair):
            a_sb[pair] = load_tile(f"a{pair}", [P, PACK, 2 * C], F32)
            nc.sync.dma_start(a_sb[pair][:], a_rows[:, :, 2 * pair * C : 2 * (pair + 1) * C])

        nc.sync.dma_start(offsets[:], offs)
        wt0_rows = keep.tile([P, PASSES, 4, P // 4], I32, name="wt0_rows", align_bytes=64)
        nc.sync.dma_start(
            wt0_rows[0:4].rearrange("r s q w -> r (s q) w"),
            wt_scales[:, :, 0:P].bitcast(I32).rearrange("s (q r) w -> r (s q) w", r=4),
        )
        load_dy(0)
        wt0_w = keep.tile([P, PASSES, FP4_BYTES * P], U8, name="wt0", tag="wt0_slot", align_bytes=64)
        nc.sync.dma_start(wt0_w[:].bitcast(I32), wt_words[:, :, 0 : FP4_BYTES * P].bitcast(I32).rearrange("s p w -> p s w"))
        for q in range(4):
            nc.vector.tensor_copy(wt0_s[32 * q : 32 * q + 4].bitcast(I32), wt0_rows[0:4, :, q, :])
        load_scales(dy_s, dy_scales)
        load_dy(1)
        load_scales(wb_s, wbt_scales.rearrange("e s b w -> (e s) b w"))
        nc.sync.dma_start(g_rows[0:E, :], gate[0:1, :].rearrange("o (e u) -> (o e) u", e=E))
        wb_w.update(load_adapters("wb0", wbt_words, 0, 1))
        wb_w.update(load_adapters("wb1", wbt_words, 1, 2))
        load_a(0)
        wb_w.update(load_adapters("wb2", wbt_words, 2, E))
        wa_rows = wat_scales.rearrange("e s b w -> (e s) b w")
        load_scales(wa_s[0], wa_rows[0:2])
        wa_w.update(load_adapters("wa0", wat_words, 0, 2))
        load_a(1)
        load_scales(wa_s[1], wa_rows[2:E])
        wa_w.update(load_adapters("wa1", wat_words, 2, E))
        wt_w = load_tile("wt", [P, PASSES, FP4_BYTES * (K - P)], U8)
        nc.sync.dma_start(wt_w[:].bitcast(I32), wt_words[:, :, FP4_BYTES * P :].bitcast(I32).rearrange("s p w -> p s w"))
        load_scales(wt_s, wt_scales[:, :, P:K])
        wt_tile = {0: (wt0_w[:], wt0_s[:])}
        for kt in range(1, KT):
            wt_tile[kt] = (wt_w[:, :, FP4_BYTES * (kt - 1) * P : FP4_BYTES * kt * P], wt_s[:, :, (kt - 1) * P : kt * P])

        g_col = keep.tile([P, ZEROS], F32, name="g_col", tag="gate_slot", align_bytes=64)
        g_ps = psum.tile([P, P], F32, name="g_ps", tag="bank_d")
        nc.tensor.transpose(g_ps[:], g_rows[:], ident[:])
        nc.scalar.copy(g_col[:, 0:E], g_ps[:, 0:E])

        slot_w = [keep.tile([P, S], U32, name=f"slot_w{s}", align_bytes=64) for s in range(PASSES)]
        slot_s = {}
        mask, h_sb, dh, dh_w, dh_s = {}, {}, {}, {}, {}

        def slots(e0, e1):
            return slice(e0 * C, e1 * C)

        def entries(part):
            return offsets[:, part.start // LIST_ROWS : part.stop // LIST_ROWS]

        def gather_words(s):
            nc.vector.tensor_copy(slot_w[s][:], dy_w[s].bitcast(U32).indirect(offsets[:]))

        def gather_scales(s, pair):
            nc.vector.tensor_copy(slot_s[pair][:, s, :], dy_s[:, s, :].indirect(entries(slots(2 * pair, 2 * pair + 2))))

        def make_mask(pair):
            mask[pair] = keep.tile([P, 2 * C, PACK], BF16, name=f"mask{pair}", tag="mask_slot", align_bytes=64)
            nc.vector.tensor_scalar(
                out=mask[pair][:].rearrange("p (c i) d -> p c d i", i=4),
                in0=a_sb[pair][:].rearrange("p d (c i) -> p c d i", i=4),
                scalar1=0.0,
                scalar2=None,
                op0=ALU.is_gt,
            )

        def first_product(e, banks):
            h_sb[e] = keep.tile([P, 2, P, 2], BF16, name=f"h_sb{e}", align_bytes=64)
            width = H // len(banks)
            for half, bank in enumerate(banks):
                c0, c1 = half * width, (half + 1) * width
                h_ps = psum.tile([P, width], F32, name="h_ps", tag=bank)
                for s in range(PASSES):
                    nc.tensor.matmul_mx(
                        out=h_ps[:],
                        lhsT=slot_w[s][:, slots(e, e + 1)].bitcast(FP8X4),
                        lhsT_scale=slot_s[e // 2][:, s, slots(e % 2, e % 2 + 1)],
                        rhs=wb_w[e][:, s, FP4_BYTES * c0 : FP4_BYTES * c1].bitcast(FP4X4),
                        rhs_scale=wb_s[:, e * PASSES + s, c0:c1],
                        start=(s == 0),
                        stop=(s == PASSES - 1),
                    )
                by_word = h_ps[:].rearrange("u (m w t) -> u w m t", w=2, t=2)
                nc.scalar.activation(
                    h_sb[e][:, :, c0 // PACK : c1 // PACK, :], by_word, COPY, scale=g_col[:, e : e + 1]
                )

        def turn_and_mask(pair, bank):
            turned = psum.tile([P, 2, 2 * C], F32, name="turned", tag=bank)
            for n in range(2):
                words = h_sb[2 * pair + n][:].rearrange("u w m t -> u (w m t)").bitcast(F32)
                for w in range(2):
                    nc.tensor.transpose(turned[:, w, slots(n, n + 1)], words[:, w * P : (w + 1) * P], ident[:])
            dh[pair] = keep.tile([P, 2 * C * PACK], BF16, name=f"dh{pair}", align_bytes=64)
            nc.vector.tensor_tensor(
                dh[pair][:].rearrange("p (u w t) -> p u w t", w=2, t=2),
                turned[:].bitcast(BF16).rearrange("p w (u t) -> p u w t", t=2),
                mask[pair][:].rearrange("p u (w t) -> p u w t", t=2),
                ALU.mult,
            )

        def quantize(pair):
            words = keep.tile([P, 2 * C], U32, name=f"dh_w{pair}", align_bytes=64)
            scales = keep.tile([P, 2 * C], U8, name=f"dh_s{pair}", align_bytes=64)
            nc.vector.quantize_mx(out=words[:].bitcast(FP8X4), scales=scales[:], in_=dh[pair][:])
            for n in range(2):
                dh_w[2 * pair + n] = words[:, slots(n, n + 1)]
                dh_s[2 * pair + n] = scales[:, slots(n, n + 1)]

        def second_products(parts, bank):
            dx_ps = psum.tile([P, len(parts) * C], F32, name="dx_ps", tag=bank)
            for n, (kt, e) in enumerate(parts):
                nc.tensor.matmul_mx(
                    out=dx_ps[:, slots(n, n + 1)],
                    lhsT=wa_w[e][:, 0, FP4_BYTES * kt * P : FP4_BYTES * (kt + 1) * P].bitcast(FP4X4),
                    lhsT_scale=wa_s[e // 2][:, e % 2, kt * P : (kt + 1) * P],
                    rhs=dh_w[e].bitcast(FP8X4),
                    rhs_scale=dh_s[e],
                    start=True,
                    stop=True,
                )
            return dx_ps

        def row(kt, e0, e1):
            return [(kt, e) for e in range(e0, e1)]

        def scatter_vector(kt, part, source):
            nc.vector.tensor_copy(windows[kt][:].indirect(entries(part)), source)

        def scatter_scalar(kt, part, source):
            nc.scalar.activation(windows[kt][:].indirect(entries(part)), source, COPY)

        def base_pass(kt, c0, c1, s, base_ps):
            nc.tensor.matmul_mx(
                out=base_ps[:],
                lhsT=wt_tile[kt][0][:, s, :].bitcast(FP4X4),
                lhsT_scale=wt_tile[kt][1][:, s, :],
                rhs=dy_w[s][:, c0:c1].bitcast(FP8X4),
                rhs_scale=dy_s[:, s, c0:c1],
                start=(s == 0),
                stop=(s == PASSES - 1),
            )

        def base_product(kt, c0, c1, bank):
            base_ps = psum.tile([P, c1 - c0], F32, name="base_ps", tag=bank)
            for s in range(PASSES):
                base_pass(kt, c0, c1, s, base_ps)
            return base_ps

        total = {}

        def store(kt, c0, c1, queue):
            queue.dma_start(out[kt * P : (kt + 1) * P, c0:c1], total[kt][:, c0:c1])

        def add_gpsimd(kt, c0, c1, base_sb, queue):
            nc.gpsimd.tensor_tensor(total[kt][:, c0:c1], base_sb, windows[kt][:, c0:c1], ALU.add)
            store(kt, c0, c1, queue)

        def add_vector(kt, c0, c1, base_ps):
            nc.vector.tensor_tensor(total[kt][:, c0:c1], windows[kt][:, c0:c1], base_ps[:], ALU.add)
            store(kt, c0, c1, nc.sync)

        base0 = keep.tile([P, BANK], F32, name="base0", tag="base_slot", align_bytes=64)
        base0_rest = keep.tile([P, BANK], F32, name="base0_rest", align_bytes=64)
        first_ps = [psum.tile([P, BANK], F32, name="first_ps", tag=bank) for bank in ("bank_f", "bank_g")]
        for s in range(PASSES):
            for half in range(2):
                base_pass(0, half * BANK, (half + 1) * BANK, s, first_ps[half])
        nc.scalar.copy(base0[:], first_ps[0][:])
        nc.scalar.copy(base0_rest[:], first_ps[1][:])
        slot_s[0] = keep.tile([P, PASSES, 2 * C], U8, name="slot_s0", align_bytes=64)
        slot_s[1] = keep.tile([P, PASSES, 2 * C], U8, name="slot_s1", tag="wt0_slot", align_bytes=64)
        gather_words(0)
        for s in range(PASSES):
            gather_scales(s, 0)
        gather_words(1)
        for s in range(PASSES):
            gather_scales(s, 1)
        first_product(0, ("bank_a", "bank_e"))
        first_product(1, ("bank_b", "bank_h"))
        make_mask(0)
        turn_and_mask(0, "bank_c")
        first_product(2, ("bank_h", "bank_b"))
        first_product(3, ("bank_f", "bank_g"))
        quantize(0)

        both = keep.tile([P, 2 * S], F32, name="both", tag="gate_slot", align_bytes=64)
        dx = {0: both[:, 0:S], 3: both[:, S : 2 * S]}
        nc.scalar.copy(dx[0][:, slots(0, 2)], second_products(row(0, 0, 2), "bank_d")[:])
        nc.scalar.copy(dx[3][:, slots(0, 2)], second_products(row(3, 0, 2), "bank_g")[:])
        ps1 = second_products(row(1, 0, 2), "bank_a")
        ps2 = second_products(row(2, 0, 2), "bank_e")
        scatter_scalar(0, slots(0, 2), dx[0][:, slots(0, 2)])
        make_mask(1)
        dx[1] = loads.tile([P, S], F32, name="dx1", offset=place["a1"], align_bytes=64)[:]
        nc.vector.tensor_copy(dx[1][:, slots(0, 2)], ps1[:])
        turn_and_mask(1, "bank_d")
        dx2_first = loads.tile([P, 2 * C], F32, name="dx2_first", offset=place["a1"] + 4 * S, align_bytes=64)
        nc.vector.tensor_copy(dx2_first[:], ps2[:])
        quantize(1)
        scatter_vector(2, slots(0, 2), dx2_first[:])
        scatter_scalar(3, slots(0, 1), dx[3][:, slots(0, 1)])

        dx2_second = keep.tile([P, 2 * C], F32, name="dx2_second", align_bytes=64)
        nc.scalar.copy(dx[0][:, slots(2, E)], second_products(row(0, 2, E), "bank_b")[:])
        nc.vector.tensor_copy(dx[1][:, slots(2, E)], second_products(row(1, 2, E), "bank_c")[:])
        ps = second_products(row(2, 2, E) + row(3, 2, E), "bank_a")
        nc.scalar.copy(dx2_second[:], ps[:, slots(0, 2)])
        scatter_scalar(0, slots(2, E), dx[0][:, slots(2, E)])
        nc.scalar.copy(dx[3][:, slots(2, E)], ps[:, slots(2, E)])
        scatter_scalar(2, slots(2, E), dx2_second[:])
        scatter_scalar(3, slots(1, E), dx[3][:, slots(1, E)])
        base3 = keep.tile([P, SHARE], F32, name="base3", align_bytes=64)
        nc.vector.tensor_copy(base3[:], base_product(3, T - SHARE, T, "bank_e")[:])
        scatter_vector(1, slots(0, E), dx[1])

        for kt in (0, 3):
            total[kt] = keep.tile([P, T], F32, name=f"total{kt}", align_bytes=64)
        add_gpsimd(0, 0, BANK, base0[:], nc.sync)
        add_gpsimd(0, BANK, T, base0_rest[:], nc.sync)
        later = keep.tile([P, 2 * T], F32, name="later", tag="base_slot", align_bytes=64)
        total[1], total[2] = later[:, 0:T], later[:, T : 2 * T]
        add_vector(2, 0, BANK, base_product(2, 0, BANK, "bank_b"))
        add_vector(2, BANK, T, base_product(2, BANK, T, "bank_c"))
        add_vector(1, 0, BANK, base_product(1, 0, BANK, "bank_d"))
        add_vector(1, BANK, T, base_product(1, BANK, T, "bank_f"))
        add_vector(3, 0, BANK, base_product(3, 0, BANK, "bank_a"))
        add_vector(3, BANK, T - SHARE, base_product(3, BANK, T - SHARE, "bank_e"))
        add_gpsimd(3, T - SHARE, T, base3[:], nc.scalar)
